import numpy as np, ml_dtypes
CORES = [1,5,17,21,33,37,49,53]
N = 8
BF = ml_dtypes.bfloat16
S, F, L, RO, A, TH, BYG = 4096, 768, 256, 3, 704, 8, 1
def whole(x, hi):
    return np.minimum(x.astype(np.int64), hi)
def parts(rng):
    a = rng.choice(np.array([0.2, 0.3, 0.4, 0.5]), (N, 8, 1, 1)).astype(np.float32)
    t = whole(256 * rng.random((N, 8, 16, S), dtype=np.float32) ** a, 255)
    t = np.where(rng.random((N, 8, 1, S)) < 0.25, 255, t)
    return t, rng.integers(0, 255, (N, 8, 16, F)), rng.integers(0, S, (N, 8, 16, F)), rng.integers(0, S, (N, 8, 16, F))
def pack(t, z, eh, ef):
    return {"tab": t.reshape(N, 128, S).astype(np.float32).astype(BF), "zf": z.reshape(N, 128, F).astype(np.float32).astype(BF),
            "eh": np.ascontiguousarray(eh.reshape(N, 128, F)).astype(np.int32), "ef": np.ascontiguousarray(ef.reshape(N, 128, F)).astype(np.int32)}
def setup_inputs(rng):
    return pack(*parts(rng))
def setup_inputs_full(rng):
    t, z, eh, ef = parts(rng)
    for g in (0, 5):
        t[:, g] = 255; eh[:, g] = rng.integers(F, S, (N, 16, F)); ef[:, g] = rng.integers(F, S, (N, 16, F))
        eh[:, g, 0] = np.argsort(rng.random((N, F)), axis=1)
    f = np.arange(F); c = F - A; see = (f >= A - c) & (f < A)
    m = np.flatnonzero(see)
    for g in (2, 7):
        p = np.argsort(rng.random((N, S // 2)), axis=1)[:, :L]
        t[:, g] = 255; eh[:, g] = rng.integers(S // 2, S - 64, (N, 16, F)); ef[:, g] = rng.integers(S // 2, S - 64, (N, 16, F))
        z[:, g] = np.where(f < L, rng.integers(160, 255, (N, 16, F)), np.where(see, rng.integers(100, 160, (N, 16, F)), rng.integers(0, 100, (N, 16, F))))
        eh[:, g, 0] = np.where(see, eh[:, g, 0], p[:, f % L])
        for r in range(N):
            q = (r + 1 + (2 + BYG * g) % (N - 1)) % N
            a, b = m[1::4], m[3::4]
            ef[r, g, rng.integers(0, 16, len(a)), a] = p[q, L - c - 1]
            ef[r, g, rng.integers(0, 16, len(b)), b] = np.max(p[q])
    return pack(t, z, eh, ef)
def setup_inputs_ties(rng):
    t, z, eh, ef = parts(rng)
    pat = np.array([0, 0, 2, 3, 5, TH - 2, TH - 2, TH - 2, TH - 1, TH - 1, TH - 1, TH - 1, TH, TH, TH, 16])
    place = np.argsort(rng.random((N, 4, 16, S), dtype=np.float32), axis=2)
    t[:, :4] = np.where(place < pat[np.arange(S) % 16], 0, 255)
    for x in (eh, ef):
        top = rng.choice(np.array([8, 12, 12, 12, 15, 16]), (N, 4, 1, F))
        x[:, :4] = 16 * rng.integers(0, S // 16, (N, 4, 16, F)) + (rng.random((N, 4, 16, F)) * top).astype(np.int64)
    v = np.array([0, 1, 127, 128, 254, 255])
    t[:, 4:] = rng.choice(v, (N, 4, 16, S), p=[0.04, 0.04, 0.1, 0.12, 0.3, 0.4]); z[:, 4:] = rng.choice(v[:5], (N, 4, 16, F))
    return pack(t, z, eh, ef)
def setup_inputs_alike(rng):
    t, z, eh, ef = parts(rng); few = np.array([0, S - 1, S // 2, 3])
    eh[:, 0] = rng.choice(few, (N, 16, F)); eh[:, 1] = rng.integers(0, S, (N, 1, F))
    t[:, 2] = 255; eh[:, 2] = rng.integers(0, S, (N, 1, 1))
    eh[:, 3] = S - 1 - rng.integers(0, 12, (N, 16, F)); ef[:, 3] = S - 1 - rng.integers(0, 12, (N, 16, F))
    ef[:, 4] = rng.choice(few, (N, 16, F))
    for x in (z, eh, ef): x[:, 5, :, 1::2] = x[:, 5, :, 0::2]
    return pack(t, z, eh, ef)
def setup_inputs_hard(rng):
    t, z, eh, ef = parts(rng)
    t[:, 0] = 0; t[rng.integers(0, N), 1] = 0; t[:, 2] = 255
    z[:, 3] = 0; t[:, 3] = np.maximum(t[:, 3], 1)
    z[:, 4] = 254; t[:, 4] = np.where(rng.random((N, 16, S)) < 0.8, 255, t[:, 4])
    return pack(t, z, eh, ef)
def setup_inputs_spread(rng):
    u = np.float32(2) ** -rng.integers(-2, 6, (N, 8, 1, S)).astype(np.float32); v = np.float32(2) ** rng.integers(-2, 5, (N, 8, 1, F)).astype(np.float32)
    t = whole(256 * rng.random((N, 8, 16, S), dtype=np.float32) ** u, 255); z = whole(255 * rng.random((N, 8, 16, F), dtype=np.float32) ** v, 254)
    e = [whole(S * rng.random((N, 8, 16, F)) ** (2.0 ** rng.integers(0, 3, (N, 8, 16, 1))), S - 1) for i in range(2)]
    return pack(t, z, e[0], e[1])
def check_inputs(d):
    bad = []
    for k, hi in (("tab", 255), ("zf", 254), ("eh", S - 1), ("ef", S - 1)):
        v = np.asarray(d[k]).astype(np.float64)
        if not (np.min(v) >= 0 and np.max(v) <= hi): bad.append("range of " + k)
        if not np.all(v == np.floor(v)): bad.append("whole numbers in " + k)
    return bad
def reference(tab, zf, eh, ef):
    t = tab.astype(np.float32).astype(np.int32).reshape(N, 8, 16, S); z = zf.astype(np.float32).astype(np.int32).reshape(N, 8, 16, F)
    home = eh.astype(np.int64).reshape(N, 8, 16, F); far = ef.astype(np.int64).reshape(N, 8, 16, F)
    d = np.zeros((N, 8, F), np.int64); oc = np.full((N, 8, S), -1, np.int64); free = np.ones((N, 8, F), bool)
    for step in range(RO):
        old = np.array(t)
        turn = (np.arange(F) + A * step) % F
        for r in range(N):
            for g in range(8):
                q = (r + 1 + (step + BYG * g) % (N - 1)) % N
                ln = turn[free[r, g][turn]][:L]
                zl = z[r, g][:, ln]
                sh = (home[r, g][:, ln] + d[r, g, ln]) & (S - 1); sf = (far[r, g][:, ln] + d[r, g, ln]) & (S - 1)
                ph = np.sum(old[r, g][:, sh] <= zl[:, None, :], axis=0); pf = np.sum(old[q, g][:, sf] <= zl[:, None, :], axis=0)
                k = np.argmax(ph, axis=0)
                worst = np.maximum(np.max(ph, axis=0), np.max(pf, axis=0)); go = worst < TH
                d[r, g, ln] += np.where(go, 0, worst)
                cl = np.flatnonzero(go)
                s, first = np.unique(sh[k, np.arange(L)][cl], return_index=True)
                w = cl[first]; was = oc[r, g, s]; was = was[was >= 0]
                d[r, g, was] += 1; free[r, g, was] = True
                t[r, g][:, s] = zl[:, w]; oc[r, g, s] = ln[w]; free[r, g, ln[w]] = False
    return {"yt": t.reshape(N, 128, S).astype(np.float32).astype(BF), "yo": oc.astype(np.float32), "yd": d.astype(np.float32)}

@@ -1,0 +1,695 @@
+import numpy as np
+from concourse.bass import DstId, RemoteDMATransfer
+from concourse.mybir import AluOpType as A, AxisListType, ActivationFunctionType as AF
+
+N, NG, NS, NF, NL = 8, 8, 4096, 768, 256
+WR = 32
+NT = NS + WR + 3 * NL
+DUMP = NS + WR
+TYPES = {"b": "bfloat16", "f": "float32", "i": "int32", "u": "uint16"}
+SCRATCH = {"psb": ("psum", [128, 4096], "float32")}
+for _where, _shape, _names in (
+        ("sbuf", [128, NT], "b:tb b:f1 b:f2 f:occ"), ("sbuf", [128, NF], "i:eh_s i:ef_s b:z_s b:zf1 b:zf2 b:st f:stc b:ydm f:idf b:ihi b:ilo b:ihl"),
+        ("sbuf", [128, 4096], "b:zrep b:zrepf b:cmph b:cmpf"), ("sbuf", [128, 2048], "b:nrow"),
+        ("sbuf", [128, NL], "i:efq b:zql f:xp f:xf f:dc u:offh u:offf b:zl b:dl f:lnf1 f:lnf2 b:st1 f:st1c f:st2 b:b1 b:b3 b:zu "
+                            "b:ctx b:gr b:gle b:glo b:ngt b:t1 b:junk i:rep_i u:rep"),
+        ("sbuf", [128, 16], "u:w0 u:u10 u:u20 f:mk b:li"), ("sbuf", [128, 32], "u:w1 u:w2 u:u21"),
+        ("sbuf", [128, N * 16], "u:la0"), ("sbuf", [128, N * 32], "u:la1"),
+        ("sbuf", [128, 2, 64], "f:kh f:k1 b:fh b:m1"), ("sbuf", [128, 2, 32], "f:k2 b:m2"), ("sbuf", [128, 2, 16], "f:k3 b:m3"),
+        ("sbuf", [128, 2, 8], "i:hki i:whi b:m4 b:wm b:ng b:go_ f:rr b:nd"), ("sbuf", [128, 8, 2], "b:wq b:wland"),
+        ("sbuf", [128, 2, 24], "i:di b:sd b:sdg b:dd0 b:dd1 b:dd2"), ("sbuf", [128, 2, 40], "b:ttl"), ("sbuf", [128, 2, 56], "b:cdl"),
+        ("sbuf", [128, 48], "b:uu f:vb b:scn f:dst u:dsu f:yc"),
+        ("sbuf", [128, 8], "i:pc i:pmi f:ck f:pmf f:pcf b:blkf b:blkk"), ("sbuf", [128, 64], "i:li_i"), ("sbuf", [128, 144], "b:ew b:ela b:elb b:el"),
+        ("sbuf", [128, 128], "f:pmx f:z32 b:idb b:err b:ere b:ero b:er b:er2 b:onb b:ntr"), ("sbuf", [128, 512], "b:ob"),
+        ("sbuf", [128, 1024], "b:zb b:mmk b:ngc"),
+        ("dram", [1024, 32], "i:rd b:zq i:rl b:zqd"), ("dram", [1024, 512], "b:td b:fd1 b:fd2"), ("dram", [1024, 96], "b:zd b:zd1 b:zd2"),
+        ("dram", [128, NS], "b:hb"), ("dram", [128, NF], "b:hz")):
+    for _n in _names.split():
+        SCRATCH[_n[2:]] = (_where, _shape, TYPES[_n[0]])
+ENG = {"v": "ev", "s": "es", "p": "ep", "g": "eg"}
+SEMAPHORES = (["ev", "es", "ep", "eg", "lsem", "l_hb", "a_req", "a_wf", "a_l0", "a_l1", "a_f1", "a_f2", "a_hb", "a_hz"]
+              + ["d%d" % k for k in range(24)])
+WRITES = ("out", "accum_out", "ap")
+MASKS = {}
+ALL = slice(None)
+
+
+def asked(r, g, t):
+    return (r + 1 + (t + g) % (N - 1)) % N
+
+
+def asker(q, g, t):
+    return (q - 1 - (t + g) % (N - 1)) % N
+
+
+def dst_id(topo, c):
+    a = topo.addr(c)
+    return DstId(rid=a[0], pnc=a[1])
+
+
+def off_chip(topo, src, dst):
+    return topo.chip(src) != topo.chip(dst)
+
+
+def far_engines(core, T, topo):
+    for c in T.cores:
+        if off_chip(topo, core, c):
+            return topo.engines(core, c)
+    return []
+
+
+def near_engines(core, dst, T, topo):
+    far = far_engines(core, T, topo)
+    return [e for e in topo.engines(core, dst) if e not in far]
+
+
+def helper_of(core, T, topo):
+    for c in topo.cores_of(core):
+        if T.rank_of(c) is None and topo.die(c) == topo.die(core) and all(topo.may_write(c, d) for d in T.cores):
+            return c
+
+
+def singles(core, dsts, T, topo):
+    nf, nn, out = 0, 0, []
+    for d in dsts:
+        if off_chip(topo, core, d):
+            out.append(topo.engines(core, d)[nf])
+            nf += 1
+        else:
+            out.append(near_engines(core, d, T, topo)[nn])
+            nn += 1
+    return out
+
+
+def bits(engines):
+    m = 0
+    for e in engines:
+        m |= 1 << e
+    return m
+
+
+def v(name, *idx):
+    return ("v", name, idx if idx else (ALL,))
+
+
+def ind(win, off):
+    return ("i", win, off)
+
+
+def is_view(x):
+    return isinstance(x, tuple) and len(x) == 3 and x[0] in ("v", "i")
+
+
+def region(view):
+    name, idx = view[1], view[2]
+    shape = SCRATCH[name][1]
+    key = (name, str(idx))
+    if key not in MASKS:
+        a, b, c = idx[0].indices(shape[0])
+        n = int(np.prod(shape[1:]))
+        sel = np.arange(n).reshape(shape[1:])[tuple(idx[1:])] if len(idx) > 1 else np.arange(n)
+        m = np.zeros(n, bool)
+        m[np.asarray(sel).ravel()] = True
+        bank = 0
+        if SCRATCH[name][0] == "psum":
+            for k in range(n // 512):
+                if m[k * 512:(k + 1) * 512].any():
+                    bank |= 1 << k
+        MASKS[key] = (a, b, int.from_bytes(np.packbits(m).tobytes(), "big"), bank)
+    return MASKS[key]
+
+
+def flow(g, T):
+    queues = {"v": g.vector, "s": g.scalar, "p": g.tensor, "g": g, "y": g.sync}
+    known = {q: {} for q in queues}
+    total, acc = {}, {}
+
+    def ap(x):
+        if x[0] == "i":
+            return ap(x[1]).indirect(ap(x[2]))
+        t = T[x[1]]
+        return t[x[2] if len(x[2]) > 1 else x[2][0]]
+
+    def parts(x):
+        return [x] if x[0] == "v" else [x[1], x[2]]
+
+    def each(reads, writes):
+        for kind, xs in (("r", reads), ("w", writes)):
+            for x in xs:
+                if x[1] in SCRATCH:
+                    yield kind, x[1], region(x)
+
+    def deps(q, reads, writes, tile=None):
+        ev = []
+        for kind, name, (p0, p1, m, bank) in each(reads, writes):
+            for e in acc.get(name, ()):
+                if bank and (bank & e["bank"]) and (q != e["q"] or (tile is not None and e["tile"] not in (None, tile))):
+                    ev.append(e["ev"])
+                elif (kind == "w" or e["kind"] == "w") and e["p0"] < p1 and p0 < e["p1"] and (m & e["m"]):
+                    if bank and q == "p" and e["q"] == "p":
+                        continue
+                    if kind == "w" and e["kind"] == "r" and q == e["q"] and q in ENG:
+                        continue
+                    ev.append(e["ev"])
+        return ev
+
+    def settle(q, ev):
+        need = {}
+        for sem, cnt, clk in ev:
+            if sem not in need or need[sem][0] < cnt:
+                need[sem] = (cnt, clk)
+        for sem in sorted(need, key=lambda s: -sum(need[s][1].values())):
+            cnt, clk = need[sem]
+            if known[q].get(sem, 0) >= cnt:
+                continue
+            queues[q].wait_ge(T.sem[sem], cnt)
+            for k in clk:
+                known[q][k] = max(known[q].get(k, 0), clk[k])
+            known[q][sem] = max(known[q].get(sem, 0), cnt)
+
+    def note(q, reads, writes, event, tile=None):
+        for kind, name, (p0, p1, m, bank) in each(reads, writes):
+            old = acc.get(name, [])
+            inside = lambda e: p0 <= e["p0"] and e["p1"] <= p1 and (e["m"] & ~m) == 0
+            if kind == "w" and not bank:
+                old = [e for e in old if not inside(e)]
+            else:
+                old = [e for e in old if not (e["kind"] == kind and e["q"] == q and e["ev"][0] == event[0] and inside(e))]
+            acc[name] = old + [{"kind": kind, "q": q, "p0": p0, "p1": p1, "m": m, "bank": bank, "ev": event, "tile": tile}]
+
+    def done(who, q, sem, n, reads, writes, tile=None):
+        total[sem] = total.get(sem, 0) + n
+        clk = dict(known[q])
+        clk[sem] = total[sem]
+        note(who, reads, writes, (sem, total[sem], clk), tile)
+
+    def call(q, meth, **kw):
+        reads, writes, tile = [], [], None
+        for k in kw:
+            x = kw[k]
+            if is_view(x):
+                if k in WRITES:
+                    writes.append(parts(x)[0])
+                    reads += parts(x)[1:]
+                else:
+                    reads += parts(x)
+        if meth == "matmul":
+            p0, p1, m, bank = region(kw["lhsT"])
+            tile = p0 if p1 - p0 <= 32 else None
+        settle(q, deps(q, reads, writes, tile))
+        args = {k: (ap(kw[k]) if is_view(kw[k]) else kw[k]) for k in kw}
+        eng = queues[q]
+        f = {"tensor_copy": lambda: eng.tensor_copy(**args), "tensor_tensor": lambda: eng.tensor_tensor(**args),
+             "tensor_scalar": lambda: eng.tensor_scalar(**args), "tensor_reduce": lambda: eng.tensor_reduce(**args),
+             "scan": lambda: eng.tensor_tensor_scan(**args), "memset": lambda: eng.memset(args["ap"], args["constant"]),
+             "activation": lambda: eng.activation(**args), "matmul": lambda: eng.matmul(**args),
+             "iota": lambda: eng.iota(**args), "affine_select": lambda: eng.affine_select(**args)}[meth]
+        f().then_inc(T.sem[ENG[q]], 1)
+        done(q, q, ENG[q], 1, reads, writes, tile)
+
+    def dma(q, sem, out, in_):
+        settle(q, deps(q, [in_], [out]))
+        queues[q].dma_start(out=ap(out), in_=ap(in_)).then_inc(T.sem[sem], 16)
+        done(sem, q, sem, 16, [in_], [out])
+
+    def arrive(out, sem, cnt):
+        total[sem] = cnt
+        note("far", [], [out], (sem, cnt, {sem: cnt}))
+
+    def fused(transfers, local="lsem"):
+        srcs = [t[0] for t in transfers]
+        settle("g", deps("g", srcs, []))
+        g.remote_dma_fused([RemoteDMATransfer(dst_ids=[d[0] for d in t[1]], dma_engine_mask=bits(t[2]), remote_sem=T.sem[t[3]],
+                                              srcs=[ap(t[0])], dsts=[ap(d[1]) for d in t[1]]) for t in transfers],
+                           local_sem=T.sem[local])
+        done(local, "g", local, sum(len(t[2]) for t in transfers), srcs if local != "lsem" else [], [])
+
+    def after(q, names):
+        settle(q, [e["ev"] for n in names for e in acc.get(n, ())])
+
+    def finish():
+        for sem in total:
+            if known["g"].get(sem, 0) < total[sem]:
+                g.wait_ge(T.sem[sem], total[sem])
+
+    return {"call": call, "dma": dma, "arrive": arrive, "fused": fused, "after": after, "finish": finish}
+
+
+def blk(name, k):
+    return v(name, slice(128 * k, 128 * k + 128), ALL)
+
+
+def cols(name, a, b, step=None):
+    return v(name, ALL, slice(a, b, step))
+
+
+def rows(name, n, a, b, step=None):
+    return v(name, slice(0, n), slice(a, b, step))
+
+
+def sub(name, a, b):
+    return v(name, ALL, ALL, slice(a, b))
+
+
+def halves(a, n):
+    return sub(a, 0, n), sub(a, n, 2 * n)
+
+
+def helper_main(g, core, rank, T, topo):
+    F = flow(g, T)
+    F["arrive"](v("hb"), "a_hb", len(topo.engines(T.cores[rank], core)))
+    F["arrive"](v("hz"), "a_hz", len(topo.engines(T.cores[rank], core)))
+    F["dma"]("s", "d1", v("zd"), v("hz"))
+    F["dma"]("y", "d0", v("td"), v("hb"))
+    for t in (1, 2):
+        dst = [T.cores[asker(rank, k, t)] for k in range(NG)]
+        eng = singles(core, dst, T, topo)
+        for src, land in (("zd", "zd%d" % t), ("td", "fd%d" % t)):
+            F["fused"]([(blk(src, k), [(dst_id(topo, dst[k]), blk(land, k))], [eng[k]], "a_f%d" % t) for k in range(NG)])
+    F["finish"]()
+
+
+def rank_main(g, core, rank, T, topo):
+    F = flow(g, T)
+    C, dma, arrive, fused = F["call"], F["dma"], F["arrive"], F["fused"]
+    ps = lambda a, b, n=128: v("psb", slice(0, n), slice(a, b))
+    P6, P7 = 3072, 3584
+    row = ps(P7 + 256, P7 + 512)
+
+    def copy(q, out, in_):
+        if q == "s":
+            C("s", "activation", out=out, in_=in_, func=AF.Copy)
+        else:
+            C("v", "tensor_copy", out=out, in_=in_)
+
+    def tt(out, a, b, op):
+        C("v", "tensor_tensor", out=out, in0=a, in1=b, op=op)
+
+    def ts(out, a, s1, op, s2=None, op1=None):
+        if op1 is None:
+            C("v", "tensor_scalar", out=out, in0=a, scalar1=s1, scalar2=None, op0=op)
+        else:
+            C("v", "tensor_scalar", out=out, in0=a, scalar1=s1, scalar2=s2, op0=op, op1=op1)
+
+    def mm(out, lhsT, rhs, start=True, stop=True):
+        C("p", "matmul", out=out, lhsT=lhsT, rhs=rhs, start=start, stop=stop)
+
+    def fill(x, c):
+        C("v", "memset", ap=x, constant=c)
+
+    def iota(out, pattern, base, ch):
+        if SCRATCH[out[1]][2] == "int32":
+            C("g", "iota", out=out, pattern=pattern, base=base, channel_multiplier=ch)
+        else:
+            C("g", "iota", out=out, pattern=pattern, base=base, channel_multiplier=ch, allow_small_or_imprecise_dtypes=True)
+
+    def sel(out, in_, pattern, op, fillv, base, ch):
+        C("g", "affine_select", out=out, in_=in_, pattern=pattern, compare_op=op, fill=float(fillv), base=base, channel_multiplier=ch)
+
+    dma("y", "d0", v("rd"), v("ef", ALL, slice(0, NL)))
+    dma("s", "d1", v("zq"), v("zf", ALL, slice(0, NL)))
+    dma("s", "d3", cols("z_s", 64, 320), v("zf", ALL, slice(0, NL)))
+    dma("y", "d2", cols("eh_s", 64, 320), v("eh", ALL, slice(0, NL)))
+    dma("y", "d4", cols("tb", 0, NS), v("tab"))
+
+    iota(v("rep_i"), [[1, NL]], 0, 0)
+    copy("v", v("rep"), v("rep_i"))
+    iota(v("pc"), [[0, 8]], 0, 1)
+    fill(v("z32"), 0.0)
+    fill(v("ob"), 1.0)
+    fill(v("zb"), 0.0)
+    ts(v("pmi"), v("pc"), 15, A.bitwise_and)
+    ts(v("ck"), v("pmi"), -8192.0, A.mult, 122880.0, A.add)
+    copy("v", v("pmf"), v("pmi"))
+    sel(v("pmx"), v("z32"), [[1, 16], [16, 8]], A.not_equal, 1.0, 0, -1)
+    sel(v("blkf"), cols("ob", 0, 8), [[-16, 8]], A.is_ge, 0.0, 0, 1)
+    sel(v("blkf"), v("blkf"), [[16, 8]], A.is_ge, 0.0, 15, -1)
+    ckc, pmc = cols("ck", 0, 1), cols("pmf", 0, 1)
+
+    dst = [T.cores[asked(rank, k, 0)] for k in range(NG)]
+    eng = singles(core, dst, T, topo)
+    for src, land in (("zq", "zqd"), ("rd", "rl")):
+        fused([(blk(src, k), [(dst_id(topo, dst[k]), blk(land, k))], [eng[k]], "a_req") for k in range(NG)])
+    arrive(v("rl"), "a_req", 2 * NG)
+    arrive(v("zqd"), "a_req", 2 * NG)
+
+    iota(v("li_i"), [[16, 64]], 0, 0)
+    sel(v("idb"), cols("zb", 0, 128), [[1, 128]], A.not_equal, 1.0, 0, -1)
+    ts(cols("mk", 0, 8), v("pmf"), 0.0, A.is_equal)
+    ts(cols("mk", 8, 16), v("pmf"), 1.0, A.is_equal)
+    ts(v("blkk"), v("blkf"), 131072.0, A.mult)
+    ts(v("xp"), cols("eh_s", 64, 320), ckc, A.add)
+    copy("v", v("offh"), cols("eh_s", 64, 320))
+    copy("v", v("pcf"), v("pc"))
+    for t in range(3):
+        n = "dd%d" % t
+        fill(sub(n, 0, 8), 8.0 + t)
+        for h in range(2):
+            fill(v(n, ALL, h, slice(8, 16)), -6.0 + 8 * h)
+            ts(v(n, ALL, h, slice(16, 24)), v("pcf"), -8.0, A.add)
+    fill(sub("cdl", 48, 56), 1.0)
+    fill(v("st"), 0.0)
+    fill(v("uu"), 1.0)
+    fill(v("vb"), 0.0)
+    fill(v("ntr"), -1.0)
+    for name in ("err", "ere", "ero", "er", "er2"):
+        copy("v", v(name), cols("zb", 0, 128))
+    copy("v", v("ew"), cols("zb", 0, 144))
+    ts(v("li"), cols("li_i", 0, 16), pmc, A.add)
+    ts(v("yc"), cols("li_i", 0, 48), pmc, A.add, 961.0, A.add)
+
+    def zrep(out, win, lists):
+        for j in range(4):
+            copy("s", cols(out, 1024 * j, 1024 * j + 1024), ind(win, cols(lists, 64 * j, 64 * j + 64)))
+
+    def look(j, out, table, width, off, rep_):
+        tt(cols(out, 1024 * j, 1024 * j + 1024), ind(cols(table, 0, width), cols(off, 64 * j, 64 * j + 64)),
+           cols(rep_, 1024 * j, 1024 * j + 1024), A.is_le)
+
+    def cmpcol(name, h, k):
+        return cols(name, 2048 * h + k, 2048 * h + 2048, 16)
+
+    def key_mm(h):
+        b = 512 * h
+        mm(ps(b, b + 128), cols("xp", 128 * h, 128 * h + 128), v("pmx"), True, False)
+        for k in range(16):
+            mm(ps(b + 8 * k, b + 8 * k + 8), cmpcol("cmph", h, k), v("blkk"), False, k == 15)
+        copy("s", v("kh", ALL, h, ALL), ps(b + 64, b + 128))
+
+    def home_tree(t):
+        for h in range(2):
+            tt(v("k1", ALL, h, ALL), ps(512 * h, 512 * h + 64), v("kh", ALL, h, ALL), A.max)
+        tt(v("k2"), *halves("k1", 32), A.max)
+        tt(v("k3"), *halves("k2", 16), A.max)
+        tt(v("hki"), *halves("k3", 8), A.max)
+        for q, sh in ((0, 8), (1, 4)):
+            ts(sub("di", 8 * q, 8 * q + 8), v("hki"), sh, A.arith_shift_right, 15, A.bitwise_and)
+        ts(sub("di", 16, 24), v("hki"), 15, A.bitwise_and)
+        ts(v("whi"), v("hki"), 17, A.arith_shift_right)
+        ts(sub("cdl", 0, 24), v("di"), -8.0, A.add)
+        C("s", "activation", out=sub("cdl", 24, 48), in_=sub("cdl", 0, 24), func=AF.Square)
+        tt(v("sd"), sub("cdl", 0, 24), v("dd%d" % t), A.subtract)
+
+    def gram_rows():
+        for h in range(2):
+            mm(ps(P7 + 128 * h, P7 + 128 * h + 128, 56), v("cdl", ALL, h, ALL), v("idb"))
+        ct = rows("ctx", 56, 0, NL)
+        copy("s", ct, ps(P7, P7 + NL, 56))
+        for name, e, b in (("gr", "err", P7 + 256), ("gle", "ere", 0), ("glo", "ero", 256)):
+            mm(ps(b, b + NL), rows(e, 56, 0, 128), ct)
+        for name, b in (("gr", P7 + 256), ("gle", 0), ("glo", 256)):
+            copy("s", v(name), ps(b, b + NL))
+
+    def masks(bs):
+        for b in bs:
+            mm(ps(512 * b, 512 * b + 512), v("idb"), cols("mmk", 0, 512) if b < 4 else cols("mmk", 512, 1024), True, False)
+
+    def blocks():
+        out = []
+        for b in (3, 2, 5, 4, 1, 0):
+            if b < 4:
+                out += [(2 * b + x, 1, 512 * b + 256 * x, 256) for x in range(2)]
+            else:
+                out += [(4 * (b - 4) + x, 0, 512 * b + 128 * x, 128) for x in range(4)]
+        return out
+
+    def gram():
+        for k, h, a, n in blocks():
+            sl = slice(32 * (k // 2), 32 * (k // 2) + 32)
+            mm(ps(a, a + n), v("gle" if k % 2 == 0 else "glo", sl, slice(128 * h, 128 * h + 128)), v("gr", sl, slice(0, n)), False, False)
+
+    def far_mm(h):
+        for k in range(16):
+            a = P6 + 128 * h + 8 * k
+            mm(ps(a, a + 8), cmpcol("cmpf", h, k), v("blkf"))
+        copy("s", v("fh", ALL, h, ALL), ps(P6 + 128 * h + 64, P6 + 128 * h + 128))
+
+    def far_tree():
+        for h in range(2):
+            tt(v("m1", ALL, h, ALL), ps(P6 + 128 * h, P6 + 128 * h + 64), v("fh", ALL, h, ALL), A.max)
+        tt(v("m2"), *halves("m1", 32), A.max)
+        tt(v("m3"), *halves("m2", 16), A.max)
+
+    def decide(t, lists):
+        ts(v("ng"), v("wm"), 8.0, A.is_ge)
+        for h in range(2):
+            mm(ps(P7 + 128 * h, P7 + 128 * h + 128, 8), v("ng", ALL, h, ALL), v("idb"))
+        copy("s", rows("ngt", 8, 0, NL), ps(P7, P7 + NL, 8))
+        ts(v("go_"), v("wm"), 8.0, A.is_lt)
+        tt(sub("ttl", 32, 40), v("wm"), v("ng"), A.mult)
+        for q in range(3):
+            tt(sub("sdg", 8 * q, 8 * q + 8), sub("sd", 8 * q, 8 * q + 8), v("go_"), A.mult)
+        bl = blocks()
+        for j, (k, h, a, n) in enumerate(bl):
+            last = j == len(bl) - 1 or bl[j + 1][2] // 512 != a // 512
+            mm(ps(a, a + n), rows("ngc", 8, 128 * k, 128 * k + 128), rows("ngt", 8, 0, n), False, last)
+        for k, h, a, n in bl:
+            r = v("rr", ALL, h, slice(k, k + 1))
+            if a // 512 in (0, 2, 4):
+                C("v", "tensor_reduce", out=r, in_=ps(a, a + n), axis=AxisListType.X, op=A.max)
+            else:
+                C("s", "activation", out=cols("junk", 0, n), in_=ps(a, a + n), func=AF.Relu, accum_out=r)
+        ts(v("nd"), v("rr"), 0.5, A.is_lt)
+        for q in range(3):
+            tt(sub("ttl", 8 * q, 8 * q + 8), sub("sdg", 8 * q, 8 * q + 8), v("nd"), A.mult)
+        tt(sub("ttl", 24, 32), v("go_"), v("nd"), A.mult)
+        for h in range(2):
+            mm(ps(P7 + 128 * h, P7 + 128 * h + 128, 40), v("ttl", ALL, h, ALL), v("idb"))
+        copy("v", rows("t1", 40, 0, NL), ps(P7, P7 + NL, 40))
+        mm(ps(P6, P6 + 16), v("idb"), v("li"), True, False)
+        for i in range(16):
+            mm(ps(P6, P6 + 16), rows("ew", 40, 15 - i, 143 - i), rows("t1", 40, i, NL, 16), False, i == 15)
+        mm(row, rows("er2" if t == 2 else "er", 40, 0, 128), rows("t1", 40, 0, NL))
+        ts(cols(lists, 0, 16), ps(P6, P6 + 16), float(DUMP + NL * t), A.add)
+
+    def tell(src, width, land, sem):
+        far = [c for c in T.cores if off_chip(topo, core, c)]
+        near = [c for c in T.cores if c != core and not off_chip(topo, core, c)]
+        tr = []
+        for ds, en in ((far, far_engines(core, T, topo)), (near, near_engines(core, near[0], T, topo) if near else [])):
+            if ds:
+                tr.append((cols(src, 0, width), [(dst_id(topo, d), cols(land, width * rank, width * rank + width)) for d in ds], en, sem))
+        fused(tr)
+
+    told = sum(len(far_engines(c, T, topo)) if off_chip(topo, c, core) else len(near_engines(c, core, T, topo)) for c in T.cores if c != core)
+
+    def gathered(name, land, width, t, sem):
+        for k in range(NG):
+            sl = slice(16 * k, 16 * k + 16)
+            q = asked(rank, k, t)
+            dma("y", sem, v(name, sl, ALL), v(land, sl, slice(width * q, width * q + width)))
+
+    zrep("zrep", cols("z_s", 64, 320), "rep")
+    dma("s", "d8", v("zql"), v("zqd"))
+    dma("y", "d7", v("efq"), v("rl"))
+    dma("s", "d5", cols("z_s", 320, NF), v("zf", ALL, slice(NL, 704)))
+    dma("s", "d6", cols("z_s", 0, 64), v("zf", ALL, slice(704, NF)))
+    dma("y", "d9", cols("eh_s", 320, NF), v("eh", ALL, slice(NL, 704)))
+    dma("y", "d10", cols("eh_s", 0, 64), v("eh", ALL, slice(704, NF)))
+    dma("y", "d11", cols("ef_s", 64, NF), v("ef", ALL, slice(0, 704)))
+    dma("y", "d12", cols("ef_s", 0, 64), v("ef", ALL, slice(704, NF)))
+    iota(v("ihi"), [[256, 3], [0, 256]], 0, 0)
+    iota(v("ilo"), [[0, 3], [1, 256]], 0, 0)
+    for q, i, c in ((0, 0, 2), (1, 1, 2), (2, 2, 2), (3, 3, -1), (4, 3, -1), (5, 3, -1), (6, 4, -1)):
+        x = rows("err", 56, i, 128, 16)
+        sel(x, x, [[1, 8]], A.not_equal, c, 8 * q, -1)
+    for name, odd in (("ere", 0), ("ero", 1)):
+        for q, i in ((0, 0), (1, 1), (2, 2), (6, 3), (3, 4), (4, 4), (5, 4)):
+            x = rows(name, 56, 16 * odd + i, 128, 32)
+            sel(x, x, [[2, 4]], A.not_equal, 1.0, 8 * q + odd, -1)
+    sel(cols("mmk", 0, 512), v("ob"), [[0, 2], [-1, 256]], A.is_gt, -4096.0, 128, 1)
+    sel(cols("mmk", 512, 1024), v("ob"), [[0, 4], [-1, 128]], A.is_gt, -4096.0, 0, 1)
+    F["after"]("g", ["efq", "zql"])
+    hp = helper_of(core, T, topo)
+    he = topo.engines(core, hp)
+    fused([(v("z_s"), [(dst_id(topo, hp), v("hz"))], he, "a_hz")])
+    fused([(cols("tb", 0, NS), [(dst_id(topo, hp), v("hb"))], he, "a_hb")], "l_hb")
+
+    for j in range(4):
+        look(j, "cmph", "tb", NS, "offh", "zrep")
+        if j == 1:
+            key_mm(0)
+    ts(v("ihi"), v("ihi"), cols("mk", 0, 1), A.mult)
+    ts(v("ilo"), v("ilo"), cols("mk", 8, 9), A.mult)
+    tt(v("ihl"), v("ihi"), v("ilo"), A.add)
+    copy("v", v("offf"), v("efq"))
+    key_mm(1)
+    zrep("zrepf", v("zql"), "rep")
+    for j in range(4):
+        look(j, "cmpf", "tb", NS, "offf", "zrepf")
+        if j == 0:
+            home_tree(0)
+        if j == 1:
+            far_mm(0)
+    far_mm(1)
+    far_tree()
+    for h in range(2):
+        tt(v("wq", ALL, ALL, h), v("m3", ALL, h, slice(0, 8)), v("m3", ALL, h, slice(8, 16)), A.max)
+    dst = [T.cores[asker(rank, k, 0)] for k in range(NG)]
+    eng = singles(core, dst, T, topo)
+    fused([(v("wq", ALL, k, ALL), [(dst_id(topo, dst[k]), v("wland", ALL, k, ALL))], [eng[k]], "a_wf") for k in range(NG)])
+    arrive(v("wland"), "a_wf", NG)
+    gram_rows()
+    masks(range(6))
+    gram()
+    sel(rows("ngc", 8, 0, 1024), rows("zb", 8, 0, 1024), [[1, 8], [0, 128]], A.not_equal, -4096.0, 0, -1)
+    for q, c in ((0, 256), (1, 16), (2, 1)):
+        x = rows("ew", 40, 0, 143)
+        sel(x, x, [[1, 143]], A.not_equal, c, -15 + 128 * q, -16)
+    for name, q, c in (("er", 3, 128), ("er", 4, 1), ("er2", 4, 1)):
+        x = rows(name, 40, 0, 128)
+        sel(x, x, [[1, 8], [0, 16]], A.not_equal, c, 8 * q, -1)
+    sel(v("onb"), cols("ob", 0, 128), [[-16, 8], [0, 16]], A.is_ge, 0.0, 0, 1)
+    sel(v("onb"), v("onb"), [[16, 8], [0, 16]], A.is_ge, 0.0, 15, -1)
+    sel(v("ntr"), v("ntr"), [[16, 8], [0, 16]], A.is_ge, 0.0, 15, -1)
+    sel(v("ntr"), v("ntr"), [[-1, 128]], A.is_gt, 0.0, 0, 1)
+    sel(v("ela"), cols("zb", 0, 144), [[1, 144]], A.not_equal, 1.0, -15, -1)
+    sel(v("elb"), cols("zb", 0, 144), [[1, 144]], A.not_equal, 1.0, -14, -1)
+    iota(cols("idf", 0, 64), [[1, 64]], 704, 0)
+    iota(cols("idf", 64, NF), [[1, 704]], 0, 0)
+    fill(v("occ"), -1.0)
+    ts(v("ela"), v("ela"), cols("mk", 0, 1), A.mult)
+    ts(v("elb"), v("elb"), cols("mk", 8, 9), A.mult)
+    tt(v("el"), v("ela"), v("elb"), A.add)
+
+    for h in range(2):
+        tt(v("wm", ALL, h, ALL), v("whi", ALL, h, ALL), v("wland", ALL, ALL, h), A.max)
+    decide(0, "w0")
+    tell("w0", 16, "la0", "a_l0")
+    arrive(v("la0"), "a_l0", told)
+    for t in (1, 2):
+        arrive(v("fd%d" % t), "a_f%d" % t, 2 * NG)
+        arrive(v("zd%d" % t), "a_f%d" % t, 2 * NG)
+
+    def scatter(table, lists, vals):
+        copy("v", ind(v(table), cols(lists, 0, 16)), vals)
+
+    def wrap(name):
+        copy("v", cols(name, NS, DUMP), cols(name, 0, WR))
+
+    def lanes(t, m0, m1):
+        n = m1 - m0
+        C("v", "scan", out=cols("scn", 0, n), data0=cols("ob", 0, n), data1=cols("uu", 0, n), initial=0.0, op0=A.mult, op1=A.add)
+        mm(ps(0, n), v("ntr"), cols("uu", 0, n), True, False)
+        mm(ps(0, n), v("onb"), cols("scn", 0, n), False, True)
+        first = 0 if t == 1 else 704
+        copy("v", cols("nrow", 0, 64), cols("ihl", first, first + 64))
+        tt(cols("dst", 0, n), ps(0, n), cols("vb", 0, n), A.max)
+        ts(cols("dsu", 0, n), cols("dst", 0, n), 63.0, A.add)
+        copy("v", ind(cols("nrow", 0, 2048), cols("dsu", 0, n)), cols("ihl", 16 * m0, 16 * m1))
+
+    def lanes_end(lists):
+        for i in range(16):
+            mm(ps(512, 528), cols("el", 15 - i, 143 - i), cols("nrow", i, NL, 16), i == 0, i == 15)
+        copy("v", cols(lists, 16, 32), ps(512, 528))
+
+    def step(t):
+        L, tabf, lnf = "w%d" % t, "f%d" % t, "lnf%d" % t
+        ln = cols(L, 16, 32)
+        copy("v", v("zl"), ind(v("z_s"), ln))
+        C("s", "activation", out=v("dc"), in_=ind(v("st"), ln), func=AF.Identity, bias=ckc)
+        tt(v("xp"), ind(v("eh_s"), ln), v("dc"), A.add)
+        ts(v("offh"), v("xp"), ckc, A.subtract)
+        zrep("zrep", v("zl"), "rep")
+        copy("s", v("dl"), ind(v("st"), ln))
+        copy("s", v(lnf), ind(v("idf"), ln))
+        if t == 2:
+            for a, b in ((P6, 0), (P7, 384)):
+                mm(ps(a, a + 384), v("idb"), cols("st", b, b + 384), True, False)
+                mm(ps(a, a + 384), v("idb"), cols("ydm", b, b + 384), False, True)
+                copy("s", cols("stc", b, b + 384), ps(a, a + 384))
+            copy("s", v("st1c"), ind(v("stc"), cols("w1", 16, 32)))
+        masks((2, 3, 4, 5))
+        for j in range(4):
+            look(j, "cmph", "tb", DUMP, "offh", "zrep")
+            if j == 1:
+                key_mm(0)
+                tt(v("xf"), ind(v("ef_s"), ln), v("dc"), A.add)
+            if j == 2:
+                ts(v("offf"), v("xf"), ckc, A.subtract)
+        key_mm(1)
+        if t == 1:
+            scatter("f1", "u10", cols("zf1", 64, 320))
+        else:
+            scatter("f2", "u21", v("zu"))
+        wrap(tabf)
+        home_tree(t)
+        gram_rows()
+        masks((0, 1))
+        for j in range(4):
+            look(j, "cmpf", tabf, DUMP, "offf", "zrep")
+            if j == 1:
+                far_mm(0)
+                gram()
+        far_mm(1)
+        far_tree()
+        tt(v("m4"), *halves("m3", 8), A.max)
+        tt(v("wm"), v("whi"), v("m4"), A.max)
+        decide(t, L)
+
+    ts(cols("uu", 0, 16), ps(P6, P6 + 16), -0.5, A.is_ge)
+    ts(cols("dst", 0, 16), ps(P6, P6 + 16), -0.5, A.is_lt)
+    tt(cols("vb", 0, 16), cols("dst", 0, 16), cols("yc", 4, 20), A.mult)
+    dma("y", "d13", cols("f1", 0, NS), v("fd1"))
+    dma("y", "d14", v("zf1"), v("zd1"))
+    gathered("u10", "la0", 16, 1, "d15")
+    gathered("u20", "la0", 16, 2, "d16")
+    dma("y", "d17", cols("f2", 0, NS), v("fd2"))
+    dma("y", "d18", v("zf2"), v("zd2"))
+    lanes(1, 4, 32)
+    copy("v", cols("st", 64, 320), row)
+    scatter("tb", "w0", cols("z_s", 64, 320))
+    wrap("tb")
+    lanes_end("w1")
+    scatter("occ", "w0", cols("idf", 64, 320))
+    step(1)
+    tell("w1", 32, "la1", "a_l1")
+    arrive(v("la1"), "a_l1", told)
+    gathered("u21", "la1", 32, 2, "d19")
+    scatter("occ", "w1", v("lnf1"))
+    tt(v("st1"), v("dl"), row, A.add)
+    copy("v", ind(v("st"), cols("w1", 16, 32)), v("st1"))
+    tt(v("b1"), ind(v("occ"), v("w0")), cols("idf", 64, 320), A.not_equal)
+    ts(v("zu"), v("b1"), -127.0, A.mult)
+    tt(cols("st", 64, 320), cols("st", 64, 320), v("zu"), A.add)
+    for i in range(16):
+        mm(ps(640, 672), cols("el", 15 - i, 143 - i), cols("st", i, 512, 16), i == 0, i == 15)
+    scatter("tb", "w1", v("zl"))
+    wrap("tb")
+    ts(cols("uu", 0, 32), ps(640, 672), 255.0, A.is_lt)
+    ts(cols("dst", 0, 32), ps(640, 672), 255.0, A.is_ge)
+    fill(cols("vb", 32, 48), 0.0)
+    fill(cols("uu", 32, 48), 1.0)
+    tt(cols("vb", 0, 32), cols("dst", 0, 32), cols("yc", 0, 32), A.mult)
+    lanes(2, 0, 44)
+    ts(v("ydm"), v("st"), 128.0, A.is_ge, -128.0, A.mult)
+    lanes_end("w2")
+    scatter("f2", "u20", cols("zf2", 64, 320))
+    copy("s", v("zu"), ind(v("zf2"), cols("u21", 16, 32)))
+    step(2)
+    scatter("tb", "w2", v("zl"))
+    dma("y", "d20", v("yt"), cols("tb", 0, NS))
+    scatter("occ", "w2", v("lnf2"))
+    dma("s", "d21", v("yo"), v("occ", slice(0, 128, 16), slice(0, NS)))
+    tt(v("st2"), v("dl"), row, A.add)
+    tt(v("zu"), ind(v("occ"), cols("w1", 0, 16)), v("lnf1"), A.not_equal)
+    tt(v("st1c"), v("st1c"), v("zu"), A.add)
+    copy("v", ind(v("stc"), cols("w1", 16, 32)), v("st1c"))
+    tt(v("b3"), ind(v("occ"), v("w0")), cols("idf", 64, 320), A.not_equal)
+    tt(v("b3"), v("b3"), v("b1"), A.is_gt)
+    copy("v", ind(v("stc"), cols("w2", 16, 32)), v("st2"))
+    tt(cols("stc", 64, 320), cols("stc", 64, 320), v("b3"), A.add)
+    dma("y", "d22", v("yd", ALL, slice(0, 704)), v("stc", slice(0, 128, 16), slice(64, NF)))
+    dma("s", "d23", v("yd", ALL, slice(704, NF)), v("stc", slice(0, 128, 16), slice(0, 64)))
+    F["finish"]()
+
+
+def rank_program(g, core, T, topo):
+    rank = T.rank_of(core)
+    if rank is not None:
+        rank_main(g, core, rank, T, topo)
+        return
+    for c in topo.cores_of(core):
+        if T.rank_of(c) is not None and helper_of(c, T, topo) == core:
+            helper_main(g, core, T.rank_of(c), T, topo)
+            return

@@ -1,35 +1,39 @@
 import numpy as np
 from concourse.bass import DstId, RemoteDMATransfer
-from concourse.mybir import AluOpType as A, AxisListType, ActivationFunctionType as AF
+from concourse.mybir import AluOpType as A, ActivationFunctionType as AF
 
 N, NG, NS, NF, NL = 8, 8, 4096, 768, 256
 WR = 32
 NT = NS + WR + 3 * NL
 DUMP = NS + WR
+FIX = 64
+DYN = NL - FIX
+ZC = NL + 16
 TYPES = {"b": "bfloat16", "f": "float32", "i": "int32", "u": "uint16"}
 SCRATCH = {"psb": ("psum", [128, 4096], "float32")}
 for _where, _shape, _names in (
-        ("sbuf", [128, NT], "b:tb b:f1 b:f2 f:occ"), ("sbuf", [128, NF], "i:eh_s i:ef_s b:z_s b:zf1 b:zf2 b:st f:stc b:ydm f:idf b:ihi b:ilo b:ihl"),
-        ("sbuf", [128, 4096], "b:zrep b:zrepf b:cmph b:cmpf"), ("sbuf", [128, 2048], "b:nrow"),
-        ("sbuf", [128, NL], "i:efq b:zql f:xp f:xf f:dc u:offh u:offf b:zl b:dl f:lnf1 f:lnf2 b:st1 f:st1c f:st2 b:b1 b:b3 b:zu "
-                            "b:ctx b:gr b:gle b:glo b:ngt b:t1 b:junk i:rep_i u:rep"),
-        ("sbuf", [128, 16], "u:w0 u:u10 u:u20 f:mk b:li"), ("sbuf", [128, 32], "u:w1 u:w2 u:u21"),
-        ("sbuf", [128, N * 16], "u:la0"), ("sbuf", [128, N * 32], "u:la1"),
-        ("sbuf", [128, 2, 64], "f:kh f:k1 b:fh b:m1"), ("sbuf", [128, 2, 32], "f:k2 b:m2"), ("sbuf", [128, 2, 16], "f:k3 b:m3"),
-        ("sbuf", [128, 2, 8], "i:hki i:whi b:m4 b:wm b:ng b:go_ f:rr b:nd"), ("sbuf", [128, 8, 2], "b:wq b:wland"),
-        ("sbuf", [128, 2, 24], "i:di b:sd b:sdg b:dd0 b:dd1 b:dd2"), ("sbuf", [128, 2, 40], "b:ttl"), ("sbuf", [128, 2, 56], "b:cdl"),
-        ("sbuf", [128, 48], "b:uu f:vb b:scn f:dst u:dsu f:yc"),
-        ("sbuf", [128, 8], "i:pc i:pmi f:ck f:pmf f:pcf b:blkf b:blkk"), ("sbuf", [128, 64], "i:li_i"), ("sbuf", [128, 144], "b:ew b:ela b:elb b:el"),
-        ("sbuf", [128, 128], "f:pmx f:z32 b:idb b:err b:ere b:ero b:er b:er2 b:onb b:ntr"), ("sbuf", [128, 512], "b:ob"),
-        ("sbuf", [128, 1024], "b:zb b:mmk b:ngc"),
-        ("dram", [1024, 32], "i:rd b:zq i:rl b:zqd"), ("dram", [1024, 512], "b:td b:fd1 b:fd2"), ("dram", [1024, 96], "b:zd b:zd1 b:zd2"),
-        ("dram", [128, NS], "b:hb"), ("dram", [128, NF], "b:hz")):
+        ("sbuf", [128, NT], "b:tb f:occ"),
+        ("sbuf", [128, NF], "i:eh_s b:z_s b:pay b:pay2 f:idf b:g1 b:g2 b:g3 f:ydf"),
+        ("sbuf", [128, NF + 64], "i:efq1 i:efq2 b:zq1 b:zq2"),
+        ("sbuf", [128, 4096], "b:zrh b:zrf b:cmh b:cmf b:gth b:gtf"), ("sbuf", [128, 1280], "b:nrow"),
+        ("sbuf", [128, NL], "i:efq0 f:xp f:xq f:dc f:dq u:offh u:offf b:zlh b:zlf f:lnf1 f:lnf2 b:b1 b:b3 b:t1 b:st b:nst "
+                            "f:kh b:kf b:rst b:dm b:m16 b:rr b:pm1 b:pm2 b:mid"),
+        ("sbuf", [128, ZC], "b:r1 b:r2 b:r3"), ("sbuf", [128, 8, 384], "b:eq"), ("sbuf", [128, 384], "b:tri"),
+        ("sbuf", [128, 16], "u:w0 u:lq b:li i:hki b:wq0 b:wq1 b:wq2 u:lst f:tmp"), ("sbuf", [128, 32], "u:w1 u:w2 u:inv1 u:dsu u:lrep i:whi b:wm"),
+        ("sbuf", [128, 24], "f:msg1 f:msg2"), ("sbuf", [128, N * 24], "f:la1 f:la2"), ("sbuf", [128, N * 16], "b:lr0 b:lr1 b:lr2"),
+        ("sbuf", [128, 16, 2], "i:di b:go_ b:ng b:win b:dd0 b:dd1 b:dd2 b:sd b:cd"), ("sbuf", [128, 2, 32], "b:ttl"),
+        ("sbuf", [128, 48], "b:uu f:vb b:scn f:dst f:yc f:yw u:inv2"),
+        ("sbuf", [128, 8], "i:pi i:qi i:q2 b:blkf b:blkh b:blkk b:blkj"), ("sbuf", [128, 32], "f:pc"),
+        ("sbuf", [128, 144], "b:ew b:el b:el2 b:el3 b:eln"),
+        ("sbuf", [128, 128], "f:id32 b:idb b:idn b:er b:onb b:onb1 b:ntr b:ex2 b:mk2 b:ob b:r16"), ("sbuf", [128, 1024], "b:sg"),
+        ("dram", [1024, 32], "i:rd b:zd i:rl b:zl"), ("dram", [1024, 96], "i:rda b:zda i:rl1 i:rl2 b:zl1 b:zl2")):
     for _n in _names.split():
         SCRATCH[_n[2:]] = (_where, _shape, TYPES[_n[0]])
 ENG = {"v": "ev", "s": "es", "p": "ep", "g": "eg"}
-SEMAPHORES = (["ev", "es", "ep", "eg", "lsem", "l_hb", "a_req", "a_wf", "a_l0", "a_l1", "a_f1", "a_f2", "a_hb", "a_hz"]
-              + ["d%d" % k for k in range(24)])
+SEMAPHORES = (["ev", "es", "ep", "eg", "lsem", "a_q0", "a_q1", "a_q2", "a_b1", "a_b2", "a_r0", "a_r1", "a_r2"]
+              + ["d%d" % k for k in range(28)])
 WRITES = ("out", "accum_out", "ap")
+CYCLE, WAKE = 0.83, 60.0
 MASKS = {}
 ALL = slice(None)
 
@@ -61,12 +65,6 @@ def far_engines(core, T, topo):
 def near_engines(core, dst, T, topo):
     far = far_engines(core, T, topo)
     return [e for e in topo.engines(core, dst) if e not in far]
-
-
-def helper_of(core, T, topo):
-    for c in topo.cores_of(core):
-        if T.rank_of(c) is None and topo.die(c) == topo.die(core) and all(topo.may_write(c, d) for d in T.cores):
-            return c
 
 
 def singles(core, dsts, T, topo):
@@ -122,7 +120,7 @@ def region(view):
 def flow(g, T):
     queues = {"v": g.vector, "s": g.scalar, "p": g.tensor, "g": g, "y": g.sync}
     known = {q: {} for q in queues}
-    total, acc = {}, {}
+    total, acc, ops, banks = {}, {}, [], [{} for _ in range(8)]
 
     def ap(x):
         if x[0] == "i":
@@ -139,19 +137,64 @@ def flow(g, T):
                 if x[1] in SCRATCH:
                     yield kind, x[1], region(x)
 
-    def deps(q, reads, writes, tile=None):
-        ev = []
+    def add(q, reads, writes, go, sem, n, busy, late=0.0, after=()):
+        me, dep = len(ops), {k: q != "g" or ops[k]["q"] != "g" for k in after}
         for kind, name, (p0, p1, m, bank) in each(reads, writes):
-            for e in acc.get(name, ()):
-                if bank and (bank & e["bank"]) and (q != e["q"] or (tile is not None and e["tile"] not in (None, tile))):
-                    ev.append(e["ev"])
-                elif (kind == "w" or e["kind"] == "w") and e["p0"] < p1 and p0 < e["p1"] and (m & e["m"]):
-                    if bank and q == "p" and e["q"] == "p":
-                        continue
-                    if kind == "w" and e["kind"] == "r" and q == e["q"] and q in ENG:
-                        continue
-                    ev.append(e["ev"])
-        return ev
+            if bank:
+                for b in range(8):
+                    if bank >> b & 1:
+                        for who, k in banks[b].items():
+                            if k != me:
+                                dep[k] = dep.get(k, False) or who != q
+                        banks[b][q] = me
+                continue
+            old = acc.get(name, [])
+            for e in old:
+                if (kind == "w" or e["kind"] == "w") and e["p0"] < p1 and p0 < e["p1"] and (m & e["m"]) and e["op"] != me:
+                    dep[e["op"]] = True
+            if kind == "w":
+                old = [e for e in old if not (p0 <= e["p0"] and e["p1"] <= p1 and (e["m"] & ~m) == 0)]
+            acc[name] = old + [{"kind": kind, "p0": p0, "p1": p1, "m": m, "op": me}]
+        ops.append({"q": q, "go": go, "sem": sem, "n": n, "busy": busy, "late": late, "dep": dep})
+        return me
+
+    def order():
+        way = [0.0] * len(ops)
+        users = [[] for _ in ops]
+        for k in range(len(ops) - 1, -1, -1):
+            way[k] += ops[k]["busy"] + ops[k]["late"]
+            for d, hard in ops[k]["dep"].items():
+                users[d].append(k)
+                way[d] = max(way[d], way[k] + WAKE if hard else way[k] - ops[d]["late"])
+        left = [len(o["dep"]) for o in ops]
+        ready = [0.0] * len(ops)
+        free = {q: 0.0 for q in list(queues) + [None]}
+        pool = {q: [k for k in range(len(ops)) if ops[k]["q"] == q and not left[k]] for q in free}
+        out = []
+        while len(out) < len(ops):
+            best = None
+            for q in pool:
+                if pool[q]:
+                    now = max(free[q], min(ready[k] for k in pool[q]))
+                    k = max((k for k in pool[q] if ready[k] <= now), key=lambda k: (way[k], -k))
+                    soon = [j for j in pool[q] if now < ready[j] < now + 0.5 * ops[k]["busy"] and way[j] > way[k] + ops[k]["busy"]]
+                    if soon:
+                        k = min(soon, key=lambda j: ready[j])
+                        now = ready[k]
+                    if best is None or now < best[0]:
+                        best = (now, k, q)
+            now, k, q = best
+            pool[q].remove(k)
+            out.append(k)
+            if q is not None:
+                free[q] = now + ops[k]["busy"]
+            for u in users[k]:
+                end = now + ops[k]["busy"]
+                ready[u] = max(ready[u], end + ops[k]["late"] + WAKE if ops[u]["dep"][k] else end)
+                left[u] -= 1
+                if not left[u]:
+                    pool[ops[u]["q"]].append(u)
+        return out
 
     def settle(q, ev):
         need = {}
@@ -167,24 +210,29 @@ def flow(g, T):
                 known[q][k] = max(known[q].get(k, 0), clk[k])
             known[q][sem] = max(known[q].get(sem, 0), cnt)
 
-    def note(q, reads, writes, event, tile=None):
-        for kind, name, (p0, p1, m, bank) in each(reads, writes):
-            old = acc.get(name, [])
-            inside = lambda e: p0 <= e["p0"] and e["p1"] <= p1 and (e["m"] & ~m) == 0
-            if kind == "w" and not bank:
-                old = [e for e in old if not inside(e)]
-            else:
-                old = [e for e in old if not (e["kind"] == kind and e["q"] == q and e["ev"][0] == event[0] and inside(e))]
-            acc[name] = old + [{"kind": kind, "q": q, "p0": p0, "p1": p1, "m": m, "bank": bank, "ev": event, "tile": tile}]
+    def size(x):
+        if x[0] == "i":
+            return 16 * size(x[2])[0], False
+        return bin(region(x)[2]).count("1"), SCRATCH[x[1]][2] in ("bfloat16", "uint16")
 
-    def done(who, q, sem, n, reads, writes, tile=None):
-        total[sem] = total.get(sem, 0) + n
-        clk = dict(known[q])
-        clk[sem] = total[sem]
-        note(who, reads, writes, (sem, total[sem], clk), tile)
+    def cost(q, meth, kw):
+        out = kw.get("out") or kw["ap"]
+        n, views = size(out)[0], [kw[k] for k in kw if is_view(kw[k])]
+        if meth == "matmul":
+            return max(min(64, size(kw["lhsT"])[0]), n) * 0.42 * (1 if size(kw["rhs"])[1] else 4)
+        if meth == "iota":
+            return 130 + 2 * n * CYCLE
+        if out[0] == "i":
+            return 50 + 3.8 * n * CYCLE
+        if any(x[0] == "i" for x in views):
+            return 60 + 1.56 * n * CYCLE
+        if meth == "tensor_tensor":
+            return max(64, n * (1 if any(x[1] == "psb" for x in views) else 2)) * CYCLE
+        narrow = q == "v" and all(size(x)[1] or size(x)[0] == 1 for x in views)
+        return max(64, n / 2 if narrow else n) * CYCLE
 
     def call(q, meth, **kw):
-        reads, writes, tile = [], [], None
+        reads, writes = [], []
         for k in kw:
             x = kw[k]
             if is_view(x):
@@ -193,46 +241,46 @@ def flow(g, T):
                     reads += parts(x)[1:]
                 else:
                     reads += parts(x)
-        if meth == "matmul":
-            p0, p1, m, bank = region(kw["lhsT"])
-            tile = p0 if p1 - p0 <= 32 else None
-        settle(q, deps(q, reads, writes, tile))
         args = {k: (ap(kw[k]) if is_view(kw[k]) else kw[k]) for k in kw}
         eng = queues[q]
         f = {"tensor_copy": lambda: eng.tensor_copy(**args), "tensor_tensor": lambda: eng.tensor_tensor(**args),
-             "tensor_scalar": lambda: eng.tensor_scalar(**args), "tensor_reduce": lambda: eng.tensor_reduce(**args),
+             "tensor_scalar": lambda: eng.tensor_scalar(**args),
              "scan": lambda: eng.tensor_tensor_scan(**args), "memset": lambda: eng.memset(args["ap"], args["constant"]),
              "activation": lambda: eng.activation(**args), "matmul": lambda: eng.matmul(**args),
-             "iota": lambda: eng.iota(**args), "affine_select": lambda: eng.affine_select(**args)}[meth]
-        f().then_inc(T.sem[ENG[q]], 1)
-        done(q, q, ENG[q], 1, reads, writes, tile)
+             "iota": lambda: eng.iota(**args)}[meth]
+        return add(q, reads, writes, lambda: f().then_inc(T.sem[ENG[q]], 1), ENG[q], 1, cost(q, meth, kw))
 
-    def dma(q, sem, out, in_):
-        settle(q, deps(q, [in_], [out]))
-        queues[q].dma_start(out=ap(out), in_=ap(in_)).then_inc(T.sem[sem], 16)
-        done(sem, q, sem, 16, [in_], [out])
+    def dma(q, sem, out, in_, late, after, behind):
+        k = add(q, [in_], [out], lambda: queues[q].dma_start(out=ap(out), in_=ap(in_)).then_inc(T.sem[sem], 16), sem, 16, 60, late, after)
+        if behind is not None:
+            ops[k]["dep"][behind] = False
+        return k
 
-    def arrive(out, sem, cnt):
-        total[sem] = cnt
-        note("far", [], [out], (sem, cnt, {sem: cnt}))
+    def arrive(outs, sem, cnt, mine):
+        return add(None, [], outs, None, sem, cnt, 0, 0, mine)
 
-    def fused(transfers, local="lsem"):
-        srcs = [t[0] for t in transfers]
-        settle("g", deps("g", srcs, []))
-        g.remote_dma_fused([RemoteDMATransfer(dst_ids=[d[0] for d in t[1]], dma_engine_mask=bits(t[2]), remote_sem=T.sem[t[3]],
-                                              srcs=[ap(t[0])], dsts=[ap(d[1]) for d in t[1]]) for t in transfers],
-                           local_sem=T.sem[local])
-        done(local, "g", local, sum(len(t[2]) for t in transfers), srcs if local != "lsem" else [], [])
-
-    def after(q, names):
-        settle(q, [e["ev"] for n in names for e in acc.get(n, ())])
+    def fused(transfers, late, after=()):
+        go = lambda: g.remote_dma_fused(
+            [RemoteDMATransfer(dst_ids=[d[0] for d in t[1]], dma_engine_mask=bits(t[2]), remote_sem=T.sem[t[3]],
+                               srcs=[ap(t[0])], dsts=[ap(d[1]) for d in t[1]]) for t in transfers], local_sem=T.sem["lsem"])
+        return add("g", [t[0] for t in transfers], [], go, "lsem", sum(len(t[2]) for t in transfers), 300, late, after)
 
     def finish():
+        event = {}
+        for k in order():
+            q, sem = ops[k]["q"], ops[k]["sem"]
+            total[sem] = total.get(sem, 0) + ops[k]["n"]
+            if q is None:
+                event[k] = (sem, total[sem], {sem: total[sem]})
+                continue
+            settle(q, [event[d] for d, hard in ops[k]["dep"].items() if hard])
+            ops[k]["go"]()
+            event[k] = (sem, total[sem], dict(known[q], **{sem: total[sem]}))
         for sem in total:
             if known["g"].get(sem, 0) < total[sem]:
                 g.wait_ge(T.sem[sem], total[sem])
 
-    return {"call": call, "dma": dma, "arrive": arrive, "fused": fused, "after": after, "finish": finish}
+    return {"call": call, "dma": dma, "arrive": arrive, "fused": fused, "finish": finish}
 
 
 def blk(name, k):
@@ -247,38 +295,24 @@ def rows(name, n, a, b, step=None):
     return v(name, slice(0, n), slice(a, b, step))
 
 
-def sub(name, a, b):
-    return v(name, ALL, ALL, slice(a, b))
-
-
-def halves(a, n):
-    return sub(a, 0, n), sub(a, n, 2 * n)
-
-
-def helper_main(g, core, rank, T, topo):
-    F = flow(g, T)
-    F["arrive"](v("hb"), "a_hb", len(topo.engines(T.cores[rank], core)))
-    F["arrive"](v("hz"), "a_hz", len(topo.engines(T.cores[rank], core)))
-    F["dma"]("s", "d1", v("zd"), v("hz"))
-    F["dma"]("y", "d0", v("td"), v("hb"))
-    for t in (1, 2):
-        dst = [T.cores[asker(rank, k, t)] for k in range(NG)]
-        eng = singles(core, dst, T, topo)
-        for src, land in (("zd", "zd%d" % t), ("td", "fd%d" % t)):
-            F["fused"]([(blk(src, k), [(dst_id(topo, dst[k]), blk(land, k))], [eng[k]], "a_f%d" % t) for k in range(NG)])
-    F["finish"]()
-
-
 def rank_main(g, core, rank, T, topo):
     F = flow(g, T)
-    C, dma, arrive, fused = F["call"], F["dma"], F["arrive"], F["fused"]
-    ps = lambda a, b, n=128: v("psb", slice(0, n), slice(a, b))
-    P6, P7 = 3072, 3584
+    C, arrive, fused = F["call"], F["arrive"], F["fused"]
+    ps = lambda a, b, n=128, step=None: v("psb", slice(0, n), slice(a, b, step))
+    KH, KF, P6, P7 = 2048, 2560, 3072, 3584
     row = ps(P7 + 256, P7 + 512)
+    nd, turn = [0], [0]
+
+    def dma(q, out, in_, late=3000, after=(), behind=None):
+        nd[0] += 1
+        return F["dma"](q, "d%d" % nd[0], out, in_, late, after, behind)
+
+    def act(out, in_, func=AF.Copy, **kw):
+        C("s", "activation", out=out, in_=in_, func=func, **kw)
 
     def copy(q, out, in_):
         if q == "s":
-            C("s", "activation", out=out, in_=in_, func=AF.Copy)
+            act(out, in_)
         else:
             C("v", "tensor_copy", out=out, in_=in_)
 
@@ -303,164 +337,13 @@ def rank_main(g, core, rank, T, topo):
         else:
             C("g", "iota", out=out, pattern=pattern, base=base, channel_multiplier=ch, allow_small_or_imprecise_dtypes=True)
 
-    def sel(out, in_, pattern, op, fillv, base, ch):
-        C("g", "affine_select", out=out, in_=in_, pattern=pattern, compare_op=op, fill=float(fillv), base=base, channel_multiplier=ch)
+    def by_group(pairs, dst, sem, late, after=()):
+        eng = singles(core, dst, T, topo)
+        mine = [fused([(blk(src, k), [(dst_id(topo, dst[k]), blk(land, k))], [eng[k]], sem) for k in range(NG)], late, after)
+                for src, land in pairs]
+        return arrive([v(land) for src, land in pairs], sem, len(pairs) * NG, mine)
 
-    dma("y", "d0", v("rd"), v("ef", ALL, slice(0, NL)))
-    dma("s", "d1", v("zq"), v("zf", ALL, slice(0, NL)))
-    dma("s", "d3", cols("z_s", 64, 320), v("zf", ALL, slice(0, NL)))
-    dma("y", "d2", cols("eh_s", 64, 320), v("eh", ALL, slice(0, NL)))
-    dma("y", "d4", cols("tb", 0, NS), v("tab"))
-
-    iota(v("rep_i"), [[1, NL]], 0, 0)
-    copy("v", v("rep"), v("rep_i"))
-    iota(v("pc"), [[0, 8]], 0, 1)
-    fill(v("z32"), 0.0)
-    fill(v("ob"), 1.0)
-    fill(v("zb"), 0.0)
-    ts(v("pmi"), v("pc"), 15, A.bitwise_and)
-    ts(v("ck"), v("pmi"), -8192.0, A.mult, 122880.0, A.add)
-    copy("v", v("pmf"), v("pmi"))
-    sel(v("pmx"), v("z32"), [[1, 16], [16, 8]], A.not_equal, 1.0, 0, -1)
-    sel(v("blkf"), cols("ob", 0, 8), [[-16, 8]], A.is_ge, 0.0, 0, 1)
-    sel(v("blkf"), v("blkf"), [[16, 8]], A.is_ge, 0.0, 15, -1)
-    ckc, pmc = cols("ck", 0, 1), cols("pmf", 0, 1)
-
-    dst = [T.cores[asked(rank, k, 0)] for k in range(NG)]
-    eng = singles(core, dst, T, topo)
-    for src, land in (("zq", "zqd"), ("rd", "rl")):
-        fused([(blk(src, k), [(dst_id(topo, dst[k]), blk(land, k))], [eng[k]], "a_req") for k in range(NG)])
-    arrive(v("rl"), "a_req", 2 * NG)
-    arrive(v("zqd"), "a_req", 2 * NG)
-
-    iota(v("li_i"), [[16, 64]], 0, 0)
-    sel(v("idb"), cols("zb", 0, 128), [[1, 128]], A.not_equal, 1.0, 0, -1)
-    ts(cols("mk", 0, 8), v("pmf"), 0.0, A.is_equal)
-    ts(cols("mk", 8, 16), v("pmf"), 1.0, A.is_equal)
-    ts(v("blkk"), v("blkf"), 131072.0, A.mult)
-    ts(v("xp"), cols("eh_s", 64, 320), ckc, A.add)
-    copy("v", v("offh"), cols("eh_s", 64, 320))
-    copy("v", v("pcf"), v("pc"))
-    for t in range(3):
-        n = "dd%d" % t
-        fill(sub(n, 0, 8), 8.0 + t)
-        for h in range(2):
-            fill(v(n, ALL, h, slice(8, 16)), -6.0 + 8 * h)
-            ts(v(n, ALL, h, slice(16, 24)), v("pcf"), -8.0, A.add)
-    fill(sub("cdl", 48, 56), 1.0)
-    fill(v("st"), 0.0)
-    fill(v("uu"), 1.0)
-    fill(v("vb"), 0.0)
-    fill(v("ntr"), -1.0)
-    for name in ("err", "ere", "ero", "er", "er2"):
-        copy("v", v(name), cols("zb", 0, 128))
-    copy("v", v("ew"), cols("zb", 0, 144))
-    ts(v("li"), cols("li_i", 0, 16), pmc, A.add)
-    ts(v("yc"), cols("li_i", 0, 48), pmc, A.add, 961.0, A.add)
-
-    def zrep(out, win, lists):
-        for j in range(4):
-            copy("s", cols(out, 1024 * j, 1024 * j + 1024), ind(win, cols(lists, 64 * j, 64 * j + 64)))
-
-    def look(j, out, table, width, off, rep_):
-        tt(cols(out, 1024 * j, 1024 * j + 1024), ind(cols(table, 0, width), cols(off, 64 * j, 64 * j + 64)),
-           cols(rep_, 1024 * j, 1024 * j + 1024), A.is_le)
-
-    def cmpcol(name, h, k):
-        return cols(name, 2048 * h + k, 2048 * h + 2048, 16)
-
-    def key_mm(h):
-        b = 512 * h
-        mm(ps(b, b + 128), cols("xp", 128 * h, 128 * h + 128), v("pmx"), True, False)
-        for k in range(16):
-            mm(ps(b + 8 * k, b + 8 * k + 8), cmpcol("cmph", h, k), v("blkk"), False, k == 15)
-        copy("s", v("kh", ALL, h, ALL), ps(b + 64, b + 128))
-
-    def home_tree(t):
-        for h in range(2):
-            tt(v("k1", ALL, h, ALL), ps(512 * h, 512 * h + 64), v("kh", ALL, h, ALL), A.max)
-        tt(v("k2"), *halves("k1", 32), A.max)
-        tt(v("k3"), *halves("k2", 16), A.max)
-        tt(v("hki"), *halves("k3", 8), A.max)
-        for q, sh in ((0, 8), (1, 4)):
-            ts(sub("di", 8 * q, 8 * q + 8), v("hki"), sh, A.arith_shift_right, 15, A.bitwise_and)
-        ts(sub("di", 16, 24), v("hki"), 15, A.bitwise_and)
-        ts(v("whi"), v("hki"), 17, A.arith_shift_right)
-        ts(sub("cdl", 0, 24), v("di"), -8.0, A.add)
-        C("s", "activation", out=sub("cdl", 24, 48), in_=sub("cdl", 0, 24), func=AF.Square)
-        tt(v("sd"), sub("cdl", 0, 24), v("dd%d" % t), A.subtract)
-
-    def gram_rows():
-        for h in range(2):
-            mm(ps(P7 + 128 * h, P7 + 128 * h + 128, 56), v("cdl", ALL, h, ALL), v("idb"))
-        ct = rows("ctx", 56, 0, NL)
-        copy("s", ct, ps(P7, P7 + NL, 56))
-        for name, e, b in (("gr", "err", P7 + 256), ("gle", "ere", 0), ("glo", "ero", 256)):
-            mm(ps(b, b + NL), rows(e, 56, 0, 128), ct)
-        for name, b in (("gr", P7 + 256), ("gle", 0), ("glo", 256)):
-            copy("s", v(name), ps(b, b + NL))
-
-    def masks(bs):
-        for b in bs:
-            mm(ps(512 * b, 512 * b + 512), v("idb"), cols("mmk", 0, 512) if b < 4 else cols("mmk", 512, 1024), True, False)
-
-    def blocks():
-        out = []
-        for b in (3, 2, 5, 4, 1, 0):
-            if b < 4:
-                out += [(2 * b + x, 1, 512 * b + 256 * x, 256) for x in range(2)]
-            else:
-                out += [(4 * (b - 4) + x, 0, 512 * b + 128 * x, 128) for x in range(4)]
-        return out
-
-    def gram():
-        for k, h, a, n in blocks():
-            sl = slice(32 * (k // 2), 32 * (k // 2) + 32)
-            mm(ps(a, a + n), v("gle" if k % 2 == 0 else "glo", sl, slice(128 * h, 128 * h + 128)), v("gr", sl, slice(0, n)), False, False)
-
-    def far_mm(h):
-        for k in range(16):
-            a = P6 + 128 * h + 8 * k
-            mm(ps(a, a + 8), cmpcol("cmpf", h, k), v("blkf"))
-        copy("s", v("fh", ALL, h, ALL), ps(P6 + 128 * h + 64, P6 + 128 * h + 128))
-
-    def far_tree():
-        for h in range(2):
-            tt(v("m1", ALL, h, ALL), ps(P6 + 128 * h, P6 + 128 * h + 64), v("fh", ALL, h, ALL), A.max)
-        tt(v("m2"), *halves("m1", 32), A.max)
-        tt(v("m3"), *halves("m2", 16), A.max)
-
-    def decide(t, lists):
-        ts(v("ng"), v("wm"), 8.0, A.is_ge)
-        for h in range(2):
-            mm(ps(P7 + 128 * h, P7 + 128 * h + 128, 8), v("ng", ALL, h, ALL), v("idb"))
-        copy("s", rows("ngt", 8, 0, NL), ps(P7, P7 + NL, 8))
-        ts(v("go_"), v("wm"), 8.0, A.is_lt)
-        tt(sub("ttl", 32, 40), v("wm"), v("ng"), A.mult)
-        for q in range(3):
-            tt(sub("sdg", 8 * q, 8 * q + 8), sub("sd", 8 * q, 8 * q + 8), v("go_"), A.mult)
-        bl = blocks()
-        for j, (k, h, a, n) in enumerate(bl):
-            last = j == len(bl) - 1 or bl[j + 1][2] // 512 != a // 512
-            mm(ps(a, a + n), rows("ngc", 8, 128 * k, 128 * k + 128), rows("ngt", 8, 0, n), False, last)
-        for k, h, a, n in bl:
-            r = v("rr", ALL, h, slice(k, k + 1))
-            if a // 512 in (0, 2, 4):
-                C("v", "tensor_reduce", out=r, in_=ps(a, a + n), axis=AxisListType.X, op=A.max)
-            else:
-                C("s", "activation", out=cols("junk", 0, n), in_=ps(a, a + n), func=AF.Relu, accum_out=r)
-        ts(v("nd"), v("rr"), 0.5, A.is_lt)
-        for q in range(3):
-            tt(sub("ttl", 8 * q, 8 * q + 8), sub("sdg", 8 * q, 8 * q + 8), v("nd"), A.mult)
-        tt(sub("ttl", 24, 32), v("go_"), v("nd"), A.mult)
-        for h in range(2):
-            mm(ps(P7 + 128 * h, P7 + 128 * h + 128, 40), v("ttl", ALL, h, ALL), v("idb"))
-        copy("v", rows("t1", 40, 0, NL), ps(P7, P7 + NL, 40))
-        mm(ps(P6, P6 + 16), v("idb"), v("li"), True, False)
-        for i in range(16):
-            mm(ps(P6, P6 + 16), rows("ew", 40, 15 - i, 143 - i), rows("t1", 40, i, NL, 16), False, i == 15)
-        mm(row, rows("er2" if t == 2 else "er", 40, 0, 128), rows("t1", 40, 0, NL))
-        ts(cols(lists, 0, 16), ps(P6, P6 + 16), float(DUMP + NL * t), A.add)
+    told = sum(len(far_engines(c, T, topo)) if off_chip(topo, c, core) else len(near_engines(c, core, T, topo)) for c in T.cores if c != core)
 
     def tell(src, width, land, sem):
         far = [c for c in T.cores if off_chip(topo, core, c)]
@@ -469,218 +352,385 @@ def rank_main(g, core, rank, T, topo):
         for ds, en in ((far, far_engines(core, T, topo)), (near, near_engines(core, near[0], T, topo) if near else [])):
             if ds:
                 tr.append((cols(src, 0, width), [(dst_id(topo, d), cols(land, width * rank, width * rank + width)) for d in ds], en, sem))
-        fused(tr)
+        mine = fused(tr, 3000)
+        arrive([cols(land, width * r, width * r + width) for r in range(N) if r != rank], sem, told, [mine])
+        return mine
 
-    told = sum(len(far_engines(c, T, topo)) if off_chip(topo, c, core) else len(near_engines(c, core, T, topo)) for c in T.cores if c != core)
+    first = [dma("y", v("rd"), v("ef", ALL, slice(0, NL))),
+             dma("s", v("zd"), v("zf", ALL, slice(0, NL))),
+             dma("s", cols("z_s", 64, 320), v("zf", ALL, slice(0, NL))),
+             dma("y", cols("eh_s", 64, 320), v("eh", ALL, slice(0, NL)))]
+    table = dma("y", cols("tb", 0, NS), v("tab"), 6000, behind=first[3])
 
-    def gathered(name, land, width, t, sem):
+    iota(v("pi"), [[0, 8]], 0, 1)
+    iota(v("rr"), [[1, NL]], 0, 0)
+    iota(v("r16"), [[1, 8], [0, 16]], 0, 0)
+    iota(v("m16"), [[0, 16], [1, 16]], 0, 0)
+    by_group((("zd", "zl"), ("rd", "rl")), [T.cores[asked(rank, k, 0)] for k in range(NG)], "a_q0", 5000)
+
+    PC = {n: cols("pc", k, k + 1) for k, n in enumerate(
+        "p a g ck m0 m1 m01 m2 m3 c15 half wq ewc erc h1 h2 x y".split())}
+    pint = cols("pi", 0, 1)
+
+    def bitcol(out, sh, mask):
+        ts(cols("qi", 0, 1), pint, sh, A.arith_shift_right, mask, A.bitwise_and)
+        copy("v", out, cols("qi", 0, 1))
+
+    copy("v", PC["p"], pint)
+    bitcol(PC["a"], 0, 15)
+    bitcol(PC["g"], 4, 7)
+    ts(PC["ck"], PC["a"], -8192.0, A.mult, 122880.0, A.add)
+    r128, r144 = cols("rr", 0, 128), cols("rr", 0, 144)
+    ts(v("id32"), r128, PC["p"], A.is_equal)
+    ts(v("idb"), r128, PC["p"], A.is_equal)
+    ts(v("idn"), r128, PC["p"], A.is_equal, -1.0, A.mult)
+    for name, w in (("blkf", 1.0), ("blkh", 0.5), ("blkk", 131072.0), ("blkj", 65536.0)):
+        ts(v(name), cols("rr", 0, 8), PC["g"], A.is_equal, w, A.mult)
+    fill(v("ob"), 1.0)
+    fill(cols("mid", 0, 128), 8.0)
+    fill(cols("mid", 128, NL), 8.0 * 131072)
+    ts(v("xp"), cols("eh_s", 64, 320), PC["ck"], A.add)
+    copy("v", v("offh"), cols("eh_s", 64, 320))
+    ts(v("rst"), v("m16"), 0.0, A.not_equal)
+
+    def zrep(q, tab, a, b, src=None):
+        for k in range(16):
+            copy(q, cols("zr" + tab, 16 * a + k, 16 * b, 16), src or cols("zl" + tab, a, b))
+
+    def look(q, tab, a, b, width=DUMP, src=None):
+        n, h, p0 = b - a, a // 128, a % 128
+        z = src or cols("zl" + tab, a, b)
+        base = (KH if tab == "h" else KF) + 128 * h
+        out = lambda x, y, step=None: v("psb", slice(p0, p0 + n), slice(base + x, base + y, step))
+        got = ind(cols("tb", 0, width), cols("off" + tab, a, b))
+        if q == "v":
+            tt(cols("cm" + tab, 16 * a, 16 * b), got, cols("zr" + tab, 16 * a, 16 * b), A.is_le)
+            lhs = lambda k: cols("cm" + tab, 16 * a + k, 16 * b, 16)
+        else:
+            act(cols("gt" + tab, 16 * a, 16 * b), got)
+            per = 512 // n
+            for k0 in range(0, 16, per):
+                bank = 512 * (turn[0] % 4)
+                turn[0] += 1
+                for k in range(k0, k0 + per):
+                    o = ps(bank + n * (k - k0), bank + n * (k - k0 + 1))
+                    mm(o, v("idn"), z, True, False)
+                    mm(o, v("idb"), cols("gt" + tab, 16 * a + k, 16 * b, 16), False, True)
+                act(cols("cm" + tab, 16 * a + n * k0, 16 * a + n * (k0 + per)), ps(bank, bank + 512), AF.Sign, scale=-1.0, bias=0.5)
+            lhs = lambda k: cols("cm" + tab, 16 * a + n * k, 16 * a + n * (k + 1))
+
+        def sums():
+            first = tab == "f" and q == "v"
+            if tab == "h":
+                mm(out(0, 128), cols("xp", a, b), v("id32"), True, False)
+            if q == "s":
+                mm(out(0, 128), rows("ob", 1, 0, n), rows("mid", 1, 128, NL) if tab == "h" else rows("mid", 1, 0, 128), tab == "f", False)
+            w = {"hv": "blkk", "hs": "blkj", "fv": "blkf", "fs": "blkh"}[tab + q]
+            for k in range(16):
+                mm(out(k, 128, 16), lhs(k), v(w), first, first or k == 15)
+        return sums
+
+    lane = lambda name, h, x=ALL: v(name, ALL, slice(8 * h, 8 * h + 8), x)
+
+    def choose(t):
+        C("v", "scan", out=v("kh"), data0=v("rst"), data1=ps(KH, KH + NL), initial=0.0, op0=A.mult, op1=A.max)
+        copy("v", v("hki"), cols("kh", 15, NL, 16))
+        ts(v("di", ALL, ALL, 0), v("hki"), 6, A.arith_shift_right, 63, A.bitwise_and)
+        ts(v("di", ALL, ALL, 1), v("hki"), 63, A.bitwise_and)
+        copy("v", v("cd"), v("di"))
+        for h in range(2):
+            mm(ps(P7 + 128 * h, P7 + 128 * h + 128, 16), lane("cd", h), v("idb"))
+        act(rows("st", 16, 0, NL), ps(P7, P7 + NL, 16))
+        act(rows("nst", 16, 0, NL), ps(P7, P7 + NL, 16), scale=-1.0)
+        for x in range(2):
+            ts(cols("whi", x, 32, 2), v("hki"), 17, A.arith_shift_right)
+        tt(v("sd"), v("cd"), v("dd%d" % t), A.subtract)
+
+    def alike(ks):
+        for k in ks:
+            bank = 512 * (turn[0] % 4)
+            turn[0] += 1
+            sel = rows("sg", 16, 128 * k, 128 * k + 128)
+            for c, j, i in ((0, 0, 0), (128, 0, 128), (256, 128, 128)):
+                mm(ps(bank + c, bank + c + 128), sel, rows("st", 16, i, i + 128), True, False)
+                mm(ps(bank + c, bank + c + 128), rows("nst", 16, j, j + 128), sel, False, True)
+            tt(v("eq", ALL, k, ALL), ps(bank, bank + 384), v("tri"), A.is_equal)
+
+    def answer(t):
+        C("v", "scan", out=v("kf"), data0=v("rst"), data1=ps(KF, KF + NL), initial=0.0, op0=A.mult, op1=A.max)
+        copy("v", v("wq%d" % t), cols("kf", 15, NL, 16))
+        return tell("wq%d" % t, 16, "lr%d" % t, "a_r%d" % t)
+
+    def decide(t, lists):
+        mm(ps(P6, P6 + 16), v("idb"), v("li"), True, False)
+        tt(v("wm"), ind(v("lr%d" % t), cols("lst", 4 + 2 * t, 6 + 2 * t)), v("whi"), A.max)
+        ts(v("go_"), v("wm"), 8.0, A.is_lt)
+        ts(v("ng"), v("wm"), 8.0, A.is_ge)
         for k in range(NG):
-            sl = slice(16 * k, 16 * k + 16)
-            q = asked(rank, k, t)
-            dma("y", sem, v(name, sl, ALL), v(land, sl, slice(width * q, width * q + width)))
+            for c, j, i in ((0, 0, 0), (128, 0, 1), (256, 1, 1)):
+                a = KF + 16 * i + 2 * k
+                mm(ps(a, a + 2), v("eq", ALL, k, slice(c, c + 128)), v("go_", ALL, 8 * j + k, ALL), c != 256, c != 128)
+        for h in range(2):
+            tt(v("ttl", ALL, h, slice(24, 32)), cols("wm", 16 * h, 16 * h + 16, 2), lane("ng", h, 0), A.mult)
+        tt(v("win"), ps(KF, KF + 32), v("go_"), A.is_lt)
+        tt(v("ttl", ALL, ALL, slice(0, 16)), v("sd"), v("win"), A.mult)
+        copy("v", v("ttl", ALL, ALL, slice(16, 24)), v("win", ALL, ALL, 0))
+        for h in range(2):
+            mm(ps(P7 + 128 * h, P7 + 128 * h + 128, 32), v("ttl", ALL, h, ALL), v("idb"))
+        copy("v", rows("t1", 32, 0, NL), ps(P7, P7 + NL, 32))
+        for i in range(16):
+            mm(ps(P6, P6 + 16), rows("ew", 32, 15 - i, 143 - i), rows("t1", 32, i, NL, 16), False, i == 15)
+        mm(row, rows("er", 32, 0, 128), rows("t1", 32, 0, NL))
+        ts(cols(lists, 0, 16), ps(P6, P6 + 16), float(DUMP + NL * t), A.add)
 
-    zrep("zrep", cols("z_s", 64, 320), "rep")
-    dma("s", "d8", v("zql"), v("zqd"))
-    dma("y", "d7", v("efq"), v("rl"))
-    dma("s", "d5", cols("z_s", 320, NF), v("zf", ALL, slice(NL, 704)))
-    dma("s", "d6", cols("z_s", 0, 64), v("zf", ALL, slice(704, NF)))
-    dma("y", "d9", cols("eh_s", 320, NF), v("eh", ALL, slice(NL, 704)))
-    dma("y", "d10", cols("eh_s", 0, 64), v("eh", ALL, slice(704, NF)))
-    dma("y", "d11", cols("ef_s", 64, NF), v("ef", ALL, slice(0, 704)))
-    dma("y", "d12", cols("ef_s", 0, 64), v("ef", ALL, slice(704, NF)))
-    iota(v("ihi"), [[256, 3], [0, 256]], 0, 0)
-    iota(v("ilo"), [[0, 3], [1, 256]], 0, 0)
-    for q, i, c in ((0, 0, 2), (1, 1, 2), (2, 2, 2), (3, 3, -1), (4, 3, -1), (5, 3, -1), (6, 4, -1)):
-        x = rows("err", 56, i, 128, 16)
-        sel(x, x, [[1, 8]], A.not_equal, c, 8 * q, -1)
-    for name, odd in (("ere", 0), ("ero", 1)):
-        for q, i in ((0, 0), (1, 1), (2, 2), (6, 3), (3, 4), (4, 4), (5, 4)):
-            x = rows(name, 56, 16 * odd + i, 128, 32)
-            sel(x, x, [[2, 4]], A.not_equal, 1.0, 8 * q + odd, -1)
-    sel(cols("mmk", 0, 512), v("ob"), [[0, 2], [-1, 256]], A.is_gt, -4096.0, 128, 1)
-    sel(cols("mmk", 512, 1024), v("ob"), [[0, 4], [-1, 128]], A.is_gt, -4096.0, 0, 1)
-    F["after"]("g", ["efq", "zql"])
-    hp = helper_of(core, T, topo)
-    he = topo.engines(core, hp)
-    fused([(v("z_s"), [(dst_id(topo, hp), v("hz"))], he, "a_hz")])
-    fused([(cols("tb", 0, NS), [(dst_id(topo, hp), v("hb"))], he, "a_hb")], "l_hb")
-
-    for j in range(4):
-        look(j, "cmph", "tb", NS, "offh", "zrep")
-        if j == 1:
-            key_mm(0)
-    ts(v("ihi"), v("ihi"), cols("mk", 0, 1), A.mult)
-    ts(v("ilo"), v("ilo"), cols("mk", 8, 9), A.mult)
-    tt(v("ihl"), v("ihi"), v("ilo"), A.add)
-    copy("v", v("offf"), v("efq"))
-    key_mm(1)
-    zrep("zrepf", v("zql"), "rep")
-    for j in range(4):
-        look(j, "cmpf", "tb", NS, "offf", "zrepf")
-        if j == 0:
-            home_tree(0)
-        if j == 1:
-            far_mm(0)
-    far_mm(1)
-    far_tree()
-    for h in range(2):
-        tt(v("wq", ALL, ALL, h), v("m3", ALL, h, slice(0, 8)), v("m3", ALL, h, slice(8, 16)), A.max)
-    dst = [T.cores[asker(rank, k, 0)] for k in range(NG)]
-    eng = singles(core, dst, T, topo)
-    fused([(v("wq", ALL, k, ALL), [(dst_id(topo, dst[k]), v("wland", ALL, k, ALL))], [eng[k]], "a_wf") for k in range(NG)])
-    arrive(v("wland"), "a_wf", NG)
-    gram_rows()
-    masks(range(6))
-    gram()
-    sel(rows("ngc", 8, 0, 1024), rows("zb", 8, 0, 1024), [[1, 8], [0, 128]], A.not_equal, -4096.0, 0, -1)
-    for q, c in ((0, 256), (1, 16), (2, 1)):
-        x = rows("ew", 40, 0, 143)
-        sel(x, x, [[1, 143]], A.not_equal, c, -15 + 128 * q, -16)
-    for name, q, c in (("er", 3, 128), ("er", 4, 1), ("er2", 4, 1)):
-        x = rows(name, 40, 0, 128)
-        sel(x, x, [[1, 8], [0, 16]], A.not_equal, c, 8 * q, -1)
-    sel(v("onb"), cols("ob", 0, 128), [[-16, 8], [0, 16]], A.is_ge, 0.0, 0, 1)
-    sel(v("onb"), v("onb"), [[16, 8], [0, 16]], A.is_ge, 0.0, 15, -1)
-    sel(v("ntr"), v("ntr"), [[16, 8], [0, 16]], A.is_ge, 0.0, 15, -1)
-    sel(v("ntr"), v("ntr"), [[-1, 128]], A.is_gt, 0.0, 0, 1)
-    sel(v("ela"), cols("zb", 0, 144), [[1, 144]], A.not_equal, 1.0, -15, -1)
-    sel(v("elb"), cols("zb", 0, 144), [[1, 144]], A.not_equal, 1.0, -14, -1)
-    iota(cols("idf", 0, 64), [[1, 64]], 704, 0)
-    iota(cols("idf", 64, NF), [[1, 704]], 0, 0)
-    fill(v("occ"), -1.0)
-    ts(v("ela"), v("ela"), cols("mk", 0, 1), A.mult)
-    ts(v("elb"), v("elb"), cols("mk", 8, 9), A.mult)
-    tt(v("el"), v("ela"), v("elb"), A.add)
-
-    for h in range(2):
-        tt(v("wm", ALL, h, ALL), v("whi", ALL, h, ALL), v("wland", ALL, ALL, h), A.max)
-    decide(0, "w0")
-    tell("w0", 16, "la0", "a_l0")
-    arrive(v("la0"), "a_l0", told)
-    for t in (1, 2):
-        arrive(v("fd%d" % t), "a_f%d" % t, 2 * NG)
-        arrive(v("zd%d" % t), "a_f%d" % t, 2 * NG)
+    def wrapped(a, n, el, src, first, start=True, stop=True):
+        for i in range(16):
+            mm(ps(a, a + n), cols(el, 15 - i, 143 - i), cols(src, first + i, first + 16 * n, 16), start and i == 0, stop and i == 15)
 
     def scatter(table, lists, vals):
         copy("v", ind(v(table), cols(lists, 0, 16)), vals)
 
-    def wrap(name):
-        copy("v", cols(name, NS, DUMP), cols(name, 0, WR))
+    def wrap():
+        copy("v", cols("tb", NS, DUMP), cols("tb", 0, WR))
 
-    def lanes(t, m0, m1):
+    zrep("s", "h", 0, 128, cols("z_s", 64, 192))
+    zrep("s", "h", 128, 160, cols("z_s", 192, 224))
+    asks = [dma("y", v("efq0"), v("rl")), dma("y", v("zlf"), v("zl"))]
+    ts(PC["m0"], PC["a"], 0.0, A.is_equal)
+    ts(PC["m1"], PC["a"], 1.0, A.is_equal)
+    ts(PC["m01"], PC["a"], 2.0, A.is_lt)
+    ts(PC["m2"], PC["a"], 2.0, A.is_equal)
+    ts(PC["m3"], PC["a"], 3.0, A.is_equal)
+    ts(PC["c15"], PC["g"], 16.0, A.mult, 15.0, A.add)
+    for name, m, w in (("el", "m01", None), ("el2", "m2", None), ("el3", "m3", None), ("eln", "m0", -1.0)):
+        ts(v(name), r144, PC["c15"], A.is_equal, PC[m], A.mult)
+    ts(v("eln"), v("eln"), -1.0, A.mult)
+    bitcol(PC["half"], 1, 63)
+    bitcol(PC["x"], 0, 1)
+    ts(PC["wq"], PC["x"], -63.0, A.mult, 64.0, A.add)
+    ts(PC["x"], PC["p"], 16.0, A.is_lt)
+    tt(PC["wq"], PC["wq"], PC["x"], A.mult)
+    ts(PC["ewc"], PC["half"], 16.0, A.mult, 15.0, A.add)
+    ts(v("ew"), r144, PC["ewc"], A.is_equal, PC["wq"], A.mult)
+    ts(cols("tmp", 0, 8), cols("rr", 0, 8), PC["half"], A.is_equal, PC["wq"], A.mult)
+    for k in range(NG):
+        ts(rows("sg", 16, 128 * k, 128 * k + 128), rows("ob", 16, 0, 128), rows("tmp", 16, k, k + 1), A.mult)
+    ts(PC["x"], PC["p"], 24.0, A.is_ge, -129.0, A.mult)
+    ts(PC["erc"], PC["p"], 16.0, A.mult, -253.0, A.add)
+    tt(PC["erc"], PC["erc"], PC["x"], A.add)
+    ts(v("er"), r128, PC["erc"], A.is_equal)
+    ts(v("onb"), v("r16"), PC["g"], A.is_equal)
+    ts(v("ex2"), v("onb"), PC["m2"], A.mult)
+    ts(v("mk2"), v("idb"), PC["m2"], A.mult)
+    ts(v("ntr"), r128, PC["p"], A.is_lt, -1.0, A.mult)
+    tt(v("ntr"), v("ntr"), v("onb"), A.mult)
+    ts(v("onb1"), cols("m16", 0, 128), 1.0, A.is_equal, -1.0, A.mult)
+    tt(v("onb1"), v("onb1"), v("onb"), A.mult)
+    ts(cols("tri", 0, 128), r128, PC["p"], A.is_le, 0.5, A.mult)
+    fill(cols("tri", 128, 256), 0.0)
+    copy("v", cols("tri", 256, 384), cols("tri", 0, 128))
+    ts(v("m16"), v("m16"), PC["a"], A.is_equal)
+    for t in range(3):
+        for h in range(2):
+            fill(lane("dd%d" % t, h, 0), 64.0 + 4 * t + 2 * h)
+        ts(v("dd%d" % t, ALL, ALL, 1), cols("ob", 0, 16), PC["p"], A.mult, 32.0, A.add)
+    ts(v("yw"), cols("rr", 0, 48), 16.0, A.mult, PC["a"], A.add)
+    copy("v", v("li"), cols("yw", 0, 16))
+    ts(v("yc"), v("yw"), 600.0, A.add)
+    copy("v", cols("inv1", 0, 4), cols("yw", 0, 4))
+    copy("v", cols("w1", 16, 20), cols("yw", 0, 4))
+    copy("v", cols("w2", 16, 20), cols("yw", 44, 48))
+    copy("v", cols("inv2", 44, 48), cols("yw", 0, 4))
+    for x in range(3):
+        ts(PC["x"], PC["m0"], 256.0 * x, A.mult)
+        ts(cols("pay", 256 * x, 256 * x + 256), v("rr"), PC["m1"], A.mult, PC["x"], A.add)
+        if x == 2:
+            copy("v", v("pm2"), cols("pay", 512, NF))
+    ts(PC["x"], PC["m1"], 64.0, A.mult)
+    ts(v("pm1"), cols("pay", 256, 512), PC["x"], A.add)
+    for x, (t, sh) in enumerate(((1, 4), (2, 4), (0, 1), (1, 1), (2, 1))):
+        ts(cols("qi", x, x + 1), pint, sh, A.arith_shift_right, 7, A.bitwise_and)
+        ts(cols("qi", x, x + 1), cols("qi", x, x + 1), float(t), A.add)
+    ts(cols("q2", 0, 5), cols("qi", 0, 5), float(N - 1), A.is_ge, -float(N - 1), A.mult)
+    tt(cols("qi", 0, 5), cols("qi", 0, 5), cols("q2", 0, 5), A.add)
+    ts(cols("qi", 0, 2), cols("qi", 0, 2), -1.0, A.mult, float(rank + N - 1), A.add)
+    ts(cols("qi", 2, 5), cols("qi", 2, 5), float(rank + 1), A.add)
+    ts(cols("qi", 0, 5), cols("qi", 0, 5), N - 1, A.bitwise_and)
+    ts(cols("tmp", 0, 2), cols("qi", 0, 2), 24.0, A.mult)
+    bitcol(PC["x"], 1, 7)
+    ts(cols("tmp", 2, 5), cols("qi", 2, 5), 16.0, A.mult, PC["x"], A.add)
+    for t in (1, 2):
+        ts(cols("lst", 2 * t - 2, 2 * t - 1), cols("tmp", t - 1, t), PC["a"], A.add)
+        ts(cols("lrep", 16 * t - 16, 16 * t - 4), cols("rr", 12, 24), cols("tmp", t - 1, t), A.add)
+    for t in range(3):
+        ts(cols("lst", 4 + 2 * t, 6 + 2 * t), cols("rr", 0, 16, 8), cols("tmp", 2 + t, 3 + t), A.add)
+    for name, w in (("la1", 24), ("la2", 24), ("lr0", 16), ("lr1", 16), ("lr2", 16)):
+        fill(cols(name, w * rank, w * rank + w), 0.0)
+    for name in ("r1", "r2", "r3"):
+        fill(cols(name, NL, ZC), 0.0)
+
+    dma("y", v("rda"), v("ef"), 4000, [table])
+    dma("y", v("zda"), v("zf"), 4000, [table])
+    dma("y", cols("z_s", 320, NF), v("zf", ALL, slice(NL, 704)), after=asks)
+    dma("y", cols("z_s", 0, 64), v("zf", ALL, slice(704, NF)), after=asks)
+    dma("y", cols("eh_s", 320, NF), v("eh", ALL, slice(NL, 704)), after=asks)
+    dma("y", cols("eh_s", 0, 64), v("eh", ALL, slice(704, NF)), after=asks)
+
+    def bulk(t, after):
+        by_group((("zda", "zl%d" % t), ("rda", "rl%d" % t)), [T.cores[asked(rank, k, t)] for k in range(NG)], "a_b%d" % t, 12000, after)
+
+    for a in range(0, NT, NT // 8):
+        iota(cols("occ", a, a + NT // 8), [[0, NT // 8]], -1, 0)
+    bulk(1, ())
+
+    s0 = look("v", "h", 0, 128, NS)
+    s1 = look("s", "h", 192, 256, NS, cols("z_s", 256, 320))
+    s0()
+    s0 = look("v", "h", 128, 160, NS)
+    s1()
+    s1 = look("s", "h", 160, 192, NS, cols("z_s", 224, 256))
+    copy("v", v("offf"), v("efq0"))
+    s0()
+    zrep("v", "f", 0, 128)
+    s1()
+    s1 = look("s", "f", 192, 256, NS)
+    s0 = look("v", "f", 0, 64, NS)
+    s1()
+    s0()
+    choose(0)
+    s1 = look("s", "f", 128, 192, NS)
+    s0 = look("v", "f", 64, 128, NS)
+    s0()
+    s1()
+    bulk(2, [answer(0)])
+    for a, b, c in ((0, 64, 704.0), (64, 320, 0.0), (320, 576, 256.0), (576, NF, 512.0)):
+        act(cols("idf", a, b), cols("rr", 0, b - a), AF.Identity, bias=c)
+    alike(range(NG))
+    decide(0, "w0")
+
+    def fetch(t):
+        for name, src in (("efq%d" % t, "rl%d" % t), ("zq%d" % t, "zl%d" % t)):
+            dma("y", cols(name, 64, NF + 64), v(src))
+
+    fetch(1)
+
+    def lanes(t, m0, m1, placed):
         n = m1 - m0
+        L, pay, inv = "w%d" % t, "pay" if t == 1 else "pay2", "inv%d" % t
+        if t == 1:
+            ts(cols("uu", 0, n), placed, -0.5, A.is_ge)
+            ts(cols("dst", 0, n), placed, -0.5, A.is_lt)
+            tt(cols("vb", 0, n), cols("dst", 0, n), cols("yc", m0, m1), A.mult)
+        else:
+            ts(cols("uu", 0, n), placed, 0.5, A.is_lt)
+            tt(cols("vb", 0, n), placed, cols("yc", m0, m1), A.mult)
         C("v", "scan", out=cols("scn", 0, n), data0=cols("ob", 0, n), data1=cols("uu", 0, n), initial=0.0, op0=A.mult, op1=A.add)
-        mm(ps(0, n), v("ntr"), cols("uu", 0, n), True, False)
-        mm(ps(0, n), v("onb"), cols("scn", 0, n), False, True)
-        first = 0 if t == 1 else 704
-        copy("v", cols("nrow", 0, 64), cols("ihl", first, first + 64))
-        tt(cols("dst", 0, n), ps(0, n), cols("vb", 0, n), A.max)
+        mm(ps(KH, KH + n), v("ntr"), cols("uu", 0, n), True, False)
+        mm(ps(KH, KH + n), v("onb"), cols("scn", 0, n), False, True)
+        mm(ps(KH + 64, KH + 65), v("onb1"), cols("scn", n - 1, n))
+        if t == 1:
+            tt(cols("pay", 64, 320), row, cols("pay", 64, 320), A.add)
+        tt(cols("dst", 0, n), ps(KH, KH + n), cols("vb", 0, n), A.max)
         ts(cols("dsu", 0, n), cols("dst", 0, n), 63.0, A.add)
-        copy("v", ind(cols("nrow", 0, 2048), cols("dsu", 0, n)), cols("ihl", 16 * m0, 16 * m1))
-
-    def lanes_end(lists):
-        for i in range(16):
-            mm(ps(512, 528), cols("el", 15 - i, 143 - i), cols("nrow", i, NL, 16), i == 0, i == 15)
-        copy("v", cols(lists, 16, 32), ps(512, 528))
+        ts(cols("nrow", FIX, NL), cols("pm%d" % t, 0, DYN), ps(KH + 64, KH + 65), A.add)
+        copy("v", ind(v("nrow"), cols("dsu", 0, n)), cols(pay, 16 * m0, 16 * m1))
+        wrapped(P6 + 32, 12, "el", "nrow", FIX)
+        wrapped(P6 + 44, 12, "el2", "nrow", FIX)
+        mm(ps(KH + 65, KH + 66), v("onb"), cols("scn", n - 1, n))
+        mm(ps(KH + 128, KH + 128 + DYN), v("ex2"), cols("nrow", FIX, NL))
+        prev = "w%d" % (t - 1)
+        scatter("tb", prev, cols("z_s", 64, 320) if t == 1 else v("zlh"))
+        wrap()
+        copy("v", v("msg%d" % t), ps(P6 + 32, P6 + 56))
+        tell("msg%d" % t, 24, "la%d" % t, "a_q%d" % t)
+        copy("v", cols(L, 20, 32), ps(P6 + 32, P6 + 44))
+        act(cols("dc", FIX, NL), ps(KH + 128, KH + 128 + DYN), AF.Identity, bias=PC["ck"])
+        ts(cols(inv, m0, m1), cols("dst", 0, n), 63.0, A.add, float(NL), A.min)
+        ts(PC["y"], ps(KH + 65, KH + 66), float(FIX - 16 * m1), A.add)
+        ts(cols(inv, m1, m1 + 12), cols("yw", m1, m1 + 12), PC["y"], A.add, float(NL), A.min)
 
     def step(t):
-        L, tabf, lnf = "w%d" % t, "f%d" % t, "lnf%d" % t
-        ln = cols(L, 16, 32)
-        copy("v", v("zl"), ind(v("z_s"), ln))
-        C("s", "activation", out=v("dc"), in_=ind(v("st"), ln), func=AF.Identity, bias=ckc)
-        tt(v("xp"), ind(v("eh_s"), ln), v("dc"), A.add)
-        ts(v("offh"), v("xp"), ckc, A.subtract)
-        zrep("zrep", v("zl"), "rep")
-        copy("s", v("dl"), ind(v("st"), ln))
-        copy("s", v(lnf), ind(v("idf"), ln))
-        if t == 2:
-            for a, b in ((P6, 0), (P7, 384)):
-                mm(ps(a, a + 384), v("idb"), cols("st", b, b + 384), True, False)
-                mm(ps(a, a + 384), v("idb"), cols("ydm", b, b + 384), False, True)
-                copy("s", cols("stc", b, b + 384), ps(a, a + 384))
-            copy("s", v("st1c"), ind(v("stc"), cols("w1", 16, 32)))
-        masks((2, 3, 4, 5))
-        for j in range(4):
-            look(j, "cmph", "tb", DUMP, "offh", "zrep")
-            if j == 1:
-                key_mm(0)
-                tt(v("xf"), ind(v("ef_s"), ln), v("dc"), A.add)
-            if j == 2:
-                ts(v("offf"), v("xf"), ckc, A.subtract)
-        key_mm(1)
-        if t == 1:
-            scatter("f1", "u10", cols("zf1", 64, 320))
-        else:
-            scatter("f2", "u21", v("zu"))
-        wrap(tabf)
-        home_tree(t)
-        gram_rows()
-        masks((0, 1))
-        for j in range(4):
-            look(j, "cmpf", tabf, DUMP, "offf", "zrep")
-            if j == 1:
-                far_mm(0)
-                gram()
-        far_mm(1)
-        far_tree()
-        tt(v("m4"), *halves("m3", 8), A.max)
-        tt(v("wm"), v("whi"), v("m4"), A.max)
-        decide(t, L)
+        L, efq, zq, la = "w%d" % t, "efq%d" % t, "zq%d" % t, "la%d" % t
+        y0 = 0 if t == 1 else 704
+        f0 = y0
+        for name in (efq, zq):
+            copy("v", cols(name, 0, 64), cols(name, NF, NF + 64))
+        dyn = cols(L, 20, 32)
+        ts(cols("xp", 0, FIX), cols("eh_s", y0, y0 + FIX), PC["ck"], A.add)
+        copy("v", cols("offh", 0, FIX), cols("eh_s", y0, y0 + FIX))
+        copy("v", cols("offf", 0, FIX), cols(efq, f0, f0 + FIX))
+        sa = look("s", "f", 0, FIX, src=cols(zq, f0, f0 + FIX))
+        copy("v", v("zlh"), ind(v("z_s"), cols(L, 16, 32)))
+        tt(cols("xp", FIX, NL), ind(v("eh_s"), dyn), cols("dc", FIX, NL), A.add)
+        ts(cols("offh", FIX, NL), cols("xp", FIX, NL), PC["ck"], A.subtract)
+        zrep("v", "h", 128, 256)
+        sa()
+        sa = look("s", "h", 0, FIX)
+        sb = look("v", "h", 128, 256)
+        sa()
+        sa = look("s", "h", 64, 128)
+        sb()
+        copy("v", v("lq"), ind(v(la), cols("lst", 2 * t - 2, 2 * t - 1)))
+        tt(cols("dm", 0, DYN), ind(v(la), cols("lrep", 16 * t - 16, 16 * t - 4)), cols("m16", 0, DYN), A.mult)
+        sa()
+        mm(ps(P6 + 64, P6 + 64 + DYN), v("onb"), cols("dm", 0, DYN))
+        copy("v", cols("zlf", FIX, NL), ind(v(zq), cols("lq", 0, 12)))
+        copy("s", cols("dq", 0, DYN), ps(P6 + 64, P6 + 64 + DYN))
+        tt(cols("xq", 0, DYN), ind(v(efq), cols("lq", 0, 12)), cols("dq", 0, DYN), A.add)
+        copy("v", cols("offf", FIX, NL), cols("xq", 0, DYN))
+        sa = look("s", "f", 64, 128)
+        zrep("v", "f", 160, 256)
+        choose(t)
+        sa()
+        sa = look("s", "f", 128, 160)
+        sb = look("v", "f", 160, 192)
+        sc = look("v", "f", 192, 256)
+        sb()
+        sa()
+        sc()
+        answer(t)
+        copy("s", v("lnf%d" % t), ind(v("idf"), cols(L, 16, 32)))
+        alike(range(NG))
 
-    ts(cols("uu", 0, 16), ps(P6, P6 + 16), -0.5, A.is_ge)
-    ts(cols("dst", 0, 16), ps(P6, P6 + 16), -0.5, A.is_lt)
-    tt(cols("vb", 0, 16), cols("dst", 0, 16), cols("yc", 4, 20), A.mult)
-    dma("y", "d13", cols("f1", 0, NS), v("fd1"))
-    dma("y", "d14", v("zf1"), v("zd1"))
-    gathered("u10", "la0", 16, 1, "d15")
-    gathered("u20", "la0", 16, 2, "d16")
-    dma("y", "d17", cols("f2", 0, NS), v("fd2"))
-    dma("y", "d18", v("zf2"), v("zd2"))
-    lanes(1, 4, 32)
-    copy("v", cols("st", 64, 320), row)
-    scatter("tb", "w0", cols("z_s", 64, 320))
-    wrap("tb")
-    lanes_end("w1")
-    scatter("occ", "w0", cols("idf", 64, 320))
+    lanes(1, 4, 20, ps(P6, P6 + 16))
     step(1)
-    tell("w1", 32, "la1", "a_l1")
-    arrive(v("la1"), "a_l1", told)
-    gathered("u21", "la1", 32, 2, "d19")
+    scatter("occ", "w0", cols("idf", 64, 320))
+    fetch(2)
+    wrapped(KH, 32, "el3", "pay", 0, True, False)
+    decide(1, "w1")
+    copy("s", cols("r1", 0, NL), row)
     scatter("occ", "w1", v("lnf1"))
-    tt(v("st1"), v("dl"), row, A.add)
-    copy("v", ind(v("st"), cols("w1", 16, 32)), v("st1"))
+    copy("s", cols("g1", 0, 512), ind(v("r1"), v("inv1")))
     tt(v("b1"), ind(v("occ"), v("w0")), cols("idf", 64, 320), A.not_equal)
-    ts(v("zu"), v("b1"), -127.0, A.mult)
-    tt(cols("st", 64, 320), cols("st", 64, 320), v("zu"), A.add)
-    for i in range(16):
-        mm(ps(640, 672), cols("el", 15 - i, 143 - i), cols("st", i, 512, 16), i == 0, i == 15)
-    scatter("tb", "w1", v("zl"))
-    wrap("tb")
-    ts(cols("uu", 0, 32), ps(640, 672), 255.0, A.is_lt)
-    ts(cols("dst", 0, 32), ps(640, 672), 255.0, A.is_ge)
-    fill(cols("vb", 32, 48), 0.0)
-    fill(cols("uu", 32, 48), 1.0)
-    tt(cols("vb", 0, 32), cols("dst", 0, 32), cols("yc", 0, 32), A.mult)
-    lanes(2, 0, 44)
-    ts(v("ydm"), v("st"), 128.0, A.is_ge, -128.0, A.mult)
-    lanes_end("w2")
-    scatter("f2", "u20", cols("zf2", 64, 320))
-    copy("s", v("zu"), ind(v("zf2"), cols("u21", 16, 32)))
+    wrapped(KH, 32, "el3", "g1", 0, False, False)
+    wrapped(KH + 4, 16, "eln", "b1", 0, False, True)
+    mm(ps(0, 512), v("idb"), cols("pay", 0, 512), True, False)
+    mm(ps(0, 512), v("idb"), cols("g1", 0, 512), False, False)
+    mm(ps(64, 320), v("mk2"), v("b1"), False, True)
+    copy("s", cols("pay2", 0, 512), ps(0, 512))
+    copy("s", cols("pay2", 512, NF), cols("pay", 512, NF))
+    lanes(2, 0, 32, ps(KH, KH + 32))
     step(2)
-    scatter("tb", "w2", v("zl"))
-    dma("y", "d20", v("yt"), cols("tb", 0, NS))
+    decide(2, "w2")
+    scatter("tb", "w2", v("zlh"))
+    dma("y", v("yt"), cols("tb", 0, NS))
+    copy("s", cols("r2", 0, NL), row)
+    copy("s", v("g2"), ind(v("r2"), v("inv2")))
     scatter("occ", "w2", v("lnf2"))
-    dma("s", "d21", v("yo"), v("occ", slice(0, 128, 16), slice(0, NS)))
-    tt(v("st2"), v("dl"), row, A.add)
-    tt(v("zu"), ind(v("occ"), cols("w1", 0, 16)), v("lnf1"), A.not_equal)
-    tt(v("st1c"), v("st1c"), v("zu"), A.add)
-    copy("v", ind(v("stc"), cols("w1", 16, 32)), v("st1c"))
+    dma("s", v("yo"), v("occ", slice(0, 128, 16), slice(0, NS)))
+    tt(cols("r3", 0, NL), ind(v("occ"), cols("w1", 0, 16)), v("lnf1"), A.not_equal)
+    copy("s", cols("g3", 0, 512), ind(v("r3"), v("inv1")))
     tt(v("b3"), ind(v("occ"), v("w0")), cols("idf", 64, 320), A.not_equal)
     tt(v("b3"), v("b3"), v("b1"), A.is_gt)
-    copy("v", ind(v("stc"), cols("w2", 16, 32)), v("st2"))
-    tt(cols("stc", 64, 320), cols("stc", 64, 320), v("b3"), A.add)
-    dma("y", "d22", v("yd", ALL, slice(0, 704)), v("stc", slice(0, 128, 16), slice(64, NF)))
-    dma("s", "d23", v("yd", ALL, slice(704, NF)), v("stc", slice(0, 128, 16), slice(0, 64)))
+    for a, b in ((0, 512), (512, NF)):
+        mm(ps(a, b), v("idb"), cols("pay2", a, b), True, False)
+        mm(ps(a, b), v("idb"), cols("g2", a, b), False, a > 0)
+    mm(ps(64, 320), v("idb"), v("b3"), False, False)
+    mm(ps(0, 512), v("idb"), cols("g3", 0, 512), False, True)
+    copy("s", cols("ydf", 512, NF), ps(512, NF))
+    copy("v", cols("ydf", 0, 512), ps(0, 512))
+    dma("y", v("yd", ALL, slice(0, 704)), v("ydf", slice(2, 128, 16), slice(64, NF)))
+    dma("s", v("yd", ALL, slice(704, NF)), v("ydf", slice(2, 128, 16), slice(0, 64)))
     F["finish"]()
 
 
@@ -688,8 +738,3 @@ def rank_program(g, core, T, topo):
     rank = T.rank_of(core)
     if rank is not None:
         rank_main(g, core, rank, T, topo)
-        return
-    for c in topo.cores_of(core):
-        if T.rank_of(c) is not None and helper_of(c, T, topo) == core:
-            helper_main(g, core, T.rank_of(c), T, topo)
-            return

@@ -1,6 +1,6 @@
 import numpy as np
 from concourse.bass import DstId, RemoteDMATransfer
-from concourse.mybir import AluOpType as A, ActivationFunctionType as AF
+from concourse.mybir import AluOpType as A, AxisListType, ActivationFunctionType as AF
 
 N, NG, NS, NF, NL = 8, 8, 4096, 768, 256
 WR = 32
@@ -14,26 +14,53 @@ SCRATCH = {"psb": ("psum", [128, 4096], "float32")}
 for _where, _shape, _names in (
         ("sbuf", [128, NT], "b:tb f:occ"),
         ("sbuf", [128, NF], "i:eh_s b:z_s b:pay b:pay2 f:idf b:g1 b:g2 b:g3 f:ydf"),
-        ("sbuf", [128, NF + 64], "i:efq1 i:efq2 b:zq1 b:zq2"),
+        ("sbuf", [128, NF + 64], "i:eu1 i:eu2 b:zq1 b:zq2"),
         ("sbuf", [128, 4096], "b:zrh b:zrf b:cmh b:cmf b:gth b:gtf"), ("sbuf", [128, 1280], "b:nrow"),
-        ("sbuf", [128, NL], "i:efq0 f:xp f:xq f:dc f:dq u:offh u:offf b:zlh b:zlf f:lnf1 f:lnf2 b:b1 b:b3 b:t1 b:st b:nst "
-                            "f:kh b:kf b:rst b:dm b:m16 b:rr b:pm1 b:pm2 b:mid"),
-        ("sbuf", [128, ZC], "b:r1 b:r2 b:r3"), ("sbuf", [128, 8, 384], "b:eq"), ("sbuf", [128, 384], "b:tri"),
-        ("sbuf", [128, 16], "u:w0 u:lq b:li i:hki b:wq0 b:wq1 b:wq2 u:lst f:tmp"), ("sbuf", [128, 32], "u:w1 u:w2 u:inv1 u:dsu u:lrep i:whi b:wm"),
-        ("sbuf", [128, 24], "f:msg1 f:msg2"), ("sbuf", [128, N * 24], "f:la1 f:la2"), ("sbuf", [128, N * 16], "b:lr0 b:lr1 b:lr2"),
-        ("sbuf", [128, 16, 2], "i:di b:go_ b:ng b:win b:dd0 b:dd1 b:dd2 b:sd b:cd"), ("sbuf", [128, 2, 32], "b:ttl"),
+        ("sbuf", [128, NL], "i:efq0 f:xp f:xq f:dc f:dq u:offh u:offf b:zlh b:zlf f:lnf1 f:lnf2 b:b1 b:b3 b:t1 b:dm b:st "
+                            "f:kh b:kf b:rst b:m16 b:rr b:pm1 b:pm2 b:mid"),
+        ("sbuf", [128, ZC], "b:r1 b:r2 b:r3"), ("sbuf", [128, 8, 384], "b:eq"),
+        ("sbuf", [128, 16], "u:w0 u:lq b:li i:hki i:sli f:nsl i:whi b:wm b:gw b:gb f:thr b:ng f:tmp"),
+        ("sbuf", [128, 32], "u:w1 u:w2 u:inv1 u:dsu"), ("sbuf", [128, 48], "f:msg b:wq u:lst"),
+        ("sbuf", [128, N * 16], "b:lr0 b:lr1 b:lr2"), ("sbuf", [128, N * 24], "f:la1 f:la2"),
+        ("sbuf", [128, 16, 2], "i:di b:sd b:cd"), ("sbuf", [128, 48, 2], "b:dd"), ("sbuf", [128, 2, 32], "b:ttl"),
         ("sbuf", [128, 48], "b:uu f:vb b:scn f:dst f:yc f:yw u:inv2"),
-        ("sbuf", [128, 8], "i:pi i:qi i:q2 b:blkf b:blkh b:blkk b:blkj"), ("sbuf", [128, 32], "f:pc"),
+        ("sbuf", [128, 8], "i:pi i:qi"), ("sbuf", [128, 32], "f:pc b:blk"),
         ("sbuf", [128, 144], "b:ew b:el b:el2 b:el3 b:eln"),
         ("sbuf", [128, 128], "f:id32 b:idb b:idn b:er b:onb b:onb1 b:ntr b:ex2 b:mk2 b:ob b:r16"), ("sbuf", [128, 1024], "b:sg"),
-        ("dram", [1024, 32], "i:rd b:zd i:rl b:zl"), ("dram", [1024, 96], "i:rda b:zda i:rl1 i:rl2 b:zl1 b:zl2")):
+        ("dram", [1024, 32], "i:ed0 b:zd0 i:rl0 b:zl0"),
+        ("dram", [1024, 96], "i:eda b:zda i:rl1 i:rl2 b:zl1 b:zl2")):
     for _n in _names.split():
         SCRATCH[_n[2:]] = (_where, _shape, TYPES[_n[0]])
 ENG = {"v": "ev", "s": "es", "p": "ep", "g": "eg"}
-SEMAPHORES = (["ev", "es", "ep", "eg", "lsem", "a_q0", "a_q1", "a_q2", "a_b1", "a_b2", "a_r0", "a_r1", "a_r2"]
+SEMAPHORES = (["ev", "es", "ep", "eg", "lsem", "a_z0", "a_q0", "a_q1", "a_q2", "a_r0", "a_r1", "a_r2", "a_b1", "a_b2", "a_b3"]
               + ["d%d" % k for k in range(28)])
 WRITES = ("out", "accum_out", "ap")
-CYCLE, WAKE = 0.83, 60.0
+CYCLE, WAKE, LONG = 0.83, 60.0, 250.0
+SWEEPS = 4
+LAST = [0]
+GREEDY = True
+BULK = 11000
+TELL, ASK0 = 3000, 5300
+PIECE = 128
+ZLH = "s"
+ASKS_FIRST = False
+BY_PROGRAM = True
+ZLF = "s"
+DQ = "s"
+EARLY = 6
+FUSED = 1.56
+CALL = 28.0
+TB_EARLY = True
+BACK = "g%d"
+STRICT = False
+DC, OCC = "s", "c1"
+ASKZ = 4300
+ON_SCALAR = (0, 1, 2)
+TOP = 9.0e29
+PLAN = {t: "sh1:0:64 zhv:128:256 vh:128:256 sf1:0:64 sh2:0:64 asks sh1:64:128 sf2:0:64 sh2:64:128 sf:64:128 zfv:128:256 vf:128:256 "
+           "answer choose alike" for t in (1, 2)}
+PLAN[0] = ("zhs:0:128 sh:192:256 vh:0:128 sh:128:192 "
+           "zfv:0:160 sf1:192:256 sf1:160:192 sf2:192:256 vf:0:128 sf2:160:192 vf:128:160 answer")
 MASKS = {}
 ALL = slice(None)
 
@@ -120,7 +147,8 @@ def region(view):
 def flow(g, T):
     queues = {"v": g.vector, "s": g.scalar, "p": g.tensor, "g": g, "y": g.sync}
     known = {q: {} for q in queues}
-    total, acc, ops, banks = {}, {}, [], [{} for _ in range(8)]
+    total, acc, ops, banks, lazy = {}, {}, [], [{} for _ in range(8)], [False]
+    gate = []
 
     def ap(x):
         if x[0] == "i":
@@ -155,46 +183,85 @@ def flow(g, T):
             if kind == "w":
                 old = [e for e in old if not (p0 <= e["p0"] and e["p1"] <= p1 and (e["m"] & ~m) == 0)]
             acc[name] = old + [{"kind": kind, "p0": p0, "p1": p1, "m": m, "op": me}]
-        ops.append({"q": q, "go": go, "sem": sem, "n": n, "busy": busy, "late": late, "dep": dep})
+        for k in gate:
+            dep.setdefault(k, ops[k]["q"] != q)
+        ops.append({"lazy": lazy[0], "name": str([parts(x)[0][1:] for x in writes][:1]), "q": q, "go": go, "sem": sem, "n": n, "busy": busy, "late": late, "dep": dep})
         return me
 
     def order():
-        way = [0.0] * len(ops)
-        users = [[] for _ in ops]
-        for k in range(len(ops) - 1, -1, -1):
-            way[k] += ops[k]["busy"] + ops[k]["late"]
-            for d, hard in ops[k]["dep"].items():
-                users[d].append(k)
-                way[d] = max(way[d], way[k] + WAKE if hard else way[k] - ops[d]["late"])
-        left = [len(o["dep"]) for o in ops]
-        ready = [0.0] * len(ops)
-        free = {q: 0.0 for q in list(queues) + [None]}
-        pool = {q: [k for k in range(len(ops)) if ops[k]["q"] == q and not left[k]] for q in free}
-        out = []
-        while len(out) < len(ops):
-            best = None
-            for q in pool:
-                if pool[q]:
-                    now = max(free[q], min(ready[k] for k in pool[q]))
-                    k = max((k for k in pool[q] if ready[k] <= now), key=lambda k: (way[k], -k))
-                    soon = [j for j in pool[q] if now < ready[j] < now + 0.5 * ops[k]["busy"] and way[j] > way[k] + ops[k]["busy"]]
-                    if soon:
-                        k = min(soon, key=lambda j: ready[j])
-                        now = ready[k]
-                    if best is None or now < best[0]:
-                        best = (now, k, q)
-            now, k, q = best
-            pool[q].remove(k)
-            out.append(k)
-            if q is not None:
-                free[q] = now + ops[k]["busy"]
-            for u in users[k]:
-                end = now + ops[k]["busy"]
-                ready[u] = max(ready[u], end + ops[k]["late"] + WAKE if ops[u]["dep"][k] else end)
-                left[u] -= 1
-                if not left[u]:
-                    pool[ops[u]["q"]].append(u)
-        return out
+        n = len(ops)
+        before = [[(d, ops[d]["late"] + WAKE if hard else 0.0) for d, hard in o["dep"].items()] for o in ops]
+        behind = [[] for _ in ops]
+        way = [o["late"] for o in ops]
+        for k in range(n - 1, -1, -1):
+            way[k] += ops[k]["busy"]
+            for d, lag in before[k]:
+                behind[d].append((k, lag))
+                way[d] = max(way[d], way[k] + lag)
+
+        def place(rank_, needs, floor):
+            taken, end = {q: [] for q in queues}, [0.0] * n
+            for k in sorted(range(n), key=rank_):
+                t, busy = max([floor[k]] + [end[d] + lag for d, lag in needs[k]]), ops[k]["busy"]
+                if ops[k]["q"] is not None:
+                    iv = taken[ops[k]["q"]]
+                    j = len(iv)
+                    while j and iv[j - 1][1] > t:
+                        j -= 1
+                    while j < len(iv) and iv[j][0] < t + busy - 1e-6:
+                        t = max(t, iv[j][1])
+                        j += 1
+                    lo, hi, a, b = j, j, t, t + busy
+                    if j and iv[j - 1][1] > t - 1e-6:
+                        lo, a = j - 1, iv[j - 1][0]
+                    if j < len(iv) and iv[j][0] < b + 1e-6:
+                        hi, b = j + 1, iv[j][1]
+                    iv[lo:hi] = [(a, b)]
+                end[k] = t + busy
+            return end
+
+        if GREEDY:
+            left = [len(o["dep"]) for o in ops]
+            ready = [0.0] * n
+            free = {q: 0.0 for q in list(queues) + [None]}
+            pool = {q: [k for k in range(n) if ops[k]["q"] == q and not left[k]] for q in free}
+            out = []
+            while len(out) < n:
+                best = None
+                for q in pool:
+                    if pool[q]:
+                        now = max(free[q], min(ready[k] for k in pool[q]))
+                        k = max((k for k in pool[q] if ready[k] <= now), key=lambda k: (way[k], -k))
+                        soon = [j for j in pool[q] if now < ready[j] < now + 0.5 * ops[k]["busy"] and way[j] > way[k] + ops[k]["busy"]]
+                        if soon:
+                            k = min(soon, key=lambda j: ready[j])
+                            now = ready[k]
+                        if best is None or now < best[0]:
+                            best = (now, k, q)
+                now, k, q = best
+                pool[q].remove(k)
+                out.append(k)
+                if q is not None:
+                    free[q] = now + ops[k]["busy"]
+                for u, lag in behind[k]:
+                    ready[u] = max(ready[u], now + ops[k]["busy"] + lag)
+                    left[u] -= 1
+                    if not left[u]:
+                        pool[ops[u]["q"]].append(u)
+            return out
+        results = []
+        if BY_PROGRAM:
+            way = [-n if ops[k]["lazy"] else -k for k in range(n)]
+            for k in range(n - 1, -1, -1):
+                for d, lag in before[k]:
+                    way[d] = max(way[d], way[k])
+        for sweep in range(SWEEPS):
+            end = place(lambda k: (-way[k], k), before, [0.0] * n)
+            results.append((max(end[k] + ops[k]["late"] for k in range(n)), sorted(range(n), key=lambda k: (end[k] - ops[k]["busy"], k))))
+            way = place(lambda k: (-end[k], -k), behind, [o["late"] for o in ops])
+        LAST[0] = [r[0] for r in results]
+        LAST[1:] = [ops, before, end]
+        return min(results)[1]
 
     def settle(q, ev):
         need = {}
@@ -220,16 +287,16 @@ def flow(g, T):
         n, views = size(out)[0], [kw[k] for k in kw if is_view(kw[k])]
         if meth == "matmul":
             return max(min(64, size(kw["lhsT"])[0]), n) * 0.42 * (1 if size(kw["rhs"])[1] else 4)
-        if meth == "iota":
-            return 130 + 2 * n * CYCLE
+        if q == "g":
+            return 150 + 2 * n * CYCLE
         if out[0] == "i":
             return 50 + 3.8 * n * CYCLE
         if any(x[0] == "i" for x in views):
-            return 60 + 1.56 * n * CYCLE
+            return 60 + (FUSED if meth == "tensor_tensor" else 1.56) * n * CYCLE
         if meth == "tensor_tensor":
-            return max(64, n * (1 if any(x[1] == "psb" for x in views) else 2)) * CYCLE
+            return CALL + max(64, n * (1 if any(x[1] == "psb" for x in views) else 2)) * CYCLE
         narrow = q == "v" and all(size(x)[1] or size(x)[0] == 1 for x in views)
-        return max(64, n / 2 if narrow else n) * CYCLE
+        return CALL + max(64, n / 2 if narrow else n) * CYCLE
 
     def call(q, meth, **kw):
         reads, writes = [], []
@@ -244,26 +311,26 @@ def flow(g, T):
         args = {k: (ap(kw[k]) if is_view(kw[k]) else kw[k]) for k in kw}
         eng = queues[q]
         f = {"tensor_copy": lambda: eng.tensor_copy(**args), "tensor_tensor": lambda: eng.tensor_tensor(**args),
-             "tensor_scalar": lambda: eng.tensor_scalar(**args),
+             "tensor_scalar": lambda: eng.tensor_scalar(**args), "tensor_reduce": lambda: eng.tensor_reduce(**args),
              "scan": lambda: eng.tensor_tensor_scan(**args), "memset": lambda: eng.memset(args["ap"], args["constant"]),
              "activation": lambda: eng.activation(**args), "matmul": lambda: eng.matmul(**args),
-             "iota": lambda: eng.iota(**args)}[meth]
+             "iota": lambda: eng.iota(**args), "affine_select": lambda: eng.affine_select(**args)}[meth]
         return add(q, reads, writes, lambda: f().then_inc(T.sem[ENG[q]], 1), ENG[q], 1, cost(q, meth, kw))
 
     def dma(q, sem, out, in_, late, after, behind):
         k = add(q, [in_], [out], lambda: queues[q].dma_start(out=ap(out), in_=ap(in_)).then_inc(T.sem[sem], 16), sem, 16, 60, late, after)
         if behind is not None:
-            ops[k]["dep"][behind] = False
+            ops[k]["dep"].setdefault(behind, False)
         return k
 
-    def arrive(outs, sem, cnt, mine):
-        return add(None, [], outs, None, sem, cnt, 0, 0, mine)
+    def arrive(outs, sem, cnt, mine, late=0):
+        return add(None, [], outs, None, sem, cnt, 0, late, mine)
 
-    def fused(transfers, late, after=()):
+    def fused(transfers, late, after=(), local="lsem"):
         go = lambda: g.remote_dma_fused(
             [RemoteDMATransfer(dst_ids=[d[0] for d in t[1]], dma_engine_mask=bits(t[2]), remote_sem=T.sem[t[3]],
-                               srcs=[ap(t[0])], dsts=[ap(d[1]) for d in t[1]]) for t in transfers], local_sem=T.sem["lsem"])
-        return add("g", [t[0] for t in transfers], [], go, "lsem", sum(len(t[2]) for t in transfers), 300, late, after)
+                               srcs=[ap(t[0])], dsts=[ap(d[1]) for d in t[1]]) for t in transfers], local_sem=T.sem[local])
+        return add("g", [t[0] for t in transfers], [], go, local, sum(len(t[2]) for t in transfers), 300, late, after)
 
     def finish():
         event = {}
@@ -280,7 +347,7 @@ def flow(g, T):
             if known["g"].get(sem, 0) < total[sem]:
                 g.wait_ge(T.sem[sem], total[sem])
 
-    return {"call": call, "dma": dma, "arrive": arrive, "fused": fused, "finish": finish}
+    return {"call": call, "dma": dma, "arrive": arrive, "fused": fused, "finish": finish, "lazy": lazy, "gate": gate, "last": lambda: len(ops) - 1}
 
 
 def blk(name, k):
@@ -295,32 +362,62 @@ def rows(name, n, a, b, step=None):
     return v(name, slice(0, n), slice(a, b, step))
 
 
+def helper_of(core, T, topo):
+    for c in topo.cores_of(core):
+        if T.rank_of(c) is None and topo.die(c) == topo.die(core) and all(topo.may_write(c, d) for d in T.cores):
+            return c
+
+
+def helper_main(g, core, rank, T, topo):
+    F = flow(g, T)
+    dst = [T.cores[asker(rank, k, 2)] for k in range(NG)]
+    eng = singles(core, dst, T, topo)
+    for q, src, piece, land in (("y", "hb", "td", "fd2"), ("s", "hz", "zd2", "zl2")):
+        F["arrive"]([v(src)], "a_" + src, len(near_engines(T.cores[rank], core, T, topo)), ())
+        F["dma"](q, "d1" if q == "y" else "d2", v(piece), v(src), 3000, (), None)
+        F["fused"]([(blk(piece, k), [(dst_id(topo, dst[k]), blk(land, k))], [eng[k]], "a_f2") for k in range(NG)], 3000)
+    F["finish"]()
+
+
 def rank_main(g, core, rank, T, topo):
     F = flow(g, T)
     C, arrive, fused = F["call"], F["arrive"], F["fused"]
     ps = lambda a, b, n=128, step=None: v("psb", slice(0, n), slice(a, b, step))
     KH, KF, P6, P7 = 2048, 2560, 3072, 3584
     row = ps(P7 + 256, P7 + 512)
-    nd, turn = [0], [0]
+    nd, turn, last, sent, inline, gate = [0], [0], {}, {}, [], F["gate"]
+    setup = [False]
 
-    def dma(q, out, in_, late=3000, after=(), behind=None):
+    def dma(q, out, in_, late=3000, after=()):
         nd[0] += 1
-        return F["dma"](q, "d%d" % nd[0], out, in_, late, after, behind)
+        last[q] = F["dma"](q, "d%d" % nd[0], out, in_, late, after, last.get(q))
+        return last[q]
 
     def act(out, in_, func=AF.Copy, **kw):
-        C("s", "activation", out=out, in_=in_, func=func, **kw)
+        if inline:
+            gate.append(inline[0])
+        k = C("s", "activation", out=out, in_=in_, func=func, **kw)
+        if inline:
+            gate.pop()
+            inline[0] = k
 
     def copy(q, out, in_):
-        if q == "s":
+        if q == "s" or (setup[0] and real(out, in_)):
             act(out, in_)
+        elif q == "g":
+            C("g", "affine_select", out=out, in_=in_, pattern=[[0, FIX]], compare_op=A.is_ge, fill=0.0, base=0, channel_multiplier=0)
         else:
             C("v", "tensor_copy", out=out, in_=in_)
 
     def tt(out, a, b, op):
         C("v", "tensor_tensor", out=out, in0=a, in1=b, op=op)
 
+    real = lambda *xs: all(SCRATCH[x[1]][2] in ("float32", "bfloat16") for x in xs)
+
     def ts(out, a, s1, op, s2=None, op1=None):
-        if op1 is None:
+        if setup[0] and real(out, a) and (op, op1) in ((A.mult, A.add), (A.mult, None), (A.add, None)):
+            act(out, a, AF.Identity, scale=s1 if op == A.mult else 1.0, bias=s1 if op == A.add else s2 or 0.0)
+        elif op1 is None:
             C("v", "tensor_scalar", out=out, in0=a, scalar1=s1, scalar2=None, op0=op)
         else:
             C("v", "tensor_scalar", out=out, in0=a, scalar1=s1, scalar2=s2, op0=op, op1=op1)
@@ -329,7 +426,10 @@ def rank_main(g, core, rank, T, topo):
         C("p", "matmul", out=out, lhsT=lhsT, rhs=rhs, start=start, stop=stop)
 
     def fill(x, c):
-        C("v", "memset", ap=x, constant=c)
+        if setup[0]:
+            act(x, cols("rr", 0, x[2][1].stop - x[2][1].start), AF.Identity, scale=0.0, bias=c)
+        else:
+            C("v", "memset", ap=x, constant=c)
 
     def iota(out, pattern, base, ch):
         if SCRATCH[out[1]][2] == "int32":
@@ -337,39 +437,44 @@ def rank_main(g, core, rank, T, topo):
         else:
             C("g", "iota", out=out, pattern=pattern, base=base, channel_multiplier=ch, allow_small_or_imprecise_dtypes=True)
 
-    def by_group(pairs, dst, sem, late, after=()):
+    def by_group(pairs, dst, sem, late, after=(), local="lsem"):
         eng = singles(core, dst, T, topo)
-        mine = [fused([(blk(src, k), [(dst_id(topo, dst[k]), blk(land, k))], [eng[k]], sem) for k in range(NG)], late, after)
+        mine = [fused([(blk(src, k), [(dst_id(topo, dst[k]), blk(land, k))], [eng[k]], sem) for k in range(NG)], late, after, local)
                 for src, land in pairs]
         return arrive([v(land) for src, land in pairs], sem, len(pairs) * NG, mine)
 
     told = sum(len(far_engines(c, T, topo)) if off_chip(topo, c, core) else len(near_engines(c, core, T, topo)) for c in T.cores if c != core)
 
-    def tell(src, width, land, sem):
+    def tell(src, width, land, sem, after=(), more=0):
         far = [c for c in T.cores if off_chip(topo, core, c)]
         near = [c for c in T.cores if c != core and not off_chip(topo, core, c)]
         tr = []
         for ds, en in ((far, far_engines(core, T, topo)), (near, near_engines(core, near[0], T, topo) if near else [])):
             if ds:
-                tr.append((cols(src, 0, width), [(dst_id(topo, d), cols(land, width * rank, width * rank + width)) for d in ds], en, sem))
-        mine = fused(tr, 3000)
-        arrive([cols(land, width * r, width * r + width) for r in range(N) if r != rank], sem, told, [mine])
-        return mine
+                tr.append((src, [(dst_id(topo, d), cols(land, width * rank, width * rank + width)) for d in ds], en, sem))
+        mine = fused(tr, TELL + more, after)
+        return mine, arrive([cols(land, width * r, width * r + width) for r in range(N) if r != rank], sem, told, [mine])
 
-    first = [dma("y", v("rd"), v("ef", ALL, slice(0, NL))),
-             dma("s", v("zd"), v("zf", ALL, slice(0, NL))),
+    to_asked = lambda t: [T.cores[asked(rank, k, t)] for k in range(NG)]
+    to_asker = lambda t: [T.cores[asker(rank, k, t)] for k in range(NG)]
+
+    first = [dma("y", v("ed0"), v("ef", ALL, slice(0, NL)), 2400),
+             dma("s", v("zd0"), v("zf", ALL, slice(0, NL)), 2000),
              dma("s", cols("z_s", 64, 320), v("zf", ALL, slice(0, NL))),
              dma("y", cols("eh_s", 64, 320), v("eh", ALL, slice(0, NL)))]
-    table = dma("y", cols("tb", 0, NS), v("tab"), 6000, behind=first[3])
+    table = dma("y", cols("tb", 0, NS), v("tab"), 6000)
 
     iota(v("pi"), [[0, 8]], 0, 1)
     iota(v("rr"), [[1, NL]], 0, 0)
     iota(v("r16"), [[1, 8], [0, 16]], 0, 0)
     iota(v("m16"), [[0, 16], [1, 16]], 0, 0)
-    by_group((("zd", "zl"), ("rd", "rl")), [T.cores[asked(rank, k, 0)] for k in range(NG)], "a_q0", 5000)
+    by_group((("zd0", "zl0"),), to_asked(0), "a_z0", ASKZ)
+    sent["q0"] = by_group((("ed0", "rl0"),), to_asked(0), "a_q0", ASK0) - 1
 
+    lazy = F["lazy"]
+    lazy[0] = True
     PC = {n: cols("pc", k, k + 1) for k, n in enumerate(
-        "p a g ck m0 m1 m01 m2 m3 c15 half wq ewc erc h1 h2 x y".split())}
+        "p a g ck m0 m1 m2 m3 m01 c15 half wq ewc erc w3 w6 x y".split())}
     pint = cols("pi", 0, 1)
 
     def bitcol(out, sh, mask):
@@ -384,9 +489,10 @@ def rank_main(g, core, rank, T, topo):
     ts(v("id32"), r128, PC["p"], A.is_equal)
     ts(v("idb"), r128, PC["p"], A.is_equal)
     ts(v("idn"), r128, PC["p"], A.is_equal, -1.0, A.mult)
-    for name, w in (("blkf", 1.0), ("blkh", 0.5), ("blkk", 131072.0), ("blkj", 65536.0)):
-        ts(v(name), cols("rr", 0, 8), PC["g"], A.is_equal, w, A.mult)
+    for x, w in enumerate((1.0, 0.5, 131072.0, 65536.0)):
+        ts(cols("blk", 8 * x, 8 * x + 8), cols("rr", 0, 8), PC["g"], A.is_equal, w, A.mult)
     fill(v("ob"), 1.0)
+    setup[0] = True
     fill(cols("mid", 0, 128), 8.0)
     fill(cols("mid", 128, NL), 8.0 * 131072)
     ts(v("xp"), cols("eh_s", 64, 320), PC["ck"], A.add)
@@ -397,17 +503,32 @@ def rank_main(g, core, rank, T, topo):
         for k in range(16):
             copy(q, cols("zr" + tab, 16 * a + k, 16 * b, 16), src or cols("zl" + tab, a, b))
 
-    def look(q, tab, a, b, width=DUMP, src=None):
+    def look(q, tab, a, b, width=DUMP, src=None, part=0, table="tb", whose=None):
         n, h, p0 = b - a, a // 128, a % 128
-        z = src or cols("zl" + tab, a, b)
+        whose = whose or tab
+        z = src or cols("zl" + whose, a, b)
         base = (KH if tab == "h" else KF) + 128 * h
         out = lambda x, y, step=None: v("psb", slice(p0, p0 + n), slice(base + x, base + y, step))
-        got = ind(cols("tb", 0, width), cols("off" + tab, a, b))
+        got = ind(cols(table, 0, width), cols("off" + tab, a, b))
+        lhs = lambda k: cols("cm" + tab, 16 * a + k, 16 * b, 16)
+        if q == "b":
+            bank = 512 * (turn[0] % 4)
+            turn[0] += 1
+            mm(ps(bank, bank + n), v("idb"), z)
+            for k in range(16):
+                tt(lhs(k), cols("gt" + tab, 16 * a + k, 16 * b, 16), ps(bank, bank + n), A.is_le)
+            return
         if q == "v":
-            tt(cols("cm" + tab, 16 * a, 16 * b), got, cols("zr" + tab, 16 * a, 16 * b), A.is_le)
-            lhs = lambda k: cols("cm" + tab, 16 * a + k, 16 * b, 16)
+            for x in range(a, b, PIECE) if part != 2 else ():
+                y = min(b, x + PIECE)
+                tt(cols("cm" + tab, 16 * x, 16 * y), ind(cols(table, 0, width), cols("off" + tab, x, y)), cols("zr" + whose, 16 * x, 16 * y), A.is_le)
+            if part == 1:
+                return
         else:
-            act(cols("gt" + tab, 16 * a, 16 * b), got)
+            if part != 2:
+                act(cols("gt" + tab, 16 * a, 16 * b), got)
+            if part == 1:
+                return
             per = 512 // n
             for k0 in range(0, 16, per):
                 bank = 512 * (turn[0] % 4)
@@ -419,16 +540,14 @@ def rank_main(g, core, rank, T, topo):
                 act(cols("cm" + tab, 16 * a + n * k0, 16 * a + n * (k0 + per)), ps(bank, bank + 512), AF.Sign, scale=-1.0, bias=0.5)
             lhs = lambda k: cols("cm" + tab, 16 * a + n * k, 16 * a + n * (k + 1))
 
-        def sums():
-            first = tab == "f" and q == "v"
-            if tab == "h":
-                mm(out(0, 128), cols("xp", a, b), v("id32"), True, False)
-            if q == "s":
-                mm(out(0, 128), rows("ob", 1, 0, n), rows("mid", 1, 128, NL) if tab == "h" else rows("mid", 1, 0, 128), tab == "f", False)
-            w = {"hv": "blkk", "hs": "blkj", "fv": "blkf", "fs": "blkh"}[tab + q]
-            for k in range(16):
-                mm(out(k, 128, 16), lhs(k), v(w), first, first or k == 15)
-        return sums
+        first = tab == "f" and q == "v"
+        if tab == "h":
+            mm(out(0, 128), cols("xp", a, b), v("id32"), True, False)
+        if q == "s":
+            mm(out(0, 128), rows("ob", 1, 0, n), rows("mid", 1, 128, NL) if tab == "h" else rows("mid", 1, 0, 128), tab == "f", False)
+        w = 8 * ("fv", "fs", "hv", "hs").index(tab + q)
+        for k in range(16):
+            mm(out(k, 128, 16), lhs(k), cols("blk", w, w + 8), first, first or k == 15)
 
     lane = lambda name, h, x=ALL: v(name, ALL, slice(8 * h, 8 * h + 8), x)
 
@@ -441,47 +560,66 @@ def rank_main(g, core, rank, T, topo):
         for h in range(2):
             mm(ps(P7 + 128 * h, P7 + 128 * h + 128, 16), lane("cd", h), v("idb"))
         act(rows("st", 16, 0, NL), ps(P7, P7 + NL, 16))
-        act(rows("nst", 16, 0, NL), ps(P7, P7 + NL, 16), scale=-1.0)
-        for x in range(2):
-            ts(cols("whi", x, 32, 2), v("hki"), 17, A.arith_shift_right)
-        tt(v("sd"), v("cd"), v("dd%d" % t), A.subtract)
+        ts(v("sli"), v("hki"), NS - 1, A.bitwise_and)
+        ts(v("nsl"), v("sli"), -1.0, A.mult)
+        ts(v("whi"), v("hki"), 17, A.arith_shift_right)
+        tt(v("sd"), v("cd"), v("dd", ALL, slice(16 * t, 16 * t + 16), ALL), A.subtract)
+        sent["c%d" % t] = F["last"]()
 
-    def alike(ks):
+    def alike(t, ks=range(NG)):
         for k in ks:
-            bank = 512 * (turn[0] % 4)
-            turn[0] += 1
-            sel = rows("sg", 16, 128 * k, 128 * k + 128)
-            for c, j, i in ((0, 0, 0), (128, 0, 128), (256, 128, 128)):
-                mm(ps(bank + c, bank + c + 128), sel, rows("st", 16, i, i + 128), True, False)
-                mm(ps(bank + c, bank + c + 128), rows("nst", 16, j, j + 128), sel, False, True)
-            tt(v("eq", ALL, k, ALL), ps(bank, bank + 384), v("tri"), A.is_equal)
+            if k % 2 == 0:
+                turn[0] += 1
+            a = 512 * (turn[0] % 4) + NL * (k % 2)
+            mm(ps(a, a + NL), rows("sg", 16, 128 * k, 128 * k + 128), rows("st", 16, 0, NL))
+            for h in range(2):
+                out, own = v("eq", ALL, k, slice(NL * h, NL + 128 * h)), cols("nsl", 8 * h + k, 8 * h + k + 1)
+                if k in ON_SCALAR:
+                    act(cols("gtf", 384 * k + NL * h, 384 * k + NL + 128 * h), ps(a + 128 * h, a + NL), AF.Abs, bias=own)
+                else:
+                    ts(out, ps(a + 128 * h, a + NL), own, A.add, 0.0, A.is_equal)
+            if k in ON_SCALAR:
+                act(v("eq", ALL, k, ALL), cols("gtf", 384 * k, 384 * k + 384), AF.Relu, scale=-1.0, bias=1.0)
+        turn[0] += 1
+        sent["g%d" % t] = F["last"]()
 
     def answer(t):
         C("v", "scan", out=v("kf"), data0=v("rst"), data1=ps(KF, KF + NL), initial=0.0, op0=A.mult, op1=A.max)
-        copy("v", v("wq%d" % t), cols("kf", 15, NL, 16))
-        return tell("wq%d" % t, 16, "lr%d" % t, "a_r%d" % t)
+        copy("v", cols("wq", 16 * t, 16 * t + 16), cols("kf", 15, NL, 16))
+        sent["a%d" % t] = F["last"]()
+        sent["r%d" % t] = tell(cols("wq", 16 * t, 16 * t + 16), 16, "lr%d" % t, "a_r%d" % t)
 
     def decide(t, lists):
         mm(ps(P6, P6 + 16), v("idb"), v("li"), True, False)
-        tt(v("wm"), ind(v("lr%d" % t), cols("lst", 4 + 2 * t, 6 + 2 * t)), v("whi"), A.max)
-        ts(v("go_"), v("wm"), 8.0, A.is_lt)
+        tt(v("wm"), ind(v("lr%d" % t), cols("lst", 2 * t, 2 * t + 1)), v("whi"), A.max)
+        ts(v("gw"), v("wm"), 8.0, A.is_lt, PC["w3"], A.mult)
+        ts(cols("gb", 0, 8), cols("wm", 0, 8), 8.0, A.is_lt, TOP, A.mult)
+        ts(v("thr"), v("wm"), 8.0, A.is_lt, PC["w6"], A.mult)
         ts(v("ng"), v("wm"), 8.0, A.is_ge)
-        for k in range(NG):
-            for c, j, i in ((0, 0, 0), (128, 0, 1), (256, 1, 1)):
-                a = KF + 16 * i + 2 * k
-                mm(ps(a, a + 2), v("eq", ALL, k, slice(c, c + 128)), v("go_", ALL, 8 * j + k, ALL), c != 256, c != 128)
-        for h in range(2):
-            tt(v("ttl", ALL, h, slice(24, 32)), cols("wm", 16 * h, 16 * h + 16, 2), lane("ng", h, 0), A.mult)
-        tt(v("win"), ps(KF, KF + 32), v("go_"), A.is_lt)
-        tt(v("ttl", ALL, ALL, slice(0, 16)), v("sd"), v("win"), A.mult)
-        copy("v", v("ttl", ALL, ALL, slice(16, 24)), v("win", ALL, ALL, 0))
+        for c, j, i, w in ((0, 0, 0, "gw"), (128, 0, 1, "gb"), (256, 1, 1, "gw")):
+            for k in range(NG):
+                a, b = KF + 8 * i + k, 8 * j + k
+                mm(ps(a, a + 1), v("eq", ALL, k, slice(c, c + 128)), cols(w, b, b + 1), c + k == 0, c + k == 256 + NG - 1)
+        win = v("ttl", ALL, ALL, slice(16, 24))
+        tt(v("ttl", ALL, ALL, slice(24, 32)), v("wm"), v("ng"), A.mult)
+        tt(win, ps(KF, KF + 16), v("thr"), A.is_lt)
+        for x in range(2):
+            tt(v("ttl", ALL, ALL, slice(x, 16, 2)), v("sd", ALL, ALL, x), win, A.mult)
         for h in range(2):
             mm(ps(P7 + 128 * h, P7 + 128 * h + 128, 32), v("ttl", ALL, h, ALL), v("idb"))
         copy("v", rows("t1", 32, 0, NL), ps(P7, P7 + NL, 32))
+        if t == 1 and OCC == "t1":
+            gate[:] = [F["last"]()]
+            scatter("occ", "w0", cols("idf", 64, 320))
+            gate[:] = []
         for i in range(16):
             mm(ps(P6, P6 + 16), rows("ew", 32, 15 - i, 143 - i), rows("t1", 32, i, NL, 16), False, i == 15)
-        mm(row, rows("er", 32, 0, 128), rows("t1", 32, 0, NL))
-        ts(cols(lists, 0, 16), ps(P6, P6 + 16), float(DUMP + NL * t), A.add)
+        mm(row, rows("er", 32, 0, 128), rows("t1", 32, 0, NL), True, t > 0)
+        if t == 0:
+            mm(row, v("idb"), cols("pay", 64, 320), False, True)
+            act(cols("pay", 64, 320), row)
+        else:
+            ts(cols(lists, 0, 16), ps(P6, P6 + 16), float(DUMP + NL * t), A.add)
 
     def wrapped(a, n, el, src, first, start=True, stop=True):
         for i in range(16):
@@ -490,19 +628,13 @@ def rank_main(g, core, rank, T, topo):
     def scatter(table, lists, vals):
         copy("v", ind(v(table), cols(lists, 0, 16)), vals)
 
-    def wrap():
-        copy("v", cols("tb", NS, DUMP), cols("tb", 0, WR))
+    def wrap(table="tb"):
+        copy("v", cols(table, NS, DUMP), cols(table, 0, WR))
 
-    zrep("s", "h", 0, 128, cols("z_s", 64, 192))
-    zrep("s", "h", 128, 160, cols("z_s", 192, 224))
-    asks = [dma("y", v("efq0"), v("rl")), dma("y", v("zlf"), v("zl"))]
-    ts(PC["m0"], PC["a"], 0.0, A.is_equal)
-    ts(PC["m1"], PC["a"], 1.0, A.is_equal)
+    ts(cols("pc", 4, 8), cols("rr", 0, 4), PC["a"], A.is_equal)
     ts(PC["m01"], PC["a"], 2.0, A.is_lt)
-    ts(PC["m2"], PC["a"], 2.0, A.is_equal)
-    ts(PC["m3"], PC["a"], 3.0, A.is_equal)
     ts(PC["c15"], PC["g"], 16.0, A.mult, 15.0, A.add)
-    for name, m, w in (("el", "m01", None), ("el2", "m2", None), ("el3", "m3", None), ("eln", "m0", -1.0)):
+    for name, m in (("el", "m01"), ("el2", "m2"), ("el3", "m3"), ("eln", "m0")):
         ts(v(name), r144, PC["c15"], A.is_equal, PC[m], A.mult)
     ts(v("eln"), v("eln"), -1.0, A.mult)
     bitcol(PC["half"], 1, 63)
@@ -526,14 +658,14 @@ def rank_main(g, core, rank, T, topo):
     tt(v("ntr"), v("ntr"), v("onb"), A.mult)
     ts(v("onb1"), cols("m16", 0, 128), 1.0, A.is_equal, -1.0, A.mult)
     tt(v("onb1"), v("onb1"), v("onb"), A.mult)
-    ts(cols("tri", 0, 128), r128, PC["p"], A.is_le, 0.5, A.mult)
-    fill(cols("tri", 128, 256), 0.0)
-    copy("v", cols("tri", 256, 384), cols("tri", 0, 128))
-    ts(v("m16"), v("m16"), PC["a"], A.is_equal)
-    for t in range(3):
-        for h in range(2):
-            fill(lane("dd%d" % t, h, 0), 64.0 + 4 * t + 2 * h)
-        ts(v("dd%d" % t, ALL, ALL, 1), cols("ob", 0, 16), PC["p"], A.mult, 32.0, A.add)
+    fill(cols("xq", 0, 128), 1.0 / 3)
+    fill(cols("xq", 128, NL), 0.0)
+    C("v", "scan", out=cols("dq", 0, 128), data0=cols("xq", 0, 128), data1=cols("xq", 128, NL), initial=TOP, op0=A.mult, op1=A.add)
+    tt(cols("dq", 128, NL), cols("dq", 0, 128), v("id32"), A.mult)
+    C("v", "tensor_reduce", out=PC["w3"], in_=cols("dq", 128, NL), axis=AxisListType.X, op=A.add)
+    ts(PC["w6"], PC["w3"], 2.0, A.mult)
+    iota(v("dd", ALL, ALL, 0), [[2, 6], [0, 8]], 64, 0)
+    ts(v("dd", ALL, ALL, 1), cols("ob", 0, 48), PC["p"], A.mult, 32.0, A.add)
     ts(v("yw"), cols("rr", 0, 48), 16.0, A.mult, PC["a"], A.add)
     copy("v", v("li"), cols("yw", 0, 16))
     ts(v("yc"), v("yw"), 600.0, A.add)
@@ -548,71 +680,63 @@ def rank_main(g, core, rank, T, topo):
             copy("v", v("pm2"), cols("pay", 512, NF))
     ts(PC["x"], PC["m1"], 64.0, A.mult)
     ts(v("pm1"), cols("pay", 256, 512), PC["x"], A.add)
-    for x, (t, sh) in enumerate(((1, 4), (2, 4), (0, 1), (1, 1), (2, 1))):
-        ts(cols("qi", x, x + 1), pint, sh, A.arith_shift_right, 7, A.bitwise_and)
-        ts(cols("qi", x, x + 1), cols("qi", x, x + 1), float(t), A.add)
-    ts(cols("q2", 0, 5), cols("qi", 0, 5), float(N - 1), A.is_ge, -float(N - 1), A.mult)
-    tt(cols("qi", 0, 5), cols("qi", 0, 5), cols("q2", 0, 5), A.add)
-    ts(cols("qi", 0, 2), cols("qi", 0, 2), -1.0, A.mult, float(rank + N - 1), A.add)
-    ts(cols("qi", 2, 5), cols("qi", 2, 5), float(rank + 1), A.add)
-    ts(cols("qi", 0, 5), cols("qi", 0, 5), N - 1, A.bitwise_and)
-    ts(cols("tmp", 0, 2), cols("qi", 0, 2), 24.0, A.mult)
-    bitcol(PC["x"], 1, 7)
-    ts(cols("tmp", 2, 5), cols("qi", 2, 5), 16.0, A.mult, PC["x"], A.add)
+    ts(cols("hki", 0, 1), pint, 7, A.bitwise_and)
+    ts(cols("hki", 1, 2), pint, 4, A.arith_shift_right)
+    copy("v", cols("tmp", 8, 10), cols("hki", 0, 2))
+    ts(cols("hki", 0, 3), cols("rr", 0, 3), cols("tmp", 8, 9), A.add)
+    ts(cols("hki", 3, 5), cols("rr", 1, 3), cols("tmp", 9, 10), A.add)
+    ts(cols("hki", 8, 13), cols("hki", 0, 5), float(N - 1), A.is_ge, -float(N - 1), A.mult)
+    tt(cols("hki", 0, 5), cols("hki", 0, 5), cols("hki", 8, 13), A.add)
+    ts(cols("hki", 0, 3), cols("hki", 0, 3), float(rank + 1), A.add)
+    ts(cols("hki", 3, 5), cols("hki", 3, 5), -1.0, A.mult, float(rank + N - 1), A.add)
+    ts(cols("hki", 0, 5), cols("hki", 0, 5), N - 1, A.bitwise_and)
+    ts(cols("lst", 0, 6, 2), cols("hki", 0, 3), 16.0, A.mult, PC["a"], A.add)
+    ts(cols("lst", 6, 10, 2), cols("hki", 3, 5), 24.0, A.mult, PC["a"], A.add)
+    ts(cols("tmp", 8, 10), cols("hki", 3, 5), 24.0, A.mult)
     for t in (1, 2):
-        ts(cols("lst", 2 * t - 2, 2 * t - 1), cols("tmp", t - 1, t), PC["a"], A.add)
-        ts(cols("lrep", 16 * t - 16, 16 * t - 4), cols("rr", 12, 24), cols("tmp", t - 1, t), A.add)
-    for t in range(3):
-        ts(cols("lst", 4 + 2 * t, 6 + 2 * t), cols("rr", 0, 16, 8), cols("tmp", 2 + t, 3 + t), A.add)
-    for name, w in (("la1", 24), ("la2", 24), ("lr0", 16), ("lr1", 16), ("lr2", 16)):
+        ts(cols("lst", 12 * t - 2, 12 * t + 10), cols("rr", 12, 24), cols("tmp", 7 + t, 8 + t), A.add)
+    ts(v("m16"), v("m16"), PC["a"], A.is_equal)
+    for name, w in (("lr0", 16), ("lr1", 16), ("lr2", 16), ("la1", 24), ("la2", 24)):
         fill(cols(name, w * rank, w * rank + w), 0.0)
     for name in ("r1", "r2", "r3"):
         fill(cols(name, NL, ZC), 0.0)
+    setup[0] = False
 
-    dma("y", v("rda"), v("ef"), 4000, [table])
-    dma("y", v("zda"), v("zf"), 4000, [table])
-    dma("y", cols("z_s", 320, NF), v("zf", ALL, slice(NL, 704)), after=asks)
-    dma("y", cols("z_s", 0, 64), v("zf", ALL, slice(704, NF)), after=asks)
-    dma("y", cols("eh_s", 320, NF), v("eh", ALL, slice(NL, 704)), after=asks)
-    dma("y", cols("eh_s", 0, 64), v("eh", ALL, slice(704, NF)), after=asks)
-
-    def bulk(t, after):
-        by_group((("zda", "zl%d" % t), ("rda", "rl%d" % t)), [T.cores[asked(rank, k, t)] for k in range(NG)], "a_b%d" % t, 12000, after)
-
-    for a in range(0, NT, NT // 8):
-        iota(cols("occ", a, a + NT // 8), [[0, NT // 8]], -1, 0)
-    bulk(1, ())
-
-    s0 = look("v", "h", 0, 128, NS)
-    s1 = look("s", "h", 192, 256, NS, cols("z_s", 256, 320))
-    s0()
-    s0 = look("v", "h", 128, 160, NS)
-    s1()
-    s1 = look("s", "h", 160, 192, NS, cols("z_s", 224, 256))
-    copy("v", v("offf"), v("efq0"))
-    s0()
-    zrep("v", "f", 0, 128)
-    s1()
-    s1 = look("s", "f", 192, 256, NS)
-    s0 = look("v", "f", 0, 64, NS)
-    s1()
-    s0()
-    choose(0)
-    s1 = look("s", "f", 128, 192, NS)
-    s0 = look("v", "f", 64, 128, NS)
-    s0()
-    s1()
-    bulk(2, [answer(0)])
+    lazy[0] = False
+    dma("y", v("eda"), v("ef"), 3500, [table])
+    dma("y", v("zda"), v("zf"), 4000)
+    asks = [dma("y", v("zlf"), v("zl0")), dma("y", v("efq0"), v("rl0"))]
+    sent["b1"] = by_group((("eda", "rl1"), ("zda", "zl1")), to_asked(1), "a_b1", BULK) - 1
+    lazy[0] = True
+    for name, src in (("z_s", "zf"), ("eh_s", "eh")):
+        dma("y", cols(name, 320, NF), v(src, ALL, slice(NL, 704)), after=asks)
+        dma("y", cols(name, 0, 64), v(src, ALL, slice(704, NF)), after=asks)
+    for x, a in enumerate(range(0, NT, NT // 16)):
+        gate[:] = [sent["q0"] if x < EARLY else sent["b1"]]
+        iota(cols("occ", a, a + NT // 16), [[0, NT // 16]], -1, 0)
+    gate[:] = []
     for a, b, c in ((0, 64, 704.0), (64, 320, 0.0), (320, 576, 256.0), (576, NF, 512.0)):
         act(cols("idf", a, b), cols("rr", 0, b - a), AF.Identity, bias=c)
-    alike(range(NG))
+    lazy[0] = False
+
+    copy("v", v("offf"), v("efq0"))
+    for x in PLAN[0].split():
+        if x == "answer":
+            answer(0)
+            continue
+        what, a, b = x.split(":")
+        a, b = int(a), int(b)
+        src = cols("z_s", 64 + a, 64 + b) if what[1] == "h" else None
+        if what[0] == "z":
+            zrep(what[2], what[1], a, b, src)
+        else:
+            look(what[0], what[1], a, b, NS, src, int(what[2:] or 0))
+    by_group((("zda", "zl2"),), to_asked(2), "a_b2", BULK, [sent["r0"][0]])
+    choose(0)
+    alike(0)
+    dma("y", cols("eu1", 64, NF + 64), v("rl1"))
+    dma("y", cols("zq1", 64, NF + 64), v("zl1"))
     decide(0, "w0")
-
-    def fetch(t):
-        for name, src in (("efq%d" % t, "rl%d" % t), ("zq%d" % t, "zl%d" % t)):
-            dma("y", cols(name, 64, NF + 64), v(src))
-
-    fetch(1)
 
     def lanes(t, m0, m1, placed):
         n = m1 - m0
@@ -628,80 +752,118 @@ def rank_main(g, core, rank, T, topo):
         mm(ps(KH, KH + n), v("ntr"), cols("uu", 0, n), True, False)
         mm(ps(KH, KH + n), v("onb"), cols("scn", 0, n), False, True)
         mm(ps(KH + 64, KH + 65), v("onb1"), cols("scn", n - 1, n))
-        if t == 1:
-            tt(cols("pay", 64, 320), row, cols("pay", 64, 320), A.add)
         tt(cols("dst", 0, n), ps(KH, KH + n), cols("vb", 0, n), A.max)
         ts(cols("dsu", 0, n), cols("dst", 0, n), 63.0, A.add)
         ts(cols("nrow", FIX, NL), cols("pm%d" % t, 0, DYN), ps(KH + 64, KH + 65), A.add)
         copy("v", ind(v("nrow"), cols("dsu", 0, n)), cols(pay, 16 * m0, 16 * m1))
-        wrapped(P6 + 32, 12, "el", "nrow", FIX)
-        wrapped(P6 + 44, 12, "el2", "nrow", FIX)
+        packed = F["last"]()
+        wrapped(KF + 32, 12, "el", "nrow", FIX)
+        wrapped(KF + 44, 12, "el2", "nrow", FIX)
+        copy("v", cols("msg", 24 * t - 24, 24 * t), ps(KF + 32, KF + 56))
+        sent["m%d" % t] = F["last"]()
+        sent["q%d" % t] = tell(cols("msg", 24 * t - 24, 24 * t), 24, "la%d" % t, "a_q%d" % t)
         mm(ps(KH + 65, KH + 66), v("onb"), cols("scn", n - 1, n))
         mm(ps(KH + 128, KH + 128 + DYN), v("ex2"), cols("nrow", FIX, NL))
-        prev = "w%d" % (t - 1)
-        scatter("tb", prev, cols("z_s", 64, 320) if t == 1 else v("zlh"))
-        wrap()
-        copy("v", v("msg%d" % t), ps(P6 + 32, P6 + 56))
-        tell("msg%d" % t, 24, "la%d" % t, "a_q%d" % t)
-        copy("v", cols(L, 20, 32), ps(P6 + 32, P6 + 44))
-        act(cols("dc", FIX, NL), ps(KH + 128, KH + 128 + DYN), AF.Identity, bias=PC["ck"])
-        ts(cols(inv, m0, m1), cols("dst", 0, n), 63.0, A.add, float(NL), A.min)
-        ts(PC["y"], ps(KH + 65, KH + 66), float(FIX - 16 * m1), A.add)
-        ts(cols(inv, m1, m1 + 12), cols("yw", m1, m1 + 12), PC["y"], A.add, float(NL), A.min)
+        if t == 1 or not TB_EARLY:
+            gate[:] = [packed]
+            if t == 1:
+                ts(v("w0"), ps(P6, P6 + 16), float(DUMP), A.add)
+            scatter("tb", "w%d" % (t - 1), cols("z_s", 64, 320) if t == 1 else v("zlh"))
+            gate[:] = []
+            wrap()
+        copy("v", cols(L, 20, 32), ps(KF + 32, KF + 44))
+        if DC == "s":
+            act(cols("dc", FIX, NL), ps(KH + 128, KH + 128 + DYN), AF.Identity, bias=PC["ck"])
+        else:
+            ts(cols("dc", FIX, NL), ps(KH + 128, KH + 128 + DYN), PC["ck"], A.add)
+        act(PC["y"], ps(KH + 65, KH + 66), AF.Identity, bias=float(FIX - 16 * m1))
+
+    def way_back(t, m0, m1):
+        gate[:] = [sent[BACK % t]]
+        ts(cols("inv%d" % t, m0, m1), cols("dst", 0, m1 - m0), 63.0, A.add, float(NL), A.min)
+        ts(cols("inv%d" % t, m1, m1 + 12), cols("yw", m1, m1 + 12), PC["y"], A.add, float(NL), A.min)
+        gate[:] = []
 
     def step(t):
-        L, efq, zq, la = "w%d" % t, "efq%d" % t, "zq%d" % t, "la%d" % t
+        sent["e%d" % t] = sent["m%d" % t]
+        L, la, zq, efq = "w%d" % t, "la%d" % t, "zq%d" % t, "eu%d" % t
+        f0 = NF if t == 1 else 704
         y0 = 0 if t == 1 else 704
-        f0 = y0
-        for name in (efq, zq):
-            copy("v", cols(name, 0, 64), cols(name, NF, NF + 64))
         dyn = cols(L, 20, 32)
+        lazy[0] = True
+        gate[:] = [sent[BACK % (t - 1)]]
         ts(cols("xp", 0, FIX), cols("eh_s", y0, y0 + FIX), PC["ck"], A.add)
         copy("v", cols("offh", 0, FIX), cols("eh_s", y0, y0 + FIX))
         copy("v", cols("offf", 0, FIX), cols(efq, f0, f0 + FIX))
-        sa = look("s", "f", 0, FIX, src=cols(zq, f0, f0 + FIX))
-        copy("v", v("zlh"), ind(v("z_s"), cols(L, 16, 32)))
+        gate[:] = []
+        if "vh:0:64" in PLAN[t] or "vh1:0:64" in PLAN[t]:
+            zrep("g", "h", 0, FIX, cols("z_s", y0, y0 + FIX))
+        if "vf:0:64" in PLAN[t] or "vf1:0:64" in PLAN[t]:
+            zrep("g", "f", 0, FIX, cols(zq, y0, y0 + FIX))
+        gate[:] = [sent["e%d" % t]]
+        copy("v", cols(efq, 0, 64), cols(efq, NF, NF + 64))
+        copy("s", cols(zq, 0, 64), cols(zq, NF, NF + 64))
+        gate[:] = []
+        lazy[0] = False
+        copy(ZLH, v("zlh"), ind(v("z_s"), cols(L, 16, 32)))
+        lanes_z = F["last"]()
+        held = [sent["a%d" % (t - 1)]]
         tt(cols("xp", FIX, NL), ind(v("eh_s"), dyn), cols("dc", FIX, NL), A.add)
         ts(cols("offh", FIX, NL), cols("xp", FIX, NL), PC["ck"], A.subtract)
-        zrep("v", "h", 128, 256)
-        sa()
-        sa = look("s", "h", 0, FIX)
-        sb = look("v", "h", 128, 256)
-        sa()
-        sa = look("s", "h", 64, 128)
-        sb()
-        copy("v", v("lq"), ind(v(la), cols("lst", 2 * t - 2, 2 * t - 1)))
-        tt(cols("dm", 0, DYN), ind(v(la), cols("lrep", 16 * t - 16, 16 * t - 4)), cols("m16", 0, DYN), A.mult)
-        sa()
-        mm(ps(P6 + 64, P6 + 64 + DYN), v("onb"), cols("dm", 0, DYN))
-        copy("v", cols("zlf", FIX, NL), ind(v(zq), cols("lq", 0, 12)))
-        copy("s", cols("dq", 0, DYN), ps(P6 + 64, P6 + 64 + DYN))
-        tt(cols("xq", 0, DYN), ind(v(efq), cols("lq", 0, 12)), cols("dq", 0, DYN), A.add)
-        copy("v", cols("offf", FIX, NL), cols("xq", 0, DYN))
-        sa = look("s", "f", 64, 128)
-        zrep("v", "f", 160, 256)
-        choose(t)
-        sa()
-        sa = look("s", "f", 128, 160)
-        sb = look("v", "f", 160, 192)
-        sc = look("v", "f", 192, 256)
-        sb()
-        sa()
-        sc()
-        answer(t)
+        sent["o%d" % t] = F["last"]()
+
+        for x in PLAN[t].split():
+            if x == "asks":
+                copy("v", v("lq"), ind(v(la), cols("lst", 4 + 2 * t, 5 + 2 * t)))
+                tt(cols("dm", 0, DYN), ind(v(la), cols("lst", 12 * t - 2, 12 * t + 10)), cols("m16", 0, DYN), A.mult)
+                mm(ps(P6 + 64, P6 + 64 + DYN), v("onb"), cols("dm", 0, DYN))
+                copy("v", cols("dq", 0, DYN), ind(v(efq), cols("lq", 0, 12)))
+                copy(ZLF, cols("zlf", FIX, NL), ind(v(zq), cols("lq", 0, 12)))
+                tt(cols("xq", 0, DYN), ps(P6 + 64, P6 + 64 + DYN), cols("dq", 0, DYN), A.add)
+                copy("v", cols("offf", FIX, NL), cols("xq", 0, DYN))
+            elif x == "answer":
+                answer(t)
+            elif x == "choose":
+                choose(t)
+            elif x == "alike":
+                alike(t)
+            else:
+                what, a, b = x.split(":")
+                a, b = int(a), int(b)
+                src = None if a else cols("z_s", y0, y0 + FIX) if what[1] == "h" else cols(zq, f0, f0 + FIX)
+                if what[0] == "z":
+                    zrep(what[2], what[1], a, b, src)
+                else:
+                    gate[:] = [lanes_z] if ZLH == "s" and (t == 1 or a) else []
+                    inline[:] = [held[0]] if STRICT else []
+                    look(what[0], what[1], a, b, src=src, part=int(what[2:] or 0))
+                    held[0] = inline[0] if STRICT else 0
+                    gate[:], inline[:] = [], []
+        gate[:] = [sent["a%d" % t]]
         copy("s", v("lnf%d" % t), ind(v("idf"), cols(L, 16, 32)))
-        alike(range(NG))
+        gate[:] = []
 
     lanes(1, 4, 20, ps(P6, P6 + 16))
     step(1)
-    scatter("occ", "w0", cols("idf", 64, 320))
-    fetch(2)
+    way_back(1, 4, 20)
+    lazy[0] = True
+    if OCC != "t1":
+        gate[:] = [sent[OCC]]
+        scatter("occ", "w0", cols("idf", 64, 320))
+        gate[:] = []
     wrapped(KH, 32, "el3", "pay", 0, True, False)
+    lazy[0] = False
     decide(1, "w1")
+    by_group((("eda", "rl2"),), to_asked(2), "a_b3", BULK, [sent["q1"][0]])
+    dma("y", cols("zq2", 64, NF + 64), v("zl2"), after=[sent["q1"][1]])
+    dma("y", cols("eu2", 64, NF + 64), v("rl2"), after=[sent["r1"][1]])
     copy("s", cols("r1", 0, NL), row)
     scatter("occ", "w1", v("lnf1"))
     copy("s", cols("g1", 0, 512), ind(v("r1"), v("inv1")))
     tt(v("b1"), ind(v("occ"), v("w0")), cols("idf", 64, 320), A.not_equal)
+    if TB_EARLY:
+        scatter("tb", "w1", v("zlh"))
+        wrap()
     wrapped(KH, 32, "el3", "g1", 0, False, False)
     wrapped(KH + 4, 16, "eln", "b1", 0, False, True)
     mm(ps(0, 512), v("idb"), cols("pay", 0, 512), True, False)
@@ -711,9 +873,10 @@ def rank_main(g, core, rank, T, topo):
     copy("s", cols("pay2", 512, NF), cols("pay", 512, NF))
     lanes(2, 0, 32, ps(KH, KH + 32))
     step(2)
+    way_back(2, 0, 32)
     decide(2, "w2")
     scatter("tb", "w2", v("zlh"))
-    dma("y", v("yt"), cols("tb", 0, NS))
+    dma("y", v("yt"), cols("tb", 0, NS), 5500)
     copy("s", cols("r2", 0, NL), row)
     copy("s", v("g2"), ind(v("r2"), v("inv2")))
     scatter("occ", "w2", v("lnf2"))

@@ -3,64 +3,67 @@ from concourse.bass import DstId, RemoteDMATransfer
 from concourse.mybir import AluOpType as A, AxisListType, ActivationFunctionType as AF
 
 N, NG, NS, NF, NL = 8, 8, 4096, 768, 256
+CORES_ALL = 64
 WR = 32
 NT = NS + WR + 3 * NL
 DUMP = NS + WR
 FIX = 64
 DYN = NL - FIX
 ZC = NL + 16
+BIG = 8192.0
+NCH, CH = 8, 512
 TYPES = {"b": "bfloat16", "f": "float32", "i": "int32", "u": "uint16"}
 SCRATCH = {"psb": ("psum", [128, 4096], "float32")}
+PACKED = {}
 for _where, _shape, _names in (
-        ("sbuf", [128, NT], "b:tb f:occ"),
-        ("sbuf", [128, NF], "i:eh_s b:z_s b:pay b:pay2 f:idf b:g1 b:g2 b:g3 f:ydf"),
-        ("sbuf", [128, NF + 64], "i:eu1 i:eu2 b:zq1 b:zq2"),
-        ("sbuf", [128, 4096], "b:zrh b:zrf b:cmh b:cmf b:gth b:gtf"), ("sbuf", [128, 1280], "b:nrow"),
-        ("sbuf", [128, NL], "i:efq0 f:xp f:xq f:dc f:dq u:offh u:offf b:zlh b:zlf f:lnf1 f:lnf2 b:b1 b:b3 b:t1 b:dm b:st "
-                            "f:kh b:kf b:rst b:m16 b:rr b:pm1 b:pm2 b:mid"),
-        ("sbuf", [128, ZC], "b:r1 b:r2 b:r3"), ("sbuf", [128, 8, 384], "b:eq"),
-        ("sbuf", [128, 16], "u:w0 u:lq b:li i:hki i:sli f:nsl i:whi b:wm b:gw b:gb f:thr b:ng f:tmp"),
-        ("sbuf", [128, 32], "u:w1 u:w2 u:inv1 u:dsu"), ("sbuf", [128, 48], "f:msg b:wq u:lst"),
-        ("sbuf", [128, N * 16], "b:lr0 b:lr1 b:lr2"), ("sbuf", [128, N * 24], "f:la1 f:la2"),
-        ("sbuf", [128, 16, 2], "i:di b:sd b:cd"), ("sbuf", [128, 48, 2], "b:dd"), ("sbuf", [128, 2, 32], "b:ttl"),
-        ("sbuf", [128, 48], "b:uu f:vb b:scn f:dst f:yc f:yw u:inv2"),
-        ("sbuf", [128, 8], "i:pi i:qi"), ("sbuf", [128, 32], "f:pc b:blk"),
-        ("sbuf", [128, 144], "b:ew b:el b:el2 b:el3 b:eln"),
-        ("sbuf", [128, 128], "f:id32 b:idb b:idn b:er b:onb b:onb1 b:ntr b:ex2 b:mk2 b:ob b:r16"), ("sbuf", [128, 1024], "b:sg"),
-        ("dram", [1024, 32], "i:ed0 b:zd0 i:rl0 b:zl0"),
-        ("dram", [1024, 96], "i:eda b:zda i:rl1 i:rl2 b:zl1 b:zl2")):
+        ("sbuf", [128, NT], "b:tb b:tf1 b:tf2 f:occ"),
+        ("sbuf", [128, NF], "i:eh_s i:ef_s b:z_s b:pay b:pay2 f:idf b:g1 b:g2 b:g3 f:ydf f:dm"),
+        ("sbuf", [128, 4096], "b:zrh b:zrf b:cvh b:cvf b:gth b:gtf"), ("sbuf", [128, 512], "b:each"), ("sbuf", [128, 1280], "b:nrow"),
+        ("sbuf", [128, NL], "b:zt0 b:zt1 b:zt2 b:ztf i:efq0 f:xp0 f:xp1 f:xp2 f:xq f:dc u:oh0 u:oh1 u:oh2 u:of0 u:of1 u:of2 b:zl1 b:zl2 b:zlf b:zu1 b:zu2 b:zu3 "
+                            "f:lnf1 f:lnf2 b:b1 b:b3 b:st f:kh b:kf b:rst b:m16 b:rr b:zb b:mid b:cl b:rl b:sgn b:whr b:wr0 "
+                            "f:xx b:sq i:ri b:xw b:d0r b:uu2 b:crow b:crow2 b:bv b:ob"),
+        ("sbuf", [128, ZC], "b:r1 b:r2 b:r3"), ("sbuf", [128, 8, 384], "b:eq"), ("sbuf", [128, 144], "b:kf0 b:kf1 b:md2 b:rs2"),
+        ("sbuf", [128, 8, 3, 16], "b:apad"), ("sbuf", [128, 16, 16], "b:ut"),
+        ("sbuf", [128, 16], "u:w0 u:w0k u:lu1 u:lu2 u:lu3 i:hki f:own f:tmp f:tmq b:wq b:pl0 b:fresh f:wk u:lst"),
+        ("sbuf", [128, 32], "u:w1 u:w2 u:inv1 u:dsu f:msg"),
+        ("sbuf", [128, N * 16], "b:lr0 f:la0 f:la1"),
+        ("sbuf", [128, 16, 4], "i:di b:cd"),
+        ("sbuf", [128, 48], "b:uu b:nb f:vb b:scn f:dst u:inv2"), ("sbuf", [128, 96], "f:yw"),
+        ("sbuf", [128, 8], "i:pi f:sel"), ("sbuf", [128, 32], "f:pc b:blk u:lrep"),
+        ("sbuf", [128, 144], "b:el b:el3 b:eln"),
+        ("sbuf", [128, 128], "f:id32 b:idb b:idn b:i8k b:i8n b:onb b:onb1 b:ntr b:ex2 b:mk2 b:rsel b:wsel b:tri b:tri2 b:o32 b:o2"),
+        ("sbuf", [128, 8, 128], "b:sg"), ("sbuf", [128, 8, 16], "b:osr"),
+        ("dram", [1024, 32], "i:ed0 b:zd0 i:rl0 b:zl0 b:zd1 b:zk1 b:zk2 b:zk3"),
+        ("dram", [2 * NCH * 128, CH], "b:hc"), ("dram", [2 * NCH * 1024, CH // 8], "b:hp b:ha")):
     for _n in _names.split():
-        SCRATCH[_n[2:]] = (_where, _shape, TYPES[_n[0]])
+        if _where == "sbuf" and len(_shape) == 2 and _shape[1] <= ZC:
+            _used = SCRATCH.get("all_" + _n[0], (0, [0, 0]))[1][1]
+            PACKED[_n[2:]] = ("all_" + _n[0], _used, _shape[1])
+            SCRATCH["all_" + _n[0]] = (_where, [128, _used + (_shape[1] + 15) // 16 * 16], TYPES[_n[0]])
+        else:
+            SCRATCH[_n[2:]] = (_where, _shape, TYPES[_n[0]])
 ENG = {"v": "ev", "s": "es", "p": "ep", "g": "eg"}
-SEMAPHORES = (["ev", "es", "ep", "eg", "lsem", "a_z0", "a_q0", "a_q1", "a_q2", "a_r0", "a_r1", "a_r2", "a_b1", "a_b2", "a_b3"]
-              + ["d%d" % k for k in range(28)])
+SEMAPHORES = (["ev", "es", "ep", "eg", "lsem", "ltab", "a_z0", "a_q0", "a_r0", "a_u0", "a_u1", "a_zu", "a_z1", "a_f1", "a_f2"]
+              + ["a_c%d" % c for c in range(2 * NCH)] + ["a_p%d" % k for k in range(2 * NCH)] + ["d%d" % k for k in range(40)])
 WRITES = ("out", "accum_out", "ap")
-CYCLE, WAKE, LONG = 0.83, 60.0, 250.0
-SWEEPS = 4
-LAST = [0]
-GREEDY = True
-BULK = 11000
-TELL, ASK0 = 3000, 5300
-PIECE = 128
-ZLH = "s"
-ASKS_FIRST = False
-BY_PROGRAM = True
-ZLF = "s"
-DQ = "s"
-EARLY = 6
+CYCLE, TENSOR, WAKE = 1.0, 0.5, 60.0
+TELL, ASK0, ASKZ = 2200, 5500, 5000
+SHORT, LOAD = 1600, 6300
+SLACK = 1500
+TABLE = 10000
 FUSED = 1.56
-CALL = 28.0
-TB_EARLY = True
-BACK = "g%d"
-STRICT = False
-DC, OCC = "s", "c1"
-ASKZ = 4300
-ON_SCALAR = (0, 1, 2)
-TOP = 9.0e29
-PLAN = {t: "sh1:0:64 zhv:128:256 vh:128:256 sf1:0:64 sh2:0:64 asks sh1:64:128 sf2:0:64 sh2:64:128 sf:64:128 zfv:128:256 vf:128:256 "
-           "answer choose alike" for t in (1, 2)}
-PLAN[0] = ("zhs:0:128 sh:192:256 vh:0:128 sh:128:192 "
-           "zfv:0:160 sf1:192:256 sf1:160:192 sf2:192:256 vf:0:128 sf2:160:192 vf:128:160 answer")
+CALL = 0.0
+ON_SCALAR = {0: (0, 1, 2), 1: (), 2: ()}
+OWN_PLANE = {(t, c) for t in (1, 2) for c in range(0, NCH, 2)}
+PLAN = {1: "keys offsets th:64:128:s back:0 gh:64:128 th:224:256:s gh:224:256 zh:128:224:v sh:64:128 vh:128:224 update sh:224:256 sh:0:64 "
+           "mh:0:128:s vf:128:224 mh:224:256:s mh:128:224:v gf:0:64 choose chosen spare back:1 alike gf:64:128 sf:0:64 gf:224:256 sf:64:128 "
+           "sf:224:256 mf:128:224:v mf:224:256:s mf:0:128:s fin:0 names fin:1",
+        2: "th:192:256:s gh:64:128 th:64:128:s sf:0:64 offsets gh:224:256 sh:64:128 zh:128:224:v mh:0:128:s sh:224:256 mh:224:256:s vf:128:192 "
+           "vh:128:224 mh:128:224:v gf:64:128 choose gf:192:256 sf:64:128 back:1 chosen sf:192:256 spare alike mf:128:192:v names mf:0:128:s "
+           "mf:192:256:s fin:0 fin:1"}
+PLAN[0] = ("zh:0:128:s th:128:256:s gh:192:256 vh:0:128 gh:128:192 sh:192:256 sh:128:192 mh:0:128:v mh:128:256:s "
+           "zf:0:160:v tf:128:256:s asks gf:192:256 vf:0:128 gf:160:192 sf:192:256 vf:128:160 sf:160:192 mf:0:128:v mf:192:256:s mf:128:160:v mf:160:192:s "
+           "choose answer chosen alike")
 MASKS = {}
 ALL = slice(None)
 
@@ -84,7 +87,7 @@ def off_chip(topo, src, dst):
 
 def far_engines(core, T, topo):
     for c in T.cores:
-        if off_chip(topo, core, c):
+        if off_chip(topo, core, c) and topo.may_write(core, c):
             return topo.engines(core, c)
     return []
 
@@ -113,7 +116,23 @@ def bits(engines):
     return m
 
 
+def helpers(core, T, topo):
+    mate = [c for c in range(CORES_ALL) if topo.mates(topo.chip(c), topo.chip(core)) and topo.die(c) == topo.die(core)]
+    beside = [c for c in topo.cores_of(core) if c != core and topo.die(c) == topo.die(core)]
+    senders = [c for c in beside if topo.may_write(c, mate[0])]
+    return senders, [c for c in beside if c not in senders], [c for c in mate if topo.may_write(c, core)]
+
+
+def joiner(rank, t, c, T, topo):
+    senders, own, mate = helpers(T.cores[rank], T, topo)
+    return own[0] if (t, c) in OWN_PLANE else mate[c // 2 % 2]
+
+
 def v(name, *idx):
+    if name in PACKED:
+        whole, first, width = PACKED[name]
+        a, b, c = (idx[1] if len(idx) > 1 else ALL).indices(width)
+        return ("v", whole, (idx[0] if idx else ALL, slice(first + a, first + b, c if c > 1 else None)))
     return ("v", name, idx if idx else (ALL,))
 
 
@@ -144,11 +163,18 @@ def region(view):
     return MASKS[key]
 
 
+def size(x):
+    if x[0] == "i":
+        return 16 * size(x[2])[0], False
+    return bin(region(x)[2]).count("1"), SCRATCH[x[1]][2] in ("bfloat16", "uint16")
+
+
 def flow(g, T):
     queues = {"v": g.vector, "s": g.scalar, "p": g.tensor, "g": g, "y": g.sync}
     known = {q: {} for q in queues}
-    total, acc, ops, banks, lazy = {}, {}, [], [{} for _ in range(8)], [False]
+    total, acc, ops, banks = {}, {}, [], [{} for _ in range(8)]
     gate = []
+    lazy = [False]
 
     def ap(x):
         if x[0] == "i":
@@ -185,83 +211,85 @@ def flow(g, T):
             acc[name] = old + [{"kind": kind, "p0": p0, "p1": p1, "m": m, "op": me}]
         for k in gate:
             dep.setdefault(k, ops[k]["q"] != q)
-        ops.append({"lazy": lazy[0], "name": str([parts(x)[0][1:] for x in writes][:1]), "q": q, "go": go, "sem": sem, "n": n, "busy": busy, "late": late, "dep": dep})
+        ops.append({"lazy": lazy[0] and q is not None, "q": q, "go": go, "sem": sem, "n": n, "busy": busy, "late": late, "dep": dep})
         return me
 
     def order():
         n = len(ops)
         before = [[(d, ops[d]["late"] + WAKE if hard else 0.0) for d, hard in o["dep"].items()] for o in ops]
-        behind = [[] for _ in ops]
-        way = [o["late"] for o in ops]
-        for k in range(n - 1, -1, -1):
-            way[k] += ops[k]["busy"]
-            for d, lag in before[k]:
-                behind[d].append((k, lag))
-                way[d] = max(way[d], way[k] + lag)
+        chain, tail = [list(b) for b in before], {}
+        for k, o in enumerate(ops):
+            if o["q"] in ("v", "s", "g") and not o["lazy"]:
+                if o["q"] in tail:
+                    chain[k].append((tail[o["q"]], 0.0))
+                tail[o["q"]] = k
 
-        def place(rank_, needs, floor):
-            taken, end = {q: [] for q in queues}, [0.0] * n
-            for k in sorted(range(n), key=rank_):
-                t, busy = max([floor[k]] + [end[d] + lag for d, lag in needs[k]]), ops[k]["busy"]
-                if ops[k]["q"] is not None:
-                    iv = taken[ops[k]["q"]]
-                    j = len(iv)
-                    while j and iv[j - 1][1] > t:
-                        j -= 1
-                    while j < len(iv) and iv[j][0] < t + busy - 1e-6:
-                        t = max(t, iv[j][1])
-                        j += 1
-                    lo, hi, a, b = j, j, t, t + busy
-                    if j and iv[j - 1][1] > t - 1e-6:
-                        lo, a = j - 1, iv[j - 1][0]
-                    if j < len(iv) and iv[j][0] < b + 1e-6:
-                        hi, b = j + 1, iv[j][1]
-                    iv[lo:hi] = [(a, b)]
-                end[k] = t + busy
-            return end
-
-        if GREEDY:
-            left = [len(o["dep"]) for o in ops]
-            ready = [0.0] * n
+        def run(needs, rank_, busy):
+            behind, left, ready, start = [[] for _ in ops], [len(x) for x in needs], [0.0] * n, [0.0] * n
+            for k in range(n):
+                for d, lag in needs[k]:
+                    behind[d].append((k, lag))
             free = {q: 0.0 for q in list(queues) + [None]}
             pool = {q: [k for k in range(n) if ops[k]["q"] == q and not left[k]] for q in free}
             out = []
             while len(out) < n:
-                best = None
-                for q in pool:
-                    if pool[q]:
-                        now = max(free[q], min(ready[k] for k in pool[q]))
-                        k = max((k for k in pool[q] if ready[k] <= now), key=lambda k: (way[k], -k))
-                        soon = [j for j in pool[q] if now < ready[j] < now + 0.5 * ops[k]["busy"] and way[j] > way[k] + ops[k]["busy"]]
-                        if soon:
-                            k = min(soon, key=lambda j: ready[j])
-                            now = ready[k]
-                        if best is None or now < best[0]:
-                            best = (now, k, q)
-                now, k, q = best
+                now, q = min(((max(free[q], min(ready[k] for k in pool[q])), q) for q in pool if pool[q]), key=lambda x: x[0])
+                k = min((k for k in pool[q] if ready[k] <= now), key=rank_)
                 pool[q].remove(k)
                 out.append(k)
+                start[k] = now
                 if q is not None:
-                    free[q] = now + ops[k]["busy"]
+                    free[q] = now + busy[k]
                 for u, lag in behind[k]:
-                    ready[u] = max(ready[u], now + ops[k]["busy"] + lag)
+                    ready[u] = max(ready[u], now + busy[k] + lag)
                     left[u] -= 1
                     if not left[u]:
                         pool[ops[u]["q"]].append(u)
-            return out
-        results = []
-        if BY_PROGRAM:
-            way = [-n if ops[k]["lazy"] else -k for k in range(n)]
-            for k in range(n - 1, -1, -1):
-                for d, lag in before[k]:
-                    way[d] = max(way[d], way[k])
-        for sweep in range(SWEEPS):
-            end = place(lambda k: (-way[k], k), before, [0.0] * n)
-            results.append((max(end[k] + ops[k]["late"] for k in range(n)), sorted(range(n), key=lambda k: (end[k] - ops[k]["busy"], k))))
-            way = place(lambda k: (-end[k], -k), behind, [o["late"] for o in ops])
-        LAST[0] = [r[0] for r in results]
-        LAST[1:] = [ops, before, end]
-        return min(results)[1]
+            return out, start, behind
+
+        busy = [o["busy"] for o in ops]
+        way = [o["late"] for o in ops]
+        for k in range(n - 1, -1, -1):
+            way[k] += 0.0 if ops[k]["lazy"] else busy[k]
+            for d, lag in chain[k]:
+                way[d] = max(way[d], way[k] + lag)
+        out, start, behind = run(chain, lambda k: (-way[k], k), [0.0 if o["lazy"] else o["busy"] for o in ops])
+        due = [1e9] * n
+        for k in range(n - 1, -1, -1):
+            if ops[k]["lazy"]:
+                due[k] = min([1e9] + [(due[u] if ops[u]["lazy"] else start[u]) - lag for u, lag in behind[k]]) - busy[k]
+        taken = {q: sorted((start[k] - (SLACK if q == "g" and ops[k]["late"] else 0.0), start[k] + busy[k])
+                           for k in range(n) if ops[k]["q"] == q and not ops[k]["lazy"]) for q in queues}
+        for k in sorted(range(n), key=lambda k: (due[k], k)):
+            if ops[k]["lazy"]:
+                t = first = max([0.0] + [start[d] + busy[d] + lag + (SLACK if ops[d]["q"] == "g" != ops[k]["q"] else 0.0) for d, lag in before[k]])
+                for a, b in taken[ops[k]["q"]]:
+                    if b > t:
+                        if a >= t + busy[k]:
+                            break
+                        t = b
+                if t > due[k]:
+                    t = max(first, due[k])
+                start[k] = t
+                taken[ops[k]["q"]] = sorted(taken[ops[k]["q"]] + [(t, t + busy[k])])
+        done, out = [False] * n, []
+
+        def emit(k):
+            todo = [k]
+            while todo:
+                j = todo[-1]
+                need = [d for d, lag in chain[j] if not done[d]]
+                if need:
+                    todo.append(min(need, key=lambda d: start[d]))
+                else:
+                    todo.pop()
+                    if not done[j]:
+                        done[j] = True
+                        out.append(j)
+
+        for k in sorted(range(n), key=lambda k: (start[k], k)):
+            emit(k)
+        return out
 
     def settle(q, ev):
         need = {}
@@ -277,16 +305,11 @@ def flow(g, T):
                 known[q][k] = max(known[q].get(k, 0), clk[k])
             known[q][sem] = max(known[q].get(sem, 0), cnt)
 
-    def size(x):
-        if x[0] == "i":
-            return 16 * size(x[2])[0], False
-        return bin(region(x)[2]).count("1"), SCRATCH[x[1]][2] in ("bfloat16", "uint16")
-
     def cost(q, meth, kw):
         out = kw.get("out") or kw["ap"]
         n, views = size(out)[0], [kw[k] for k in kw if is_view(kw[k])]
         if meth == "matmul":
-            return max(min(64, size(kw["lhsT"])[0]), n) * 0.42 * (1 if size(kw["rhs"])[1] else 4)
+            return max(min(64, size(kw["lhsT"])[0]), n) * TENSOR * (1 if size(kw["rhs"])[1] else 4)
         if q == "g":
             return 150 + 2 * n * CYCLE
         if out[0] == "i":
@@ -311,10 +334,11 @@ def flow(g, T):
         args = {k: (ap(kw[k]) if is_view(kw[k]) else kw[k]) for k in kw}
         eng = queues[q]
         f = {"tensor_copy": lambda: eng.tensor_copy(**args), "tensor_tensor": lambda: eng.tensor_tensor(**args),
-             "tensor_scalar": lambda: eng.tensor_scalar(**args), "tensor_reduce": lambda: eng.tensor_reduce(**args),
-             "scan": lambda: eng.tensor_tensor_scan(**args), "memset": lambda: eng.memset(args["ap"], args["constant"]),
+             "tensor_scalar": lambda: eng.tensor_scalar(**args), "scan": lambda: eng.tensor_tensor_scan(**args),
+             "memset": lambda: eng.memset(args["ap"], args["constant"]),
              "activation": lambda: eng.activation(**args), "matmul": lambda: eng.matmul(**args),
-             "iota": lambda: eng.iota(**args), "affine_select": lambda: eng.affine_select(**args)}[meth]
+             "affine_select": lambda: eng.affine_select(**args),
+             "iota": lambda: eng.iota(**args)}[meth]
         return add(q, reads, writes, lambda: f().then_inc(T.sem[ENG[q]], 1), ENG[q], 1, cost(q, meth, kw))
 
     def dma(q, sem, out, in_, late, after, behind):
@@ -347,11 +371,11 @@ def flow(g, T):
             if known["g"].get(sem, 0) < total[sem]:
                 g.wait_ge(T.sem[sem], total[sem])
 
-    return {"call": call, "dma": dma, "arrive": arrive, "fused": fused, "finish": finish, "lazy": lazy, "gate": gate, "last": lambda: len(ops) - 1}
+    return {"call": call, "dma": dma, "arrive": arrive, "fused": fused, "finish": finish, "gate": gate, "lazy": lazy, "last": lambda: len(ops) - 1}
 
 
-def blk(name, k):
-    return v(name, slice(128 * k, 128 * k + 128), ALL)
+def blk(name, k, n=128):
+    return v(name, slice(n * k, n * k + n), ALL)
 
 
 def cols(name, a, b, step=None):
@@ -362,74 +386,91 @@ def rows(name, n, a, b, step=None):
     return v(name, slice(0, n), slice(a, b, step))
 
 
-def helper_of(core, T, topo):
-    for c in topo.cores_of(core):
-        if T.rank_of(c) is None and topo.die(c) == topo.die(core) and all(topo.may_write(c, d) for d in T.cores):
-            return c
+def carry_engines(core, T, topo):
+    senders = helpers(core, T, topo)[0]
+    every = topo.engines(core, senders[0])
+    return [every[k * len(every) // 2:(k + 1) * len(every) // 2] for k in range(2)]
 
 
-def helper_main(g, core, rank, T, topo):
-    F = flow(g, T)
-    dst = [T.cores[asker(rank, k, 2)] for k in range(NG)]
-    eng = singles(core, dst, T, topo)
-    for q, src, piece, land in (("y", "hb", "td", "fd2"), ("s", "hz", "zd2", "zl2")):
-        F["arrive"]([v(src)], "a_" + src, len(near_engines(T.cores[rank], core, T, topo)), ())
-        F["dma"](q, "d1" if q == "y" else "d2", v(piece), v(src), 3000, (), None)
-        F["fused"]([(blk(piece, k), [(dst_id(topo, dst[k]), blk(land, k))], [eng[k]], "a_f2") for k in range(NG)], 3000)
-    F["finish"]()
+def sender_main(g, core, rank, j, T, topo):
+    mine = range(j, 2 * NCH, 2)
+    for s in mine:
+        t, c = 1 + s // NCH, s % NCH
+        g.sync.wait_ge(T.sem["a_c%d" % s], len(carry_engines(T.cores[rank], T, topo)[j]))
+        g.sync.dma_start(out=T["hp"][1024 * s:1024 * s + 1024, :], in_=T["hc"][128 * s:128 * s + 128, :]).then_inc(T.sem["d%d" % s], 16)
+        g.wait_ge(T.sem["d%d" % s], 16)
+        dst = [joiner(asker(rank, k, t), t, c, T, topo) for k in range(NG)]
+        eng = singles(core, dst, T, topo)
+        part = lambda name, k: T[name][1024 * s + 128 * k:1024 * s + 128 * k + 128, :]
+        g.remote_dma_fused([RemoteDMATransfer(dst_ids=[dst_id(topo, dst[k])], dma_engine_mask=bits([eng[k]]), remote_sem=T.sem["a_p%d" % s],
+                                              srcs=[part("hp", k)], dsts=[part("ha", k)]) for k in range(NG)], local_sem=T.sem["lsem"])
+    g.wait_ge(T.sem["lsem"], NG * len(mine))
+
+
+def joiner_main(g, core, rank, jobs, T, topo):
+    dst, left = T.cores[rank], 0
+    for k, (t, c) in enumerate(jobs):
+        slot = NCH * (t - 1) + c
+        g.sync.wait_ge(T.sem["a_p%d" % slot], NG)
+        g.sync.dma_start(out=T["gth"][:, CH * k:CH * k + CH], in_=T["ha"][1024 * slot:1024 * slot + 1024, :]).then_inc(T.sem["d%d" % k], 16)
+    for k, (t, c) in enumerate(jobs):
+        g.wait_ge(T.sem["d%d" % k], 16)
+        g.remote_dma_fused([RemoteDMATransfer(dst_ids=[dst_id(topo, dst)], dma_engine_mask=topo.mask(core, dst), remote_sem=T.sem["a_f%d" % t],
+                                              srcs=[T["gth"][:, CH * k:CH * k + CH]], dsts=[T["tf%d" % t][:, CH * c:CH * c + CH]])],
+                           local_sem=T.sem["lsem"])
+        left += len(topo.engines(core, dst))
+    g.wait_ge(T.sem["lsem"], left)
 
 
 def rank_main(g, core, rank, T, topo):
     F = flow(g, T)
     C, arrive, fused = F["call"], F["arrive"], F["fused"]
     ps = lambda a, b, n=128, step=None: v("psb", slice(0, n), slice(a, b, step))
-    KH, KF, P6, P7 = 2048, 2560, 3072, 3584
-    row = ps(P7 + 256, P7 + 512)
-    nd, turn, last, sent, inline, gate = [0], [0], {}, {}, [], F["gate"]
+    B = [512 * k for k in range(8)]
+    KH, OWN, LW, KF, PS, R = B[3], B[3] + 256, B[3] + 272, (B[6], B[7]), (B[6], B[7]), B[2]
+    nd, turn, last, sent, gate, lazy = [0], [0], {}, {}, F["gate"], F["lazy"]
     setup = [False]
 
-    def dma(q, out, in_, late=3000, after=()):
+    def bank():
+        turn[0] += 1
+        return B[turn[0] % 3]
+
+    def dma(q, out, in_, late=SHORT, after=()):
         nd[0] += 1
         last[q] = F["dma"](q, "d%d" % nd[0], out, in_, late, after, last.get(q))
         return last[q]
 
     def act(out, in_, func=AF.Copy, **kw):
-        if inline:
-            gate.append(inline[0])
-        k = C("s", "activation", out=out, in_=in_, func=func, **kw)
-        if inline:
-            gate.pop()
-            inline[0] = k
-
-    def copy(q, out, in_):
-        if q == "s" or (setup[0] and real(out, in_)):
-            act(out, in_)
-        elif q == "g":
-            C("g", "affine_select", out=out, in_=in_, pattern=[[0, FIX]], compare_op=A.is_ge, fill=0.0, base=0, channel_multiplier=0)
-        else:
-            C("v", "tensor_copy", out=out, in_=in_)
-
-    def tt(out, a, b, op):
-        C("v", "tensor_tensor", out=out, in0=a, in1=b, op=op)
+        return C("s", "activation", out=out, in_=in_, func=func, **kw)
 
     real = lambda *xs: all(SCRATCH[x[1]][2] in ("float32", "bfloat16") for x in xs)
 
+    def copy(q, out, in_):
+        if q == "s" or (setup[0] and real(out, in_)):
+            return act(out, in_)
+        return C("v", "tensor_copy", out=out, in_=in_)
+
+    def tt(out, a, b, op):
+        return C("v", "tensor_tensor", out=out, in0=a, in1=b, op=op)
+
     def ts(out, a, s1, op, s2=None, op1=None):
         if setup[0] and real(out, a) and (op, op1) in ((A.mult, A.add), (A.mult, None), (A.add, None)):
-            act(out, a, AF.Identity, scale=s1 if op == A.mult else 1.0, bias=s1 if op == A.add else s2 or 0.0)
-        elif op1 is None:
-            C("v", "tensor_scalar", out=out, in0=a, scalar1=s1, scalar2=None, op0=op)
-        else:
-            C("v", "tensor_scalar", out=out, in0=a, scalar1=s1, scalar2=s2, op0=op, op1=op1)
+            return act(out, a, AF.Identity, scale=s1 if op == A.mult else 1.0, bias=s1 if op == A.add else s2 or 0.0)
+        if op1 is None:
+            return C("v", "tensor_scalar", out=out, in0=a, scalar1=s1, scalar2=None, op0=op)
+        return C("v", "tensor_scalar", out=out, in0=a, scalar1=s1, scalar2=s2, op0=op, op1=op1)
 
     def mm(out, lhsT, rhs, start=True, stop=True):
-        C("p", "matmul", out=out, lhsT=lhsT, rhs=rhs, start=start, stop=stop)
+        return C("p", "matmul", out=out, lhsT=lhsT, rhs=rhs, start=start, stop=stop)
+
+    def scan(out, d0, d1, op):
+        return C("v", "scan", out=out, data0=d0, data1=d1, initial=0.0, op0=A.mult, op1=op)
 
     def fill(x, c):
-        if setup[0]:
-            act(x, cols("rr", 0, x[2][1].stop - x[2][1].start), AF.Identity, scale=0.0, bias=c)
-        else:
-            C("v", "memset", ap=x, constant=c)
+        iota(x, [[0, size(x)[0]]], c, 0)
+
+    def keep(out, in_, op, base, ch, pattern, other=0.0):
+        C("g", "affine_select", out=out, in_=in_, pattern=pattern, compare_op=op, fill=other, base=base, channel_multiplier=ch)
 
     def iota(out, pattern, base, ch):
         if SCRATCH[out[1]][2] == "int32":
@@ -437,467 +478,507 @@ def rank_main(g, core, rank, T, topo):
         else:
             C("g", "iota", out=out, pattern=pattern, base=base, channel_multiplier=ch, allow_small_or_imprecise_dtypes=True)
 
-    def by_group(pairs, dst, sem, late, after=(), local="lsem"):
+    def by_group(src, land, dst, sem, late, after=()):
         eng = singles(core, dst, T, topo)
-        mine = [fused([(blk(src, k), [(dst_id(topo, dst[k]), blk(land, k))], [eng[k]], sem) for k in range(NG)], late, after, local)
-                for src, land in pairs]
-        return arrive([v(land) for src, land in pairs], sem, len(pairs) * NG, mine)
+        mine = fused([(blk(src, k), [(dst_id(topo, dst[k]), blk(land, k))], [eng[k]], sem) for k in range(NG)], late, after)
+        arrive([v(land)], sem, NG, [mine])
+        return mine
 
-    told = sum(len(far_engines(c, T, topo)) if off_chip(topo, c, core) else len(near_engines(c, core, T, topo)) for c in T.cores if c != core)
+    far = far_engines(core, T, topo)
 
-    def tell(src, width, land, sem, after=(), more=0):
-        far = [c for c in T.cores if off_chip(topo, core, c)]
-        near = [c for c in T.cores if c != core and not off_chip(topo, core, c)]
-        tr = []
-        for ds, en in ((far, far_engines(core, T, topo)), (near, near_engines(core, near[0], T, topo) if near else [])):
-            if ds:
-                tr.append((src, [(dst_id(topo, d), cols(land, width * rank, width * rank + width)) for d in ds], en, sem))
-        mine = fused(tr, TELL + more, after)
-        return mine, arrive([cols(land, width * r, width * r + width) for r in range(N) if r != rank], sem, told, [mine])
+    def tell(src, land, sem, after=()):
+        away = [c for c in T.cores if off_chip(topo, core, c)]
+        near = [c for c in T.cores if c != core and c not in away]
+        mine = fused([(src, [(dst_id(topo, d), cols(land, 16 * rank, 16 * rank + 16)) for d in ds], en, sem)
+                      for ds, en in ((away, far), (near, near_engines(core, near[0], T, topo)))], TELL, after)
+        told = sum(len(far) if c in away else len(near_engines(c, core, T, topo)) for c in away + near)
+        return arrive([cols(land, 16 * r, 16 * r + 16) for r in range(N) if r != rank], sem, told, [mine])
 
     to_asked = lambda t: [T.cores[asked(rank, k, t)] for k in range(NG)]
     to_asker = lambda t: [T.cores[asker(rank, k, t)] for k in range(NG)]
+    half = lambda name, h: cols(name, 128 * h, 128 * h + 128)
 
-    first = [dma("y", v("ed0"), v("ef", ALL, slice(0, NL)), 2400),
-             dma("s", v("zd0"), v("zf", ALL, slice(0, NL)), 2000),
-             dma("s", cols("z_s", 64, 320), v("zf", ALL, slice(0, NL))),
-             dma("y", cols("eh_s", 64, 320), v("eh", ALL, slice(0, NL)))]
-    table = dma("y", cols("tb", 0, NS), v("tab"), 6000)
+    dma("y", v("ed0"), v("ef", ALL, slice(0, NL)), 1800)
+    dma("s", v("zd0"), v("zf", ALL, slice(0, NL)))
+    dma("s", cols("z_s", 64, 320), v("zf", ALL, slice(0, NL)), 2000)
+    dma("y", cols("eh_s", 64, 320), v("eh", ALL, slice(0, NL)), 2200)
+    dma("y", cols("tb", 0, NS), v("tab"), LOAD)
 
     iota(v("pi"), [[0, 8]], 0, 1)
     iota(v("rr"), [[1, NL]], 0, 0)
-    iota(v("r16"), [[1, 8], [0, 16]], 0, 0)
-    iota(v("m16"), [[0, 16], [1, 16]], 0, 0)
-    by_group((("zd0", "zl0"),), to_asked(0), "a_z0", ASKZ)
-    sent["q0"] = by_group((("ed0", "rl0"),), to_asked(0), "a_q0", ASK0) - 1
+    by_group("zd0", "zl0", to_asked(0), "a_z0", ASKZ)
+    sent["q0"] = by_group("ed0", "rl0", to_asked(0), "a_q0", ASK0)
+    iota(v("each"), [[1, 32], [0, 16]], 0, 0)
 
-    lazy = F["lazy"]
-    lazy[0] = True
-    PC = {n: cols("pc", k, k + 1) for k, n in enumerate(
-        "p a g ck m0 m1 m2 m3 m01 c15 half wq ewc erc w3 w6 x y".split())}
+    PC = {n: cols("pc", k, k + 1) for k, n in enumerate("p a g ck y nu v0 v1 b3 ia l c15 m0 m1 m2 m3 m01 m80".split())}
     pint = cols("pi", 0, 1)
 
-    def bitcol(out, sh, mask):
-        ts(cols("qi", 0, 1), pint, sh, A.arith_shift_right, mask, A.bitwise_and)
-        copy("v", out, cols("qi", 0, 1))
+    def bitcol(out, sh, mask, k):
+        ts(cols("hki", k, k + 1), pint, sh, A.arith_shift_right, mask, A.bitwise_and)
+        copy("v", out, cols("hki", k, k + 1))
 
+    lazy[0] = True
     copy("v", PC["p"], pint)
-    bitcol(PC["a"], 0, 15)
-    bitcol(PC["g"], 4, 7)
+    bitcol(PC["a"], 0, 15, 0)
+    bitcol(PC["g"], 4, 7, 1)
     ts(PC["ck"], PC["a"], -8192.0, A.mult, 122880.0, A.add)
-    r128, r144 = cols("rr", 0, 128), cols("rr", 0, 144)
-    ts(v("id32"), r128, PC["p"], A.is_equal)
-    ts(v("idb"), r128, PC["p"], A.is_equal)
-    ts(v("idn"), r128, PC["p"], A.is_equal, -1.0, A.mult)
+    C("v", "memset", ap=v("ob"), constant=1.0)
+    C("v", "memset", ap=v("zb"), constant=0.0)
+    ts(v("id32"), cols("rr", 0, 128), PC["p"], A.is_equal)
+    ts(v("idb"), cols("rr", 0, 128), PC["p"], A.is_equal)
     for x, w in enumerate((1.0, 0.5, 131072.0, 65536.0)):
         ts(cols("blk", 8 * x, 8 * x + 8), cols("rr", 0, 8), PC["g"], A.is_equal, w, A.mult)
-    fill(v("ob"), 1.0)
-    setup[0] = True
-    fill(cols("mid", 0, 128), 8.0)
-    fill(cols("mid", 128, NL), 8.0 * 131072)
-    ts(v("xp"), cols("eh_s", 64, 320), PC["ck"], A.add)
-    copy("v", v("offh"), cols("eh_s", 64, 320))
-    ts(v("rst"), v("m16"), 0.0, A.not_equal)
+    bitcol(PC["l"], 0, 31, 4)
+    ts(v("each"), v("each"), PC["l"], A.is_equal, -1.0, A.mult)
+    ts(v("xp0"), cols("eh_s", 64, 320), PC["ck"], A.add)
+    copy("v", v("oh0"), cols("eh_s", 64, 320))
+    fill(cols("mid", 128, NL), 8 * 131072)
+    fill(cols("mid", 0, 128), 8)
 
-    def zrep(q, tab, a, b, src=None):
-        for k in range(16):
-            copy(q, cols("zr" + tab, 16 * a + k, 16 * b, 16), src or cols("zl" + tab, a, b))
-
-    def look(q, tab, a, b, width=DUMP, src=None, part=0, table="tb", whose=None):
-        n, h, p0 = b - a, a // 128, a % 128
-        whose = whose or tab
-        z = src or cols("zl" + whose, a, b)
-        base = (KH if tab == "h" else KF) + 128 * h
-        out = lambda x, y, step=None: v("psb", slice(p0, p0 + n), slice(base + x, base + y, step))
-        got = ind(cols(table, 0, width), cols("off" + tab, a, b))
-        lhs = lambda k: cols("cm" + tab, 16 * a + k, 16 * b, 16)
-        if q == "b":
-            bank = 512 * (turn[0] % 4)
-            turn[0] += 1
-            mm(ps(bank, bank + n), v("idb"), z)
-            for k in range(16):
-                tt(lhs(k), cols("gt" + tab, 16 * a + k, 16 * b, 16), ps(bank, bank + n), A.is_le)
-            return
-        if q == "v":
-            for x in range(a, b, PIECE) if part != 2 else ():
-                y = min(b, x + PIECE)
-                tt(cols("cm" + tab, 16 * x, 16 * y), ind(cols(table, 0, width), cols("off" + tab, x, y)), cols("zr" + whose, 16 * x, 16 * y), A.is_le)
-            if part == 1:
-                return
-        else:
-            if part != 2:
-                act(cols("gt" + tab, 16 * a, 16 * b), got)
-            if part == 1:
-                return
-            per = 512 // n
-            for k0 in range(0, 16, per):
-                bank = 512 * (turn[0] % 4)
-                turn[0] += 1
-                for k in range(k0, k0 + per):
-                    o = ps(bank + n * (k - k0), bank + n * (k - k0 + 1))
-                    mm(o, v("idn"), z, True, False)
-                    mm(o, v("idb"), cols("gt" + tab, 16 * a + k, 16 * b, 16), False, True)
-                act(cols("cm" + tab, 16 * a + n * k0, 16 * a + n * (k0 + per)), ps(bank, bank + 512), AF.Sign, scale=-1.0, bias=0.5)
-            lhs = lambda k: cols("cm" + tab, 16 * a + n * k, 16 * a + n * (k + 1))
-
-        first = tab == "f" and q == "v"
-        if tab == "h":
-            mm(out(0, 128), cols("xp", a, b), v("id32"), True, False)
-        if q == "s":
-            mm(out(0, 128), rows("ob", 1, 0, n), rows("mid", 1, 128, NL) if tab == "h" else rows("mid", 1, 0, 128), tab == "f", False)
-        w = 8 * ("fv", "fs", "hv", "hs").index(tab + q)
-        for k in range(16):
-            mm(out(k, 128, 16), lhs(k), cols("blk", w, w + 8), first, first or k == 15)
-
-    lane = lambda name, h, x=ALL: v(name, ALL, slice(8 * h, 8 * h + 8), x)
+    def lookups(t, plan=None):
+        plan = (plan or PLAN[t]).split()
+        y0 = (64, 0, 704)[t]
+        begun = set()
+        for at, x in enumerate(plan):
+            what = x.split(":")
+            if what[0] in STAGE:
+                STAGE[what[0]](t, *[int(y) for y in what[1:]])
+                continue
+            kind, tab, a, b = x[0], x[1], int(what[1]), int(what[2])
+            n, h, p0 = b - a, a // 128, a % 128
+            if t == 0:
+                z = cols("z_s", 64 + a, 64 + b) if tab == "h" else cols("zlf", a, b)
+            else:
+                z = cols("zl%d" % t, a, b) if b > FIX else cols("z_s", y0 + a, y0 + b)
+            zr, zt = ("zrf", "ztf") if t == 0 and tab == "f" else ("zrh", "zt%d" % t)
+            got = lambda x, y: ind(cols("tb" if tab == "h" or t == 0 else "tf%d" % t, 0, DUMP if t else NS), cols("o%s%d" % (tab, t), x, y))
+            if kind == "z":
+                for k in range(16):
+                    copy(what[3], cols(zr, 16 * a + k, 16 * b, 16), z)
+            elif kind == "v":
+                tt(cols("cv" + tab, 16 * a, 16 * b), got(a, b), cols(zr, 16 * a, 16 * b), A.is_le)
+            elif kind == "g":
+                act(cols("gt" + tab, 16 * a, 16 * b), got(a, b))
+            elif kind == "s":
+                for x in range(a, b, 32):
+                    bk, part = bank(), slice(x % 128, x % 128 + 32)
+                    mm(ps(bk, bk + 512), v(zt, part, slice(128 * h, 128 * h + 128)), v("each", part, ALL), True, False)
+                    mm(ps(bk, bk + 512), v("idb"), cols("gt" + tab, 16 * x, 16 * x + 512), False, True)
+                    act(cols("cv" + tab, 16 * x, 16 * x + 512), ps(bk, bk + 512), AF.Sign, scale=-1.0, bias=0.5)
+            elif kind == "t":
+                bk = bank()
+                out = v("psb", slice(p0, p0 + n), slice(bk, bk + 128))
+                mm(out, z, v("idb"))
+                copy(what[3], v(zt, slice(p0, p0 + n), slice(128 * h, 128 * h + 128)), out)
+            else:
+                wide = tab == "f" and t > 0
+                base, step = (KF[h], 17) if wide else ((KH if tab == "h" else KF[0]) + 128 * h, 16)
+                out = lambda x, y, s=None: v("psb", slice(p0, p0 + n), slice(base + x, base + y, s))
+                start = tab == "f" or not begun
+                later = [[int(z) % 128 for z in y.split(":")[1:3]] for y in plan[at + 1:] if y[:2] == "mh"]
+                stop = tab == "f" or not any(c < p0 + n and p0 < (d or 128) for c, d in later)
+                if tab == "h" and h not in begun:
+                    begun.add(h)
+                    mm(ps(base, base + 128), half("xp%d" % t, h), v("id32"), start, False)
+                    start = False
+                if what[3] == "s":
+                    mm(out(0, 8 * step), rows("ob", 1, 0, n),
+                       rows("md2", 1, 0, 136) if wide else rows("mid", 1, 128, NL) if tab == "h" else rows("mid", 1, 0, 128), start, False)
+                    start = False
+                w = 8 * ("fv", "fs", "hv", "hs").index(tab + what[3])
+                for k in range(16):
+                    mm(out(k, 8 * step, step), cols("cv" + tab, 16 * a + k, 16 * b, 16), cols("blk", w, w + 8), start and k == 0, stop and k == 15)
 
     def choose(t):
-        C("v", "scan", out=v("kh"), data0=v("rst"), data1=ps(KH, KH + NL), initial=0.0, op0=A.mult, op1=A.max)
+        scan(v("kh"), v("rst"), ps(KH, KH + NL), A.max)
         copy("v", v("hki"), cols("kh", 15, NL, 16))
-        ts(v("di", ALL, ALL, 0), v("hki"), 6, A.arith_shift_right, 63, A.bitwise_and)
+        ts(v("di", ALL, ALL, 0), v("hki"), NS - 64, A.bitwise_and)
         ts(v("di", ALL, ALL, 1), v("hki"), 63, A.bitwise_and)
+        ts(v("di", ALL, ALL, 3), v("hki"), 17, A.arith_shift_right)
         copy("v", v("cd"), v("di"))
         for h in range(2):
-            mm(ps(P7 + 128 * h, P7 + 128 * h + 128, 16), lane("cd", h), v("idb"))
-        act(rows("st", 16, 0, NL), ps(P7, P7 + NL, 16))
-        ts(v("sli"), v("hki"), NS - 1, A.bitwise_and)
-        ts(v("nsl"), v("sli"), -1.0, A.mult)
-        ts(v("whi"), v("hki"), 17, A.arith_shift_right)
-        tt(v("sd"), v("cd"), v("dd", ALL, slice(16 * t, 16 * t + 16), ALL), A.subtract)
-        sent["c%d" % t] = F["last"]()
+            mm(ps(KH + 128 * h, KH + 128 * h + 128, 32), v("cd", ALL, slice(8 * h, 8 * h + 8), ALL), v("idb"))
 
-    def alike(t, ks=range(NG)):
-        for k in ks:
-            if k % 2 == 0:
-                turn[0] += 1
-            a = 512 * (turn[0] % 4) + NL * (k % 2)
-            mm(ps(a, a + NL), rows("sg", 16, 128 * k, 128 * k + 128), rows("st", 16, 0, NL))
+    def chosen(t):
+        copy("v", rows("st", 32, 0, NL), ps(KH, KH + NL, 32))
+        for h in range(2):
+            mm(ps(OWN + 8 * h, OWN + 8 * h + 8), rows("st", 32, 128 * h, 128 * h + 128), v("osr", slice(0, 32), ALL, 0))
+        if ON_SCALAR[t]:
+            copy("v" if t else "s", v("own"), ps(OWN, OWN + 16))
+        sent["c%d" % t] = F["last"]()
+        if t == 0:
             for h in range(2):
-                out, own = v("eq", ALL, k, slice(NL * h, NL + 128 * h)), cols("nsl", 8 * h + k, 8 * h + k + 1)
-                if k in ON_SCALAR:
-                    act(cols("gtf", 384 * k + NL * h, 384 * k + NL + 128 * h), ps(a + 128 * h, a + NL), AF.Abs, bias=own)
+                mm(ps(R + 128 * h, R + 128 * h + 128), rows("st", 32, 128 * h, 128 * h + 128), rows("wsel", 32, 0, 128))
+            act(v("whr"), ps(R, R + NL))
+
+    def alike(t, first=0, end=NG):
+        for k in range(first, end):
+            a, sg = bank() if k in ON_SCALAR[t] else B[4 + k % 2], v("sg", slice(0, 32), k, ALL)
+            mm(ps(a + 128, a + 384), sg, rows("st", 32, 0, NL), True, False)
+            mm(ps(a, a + 128), sg, rows("st", 32, 128, NL), False, False)
+            mm(ps(a, a + NL), v("i8k"), v("uu2"), False, True)
+            for h, x, y in ((1, 0, 128), (0, 128, 384)):
+                own = cols("own", 8 * h + k, 8 * h + k + 1) if ON_SCALAR[t] else ps(OWN + 8 * h + k, OWN + 8 * h + k + 1)
+                if k in ON_SCALAR[t]:
+                    act(cols("gtf", 384 * k + x, 384 * k + y), ps(a + x, a + y), AF.Abs, scale=-1.0, bias=own)
                 else:
-                    ts(out, ps(a + 128 * h, a + NL), own, A.add, 0.0, A.is_equal)
-            if k in ON_SCALAR:
-                act(v("eq", ALL, k, ALL), cols("gtf", 384 * k, 384 * k + 384), AF.Relu, scale=-1.0, bias=1.0)
-        turn[0] += 1
+                    ts(v("eq", ALL, k, slice(x, y)), ps(a + x, a + y), own, A.is_equal, BIG, A.mult)
+            if k in ON_SCALAR[t]:
+                act(v("eq", ALL, k, ALL), cols("gtf", 384 * k, 384 * k + 384), AF.Relu, scale=-BIG, bias=BIG)
         sent["g%d" % t] = F["last"]()
 
     def answer(t):
-        C("v", "scan", out=v("kf"), data0=v("rst"), data1=ps(KF, KF + NL), initial=0.0, op0=A.mult, op1=A.max)
-        copy("v", cols("wq", 16 * t, 16 * t + 16), cols("kf", 15, NL, 16))
-        sent["a%d" % t] = F["last"]()
-        sent["r%d" % t] = tell(cols("wq", 16 * t, 16 * t + 16), 16, "lr%d" % t, "a_r%d" % t)
+        scan(v("kf"), v("rst"), ps(KF[0], KF[0] + NL), A.max)
+        sent["a0"] = copy("v", v("wq"), cols("kf", 15, NL, 16))
+        sent["r0"] = tell(v("wq"), "lr0", "a_r0")
 
-    def decide(t, lists):
-        mm(ps(P6, P6 + 16), v("idb"), v("li"), True, False)
-        tt(v("wm"), ind(v("lr%d" % t), cols("lst", 2 * t, 2 * t + 1)), v("whi"), A.max)
-        ts(v("gw"), v("wm"), 8.0, A.is_lt, PC["w3"], A.mult)
-        ts(cols("gb", 0, 8), cols("wm", 0, 8), 8.0, A.is_lt, TOP, A.mult)
-        ts(v("thr"), v("wm"), 8.0, A.is_lt, PC["w6"], A.mult)
-        ts(v("ng"), v("wm"), 8.0, A.is_ge)
-        for c, j, i, w in ((0, 0, 0, "gw"), (128, 0, 1, "gb"), (256, 1, 1, "gw")):
-            for k in range(NG):
-                a, b = KF + 8 * i + k, 8 * j + k
-                mm(ps(a, a + 1), v("eq", ALL, k, slice(c, c + 128)), cols(w, b, b + 1), c + k == 0, c + k == 256 + NG - 1)
-        win = v("ttl", ALL, ALL, slice(16, 24))
-        tt(v("ttl", ALL, ALL, slice(24, 32)), v("wm"), v("ng"), A.mult)
-        tt(win, ps(KF, KF + 16), v("thr"), A.is_lt)
-        for x in range(2):
-            tt(v("ttl", ALL, ALL, slice(x, 16, 2)), v("sd", ALL, ALL, x), win, A.mult)
-        for h in range(2):
-            mm(ps(P7 + 128 * h, P7 + 128 * h + 128, 32), v("ttl", ALL, h, ALL), v("idb"))
-        copy("v", rows("t1", 32, 0, NL), ps(P7, P7 + NL, 32))
-        if t == 1 and OCC == "t1":
-            gate[:] = [F["last"]()]
-            scatter("occ", "w0", cols("idf", 64, 320))
-            gate[:] = []
-        for i in range(16):
-            mm(ps(P6, P6 + 16), rows("ew", 32, 15 - i, 143 - i), rows("t1", 32, i, NL, 16), False, i == 15)
-        mm(row, rows("er", 32, 0, 128), rows("t1", 32, 0, NL), True, t > 0)
+    known_ = set()
+
+    def fin(t, h):
         if t == 0:
-            mm(row, v("idb"), cols("pay", 64, 320), False, True)
-            act(cols("pay", 64, 320), row)
+            w = half("wr0", h)
+            tt(w, ind(v("lr0"), cols("lrep", 8 * h, 8 * h + 8)), half("whr", h), A.max)
         else:
-            ts(cols(lists, 0, 16), ps(P6, P6 + 16), float(DUMP + NL * t), A.add)
+            mm(ps(KF[h] + 16, KF[h] + 136, 128, 17), v("idb"), v("cd", ALL, slice(8 * h, 8 * h + 8), 3))
+            scan(cols("kf%d" % h, 0, 136), cols("rs2", 0, 136), ps(KF[h], KF[h] + 136), A.max)
+            w = ind(cols("kf%d" % h, 0, 136), cols("lrep", 16, 24))
+        ts(half("cl", h), w, 8.0, A.is_lt)
+        act(half("rl", h), w, AF.Relu, bias=-8.0)
+        mm(ps(PS[h], PS[h] + 128), rows("st", 32, 128 * h, 128 * h + 128), rows("rsel", 32, 0, 128), True, False)
+        known_.add((t, h))
+        other = (t, 1 - h) in known_
+        todo = ([(128, 0, 0)] if h == 0 else []) + ([(256, 0, 1)] if other else []) + ([(0, 1, 1)] if h == 1 else [])
+        for at, (c, j, i) in enumerate(todo):
+            if i == j:
+                mm(ps(PS[i], PS[i] + 128), v("i8k"), half("cl", i), False, False)
+            for k in range(NG):
+                mm(ps(PS[i] + 16 * k, PS[i] + 16 * k + 16), v("eq", ALL, k, slice(c, c + 128)), cols("cl", 128 * j + 16 * k, 128 * j + 16 * k + 16),
+                   False, k == NG - 1 and (i == 0 or (other and at == len(todo) - 1)))
+
+    def scatter(table, lists, vals):
+        return copy("v", ind(v(table), cols(lists, 0, 16)), vals)
+
+    def wrap(table, q="s"):
+        copy(q, cols(table, NS, DUMP), cols(table, 0, WR))
+
+    def renew(table, lu, la, pick, vals):
+        copy("v", v(lu), ind(v(la), cols("lst", pick, pick + 1)))
+        scatter(table, lu, v(vals))
+
+    def update(t):
+        if t == 1:
+            renew("tf1", "lu1", "la0", 0, "zu1")
+        else:
+            renew("tf2", "lu3", "la1", 2, "zu3")
+        wrap("tf%d" % t, "v")
+
+    STAGE = {"choose": choose, "chosen": chosen, "alike": alike, "answer": answer, "fin": fin, "update": update}
+
+    def growth(t):
+        mm(ps(R, R + NL), rows("mid", 1, 0, 128), rows("ob", 1, 0, NL), True, False)
+        for h in range(2):
+            o = ps(R + 128 * h, R + 128 * h + 128)
+            mm(o, half("rl", h), v("idb"), False, False)
+            mm(o, half("cl", h), v("i8n"), False, t != 1 and h == 1)
+
+    def decide(t):
+        for h in range(2):
+            tt(half("xx", h), ps(PS[h], PS[h] + 128), cols("dm", NL * t + 128 * h, NL * t + 128 * h + 128), A.min)
+            mm(ps(LW + 8 * h, LW + 8 * h + 8), half("xx", h), v("sel"))
+            if t == 0:
+                act(half("sgn", h), ps(PS[h], PS[h] + 128), AF.Sign, bias=-6000.0)
+            if t == 1:
+                act(v("ut", ALL, slice(8 * h, 8 * h + 8), 3), ps(PS[h], PS[h] + 128, 128, 16), AF.Sign, bias=-6000.0)
+                mm(ps(R + 128 * h, R + 128 * h + 128), v("ut", ALL, slice(8 * h, 8 * h + 8), ALL), v("i8k"), False, h == 1)
+        copy("v", cols("w%d" % t, 0, 16), ps(LW, LW + 16))
+
+    def report(t):
+        act(cols("msg", 16 * t, 16 * t + 16), ps(LW, LW + 16))
+        sent["u%d" % t] = tell(cols("msg", 16 * t, 16 * t + 16), "la%d" % t, "a_u%d" % t)
 
     def wrapped(a, n, el, src, first, start=True, stop=True):
         for i in range(16):
             mm(ps(a, a + n), cols(el, 15 - i, 143 - i), cols(src, first + i, first + 16 * n, 16), start and i == 0, stop and i == 15)
 
-    def scatter(table, lists, vals):
-        copy("v", ind(v(table), cols(lists, 0, 16)), vals)
-
-    def wrap(table="tb"):
-        copy("v", cols(table, NS, DUMP), cols(table, 0, WR))
-
-    ts(cols("pc", 4, 8), cols("rr", 0, 4), PC["a"], A.is_equal)
-    ts(PC["m01"], PC["a"], 2.0, A.is_lt)
-    ts(PC["c15"], PC["g"], 16.0, A.mult, 15.0, A.add)
-    for name, m in (("el", "m01"), ("el2", "m2"), ("el3", "m3"), ("eln", "m0")):
-        ts(v(name), r144, PC["c15"], A.is_equal, PC[m], A.mult)
-    ts(v("eln"), v("eln"), -1.0, A.mult)
-    bitcol(PC["half"], 1, 63)
-    bitcol(PC["x"], 0, 1)
-    ts(PC["wq"], PC["x"], -63.0, A.mult, 64.0, A.add)
-    ts(PC["x"], PC["p"], 16.0, A.is_lt)
-    tt(PC["wq"], PC["wq"], PC["x"], A.mult)
-    ts(PC["ewc"], PC["half"], 16.0, A.mult, 15.0, A.add)
-    ts(v("ew"), r144, PC["ewc"], A.is_equal, PC["wq"], A.mult)
-    ts(cols("tmp", 0, 8), cols("rr", 0, 8), PC["half"], A.is_equal, PC["wq"], A.mult)
-    for k in range(NG):
-        ts(rows("sg", 16, 128 * k, 128 * k + 128), rows("ob", 16, 0, 128), rows("tmp", 16, k, k + 1), A.mult)
-    ts(PC["x"], PC["p"], 24.0, A.is_ge, -129.0, A.mult)
-    ts(PC["erc"], PC["p"], 16.0, A.mult, -253.0, A.add)
-    tt(PC["erc"], PC["erc"], PC["x"], A.add)
-    ts(v("er"), r128, PC["erc"], A.is_equal)
-    ts(v("onb"), v("r16"), PC["g"], A.is_equal)
-    ts(v("ex2"), v("onb"), PC["m2"], A.mult)
-    ts(v("mk2"), v("idb"), PC["m2"], A.mult)
-    ts(v("ntr"), r128, PC["p"], A.is_lt, -1.0, A.mult)
-    tt(v("ntr"), v("ntr"), v("onb"), A.mult)
-    ts(v("onb1"), cols("m16", 0, 128), 1.0, A.is_equal, -1.0, A.mult)
-    tt(v("onb1"), v("onb1"), v("onb"), A.mult)
-    fill(cols("xq", 0, 128), 1.0 / 3)
-    fill(cols("xq", 128, NL), 0.0)
-    C("v", "scan", out=cols("dq", 0, 128), data0=cols("xq", 0, 128), data1=cols("xq", 128, NL), initial=TOP, op0=A.mult, op1=A.add)
-    tt(cols("dq", 128, NL), cols("dq", 0, 128), v("id32"), A.mult)
-    C("v", "tensor_reduce", out=PC["w3"], in_=cols("dq", 128, NL), axis=AxisListType.X, op=A.add)
-    ts(PC["w6"], PC["w3"], 2.0, A.mult)
-    iota(v("dd", ALL, ALL, 0), [[2, 6], [0, 8]], 64, 0)
-    ts(v("dd", ALL, ALL, 1), cols("ob", 0, 48), PC["p"], A.mult, 32.0, A.add)
-    ts(v("yw"), cols("rr", 0, 48), 16.0, A.mult, PC["a"], A.add)
-    copy("v", v("li"), cols("yw", 0, 16))
-    ts(v("yc"), v("yw"), 600.0, A.add)
-    copy("v", cols("inv1", 0, 4), cols("yw", 0, 4))
+    one, zero = half("ob", 0), half("zb", 0)
+    line, by16, in16 = lambda s, n=128: [[s, n]], lambda s, n=8: [[s, n], [0, 16]], lambda n=8: [[0, n], [1, 16]]
+    keep(v("rst"), v("ob"), A.not_equal, 0, 0, in16(16))
+    iota(v("di", ALL, ALL, 2), [[0, 16]], int(BIG), 0)
+    keep(v("rsel"), one, A.is_ge, 0, 1, by16(-4))
+    keep(v("rsel"), v("rsel"), A.is_ge, 2, -1, by16(4))
+    keep(v("osr"), v("rsel"), A.not_equal, -2, 1, by16(-4))
+    for k in range(8):
+        dma("s", v("sg", slice(0, 32), ALL, slice(16 * k, 16 * k + 16)), v("osr", slice(0, 32), ALL, ALL))
+    keep(v("wsel"), one, A.is_equal, -3, 1, by16(-4))
+    for name, c in (("i8k", -BIG), ("i8n", -8.0), ("idn", -1.0)):
+        keep(v(name), zero, A.not_equal, 0, 1, line(-1), c)
+    keep(v("uu2"), v("ob"), A.is_ge, 0, 1, [[0, 2], [-1, 128]])
+    ts(v("sel"), cols("rr", 0, 8), PC["g"], A.is_equal)
+    keep(v("tri2"), zero, A.is_ge, 0, 1, line(-1), 0.5)
+    keep(v("tri"), zero, A.is_ge, 0, 1, line(-1), 1.0 / 32)
+    keep(v("tri"), v("tri"), A.not_equal, 0, 1, line(-1), -1.0 / 64)
+    keep(v("o32"), zero, A.is_gt, 0, 0, line(0), 1.0 / 32)
+    keep(v("o2"), zero, A.is_gt, 0, 0, line(0), 0.5)
+    iota(v("crow"), [[128, 2], [0, 8], [-2, 16]], 1, 0)
+    iota(v("crow2"), [[64, 2], [0, 8], [-16, 16]], -8, 0)
+    iota(cols("pc", 6, 8), [[-128, 2]], 256, -1)
+    iota(cols("tmp", 0, 6), [[128, 6]], DUMP, 1)
+    iota(v("m16"), in16(16), 0, 0)
+    ts(PC["b3"], PC["a"], 3.0, A.is_equal, BIG, A.mult)
+    ts(PC["ia"], PC["a"], 16.0, A.mult, 72.0, A.add)
+    ts(v("m16"), v("m16"), PC["a"], A.is_equal)
+    for x in range(6):
+        act(cols("dm", 128 * x, 128 * x + 128), half("m16", 0), AF.Identity, scale=cols("tmp", x, x + 1))
+    fill(v("apad", ALL, ALL, 1, ALL), 0)
+    for a, b, c in ((0, 48, 0), (48, 80, 600), (80, 96, DUMP)):
+        iota(cols("yw", a, b), line(16, b - a), c, 0)
+    act(v("yw"), v("yw"), AF.Identity, bias=PC["a"])
     copy("v", cols("w1", 16, 20), cols("yw", 0, 4))
+    copy("v", cols("inv1", 0, 4), cols("yw", 0, 4))
     copy("v", cols("w2", 16, 20), cols("yw", 44, 48))
     copy("v", cols("inv2", 44, 48), cols("yw", 0, 4))
+    keep(cols("rs2", 0, 136), cols("ob", 0, 136), A.not_equal, 0, 0, [[0, 8], [1, 17]])
+    fill(cols("md2", 0, 136), 8)
+    keep(cols("md2", 0, 136), cols("md2", 0, 136), A.not_equal, -16, 0, [[0, 8], [1, 17]])
+    fill(v("ut"), 0)
+    keep(v("onb"), one, A.is_ge, 0, 1, by16(-16))
+    keep(v("onb"), v("onb"), A.is_ge, 15, -1, by16(16))
+    keep(v("onb1"), v("onb"), A.is_equal, -1, 0, in16())
+    keep(v("ntr"), zero, A.is_ge, 0, -1, line(1), -1.0)
+    keep(v("ntr"), v("ntr"), A.is_ge, 15, -1, by16(16))
+    keep(v("ex2"), one, A.is_equal, -2, 1, by16(-16))
+    ts(cols("pc", 12, 16), cols("rr", 0, 4), PC["a"], A.is_equal)
+    ts(PC["m01"], PC["a"], 2.0, A.is_lt)
+    ts(PC["c15"], PC["g"], 16.0, A.mult, 15.0, A.add)
+    ts(PC["m80"], PC["m0"], -80.0, A.mult)
+    for name, m in (("el", "m01"), ("el3", "m3"), ("eln", "m80")):
+        ts(v(name), cols("rr", 0, 144), PC["c15"], A.is_equal, PC[m], A.mult)
+    ts(v("mk2"), v("idb"), PC["m2"], A.mult)
+    ts(cols("pc", 20, 23), cols("rr", 0, 3), PC["m0"], A.mult, float(NL), A.mult)
     for x in range(3):
-        ts(PC["x"], PC["m0"], 256.0 * x, A.mult)
-        ts(cols("pay", 256 * x, 256 * x + 256), v("rr"), PC["m1"], A.mult, PC["x"], A.add)
-        if x == 2:
-            copy("v", v("pm2"), cols("pay", 512, NF))
-    ts(PC["x"], PC["m1"], 64.0, A.mult)
-    ts(v("pm1"), cols("pay", 256, 512), PC["x"], A.add)
-    ts(cols("hki", 0, 1), pint, 7, A.bitwise_and)
-    ts(cols("hki", 1, 2), pint, 4, A.arith_shift_right)
-    copy("v", cols("tmp", 8, 10), cols("hki", 0, 2))
-    ts(cols("hki", 0, 3), cols("rr", 0, 3), cols("tmp", 8, 9), A.add)
-    ts(cols("hki", 3, 5), cols("rr", 1, 3), cols("tmp", 9, 10), A.add)
-    ts(cols("hki", 8, 13), cols("hki", 0, 5), float(N - 1), A.is_ge, -float(N - 1), A.mult)
-    tt(cols("hki", 0, 5), cols("hki", 0, 5), cols("hki", 8, 13), A.add)
-    ts(cols("hki", 0, 3), cols("hki", 0, 3), float(rank + 1), A.add)
-    ts(cols("hki", 3, 5), cols("hki", 3, 5), -1.0, A.mult, float(rank + N - 1), A.add)
-    ts(cols("hki", 0, 5), cols("hki", 0, 5), N - 1, A.bitwise_and)
-    ts(cols("lst", 0, 6, 2), cols("hki", 0, 3), 16.0, A.mult, PC["a"], A.add)
-    ts(cols("lst", 6, 10, 2), cols("hki", 3, 5), 24.0, A.mult, PC["a"], A.add)
-    ts(cols("tmp", 8, 10), cols("hki", 3, 5), 24.0, A.mult)
-    for t in (1, 2):
-        ts(cols("lst", 12 * t - 2, 12 * t + 10), cols("rr", 12, 24), cols("tmp", 7 + t, 8 + t), A.add)
-    ts(v("m16"), v("m16"), PC["a"], A.is_equal)
-    for name, w in (("lr0", 16), ("lr1", 16), ("lr2", 16), ("la1", 24), ("la2", 24)):
-        fill(cols(name, w * rank, w * rank + w), 0.0)
-    for name in ("r1", "r2", "r3"):
-        fill(cols(name, NL, ZC), 0.0)
-    setup[0] = False
-
-    lazy[0] = False
-    dma("y", v("eda"), v("ef"), 3500, [table])
-    dma("y", v("zda"), v("zf"), 4000)
-    asks = [dma("y", v("zlf"), v("zl0")), dma("y", v("efq0"), v("rl0"))]
-    sent["b1"] = by_group((("eda", "rl1"), ("zda", "zl1")), to_asked(1), "a_b1", BULK) - 1
-    lazy[0] = True
-    for name, src in (("z_s", "zf"), ("eh_s", "eh")):
-        dma("y", cols(name, 320, NF), v(src, ALL, slice(NL, 704)), after=asks)
-        dma("y", cols(name, 0, 64), v(src, ALL, slice(704, NF)), after=asks)
-    for x, a in enumerate(range(0, NT, NT // 16)):
-        gate[:] = [sent["q0"] if x < EARLY else sent["b1"]]
-        iota(cols("occ", a, a + NT // 16), [[0, NT // 16]], -1, 0)
-    gate[:] = []
+        act(cols("pay", NL * x, NL * x + NL), v("rr"), AF.Identity, scale=PC["m1"], bias=cols("pc", 20 + x, 21 + x))
     for a, b, c in ((0, 64, 704.0), (64, 320, 0.0), (320, 576, 256.0), (576, NF, 512.0)):
         act(cols("idf", a, b), cols("rr", 0, b - a), AF.Identity, bias=c)
+    for h in range(2):
+        runs = [k for k in range(NG) if k == 0 or asked(rank, k, 0) != asked(rank, k - 1, 0) + 1] + [NG]
+        for a, b in zip(runs, runs[1:]):
+            iota(cols("ri", 8 * h + a, 8 * h + b), [[17, b - a]], 16 * asked(rank, a, 0) + 8 * h + a, 0)
+    iota(cols("ri", 16, 24), line(17, 8), 16, 0)
+    copy("v", cols("lrep", 0, 24), cols("ri", 0, 24))
+    ts(cols("hki", 0, 2), cols("rr", 1, 3), PC["g"], A.add)
+    ts(cols("hki", 8, 10), cols("hki", 0, 2), float(N - 1), A.is_ge, -float(N - 1), A.mult)
+    tt(cols("hki", 0, 2), cols("hki", 0, 2), cols("hki", 8, 10), A.add)
+    ts(cols("hki", 0, 2), cols("hki", 0, 2), float(rank + 1), A.add)
+    ts(cols("hki", 0, 2), cols("hki", 0, 2), N - 1, A.bitwise_and)
+    ts(cols("lst", 0, 4, 2), cols("hki", 0, 2), 16.0, A.mult, PC["a"], A.add)
+    for name in ("lr0", "la0", "la1"):
+        fill(cols(name, 16 * rank, 16 * rank + 16), 0)
+    for name in ("r1", "r2", "r3"):
+        fill(cols(name, NL, ZC), 0)
     lazy[0] = False
 
-    copy("v", v("offf"), v("efq0"))
-    for x in PLAN[0].split():
-        if x == "answer":
-            answer(0)
-            continue
-        what, a, b = x.split(":")
-        a, b = int(a), int(b)
-        src = cols("z_s", 64 + a, 64 + b) if what[1] == "h" else None
-        if what[0] == "z":
-            zrep(what[2], what[1], a, b, src)
-        else:
-            look(what[0], what[1], a, b, NS, src, int(what[2:] or 0))
-    by_group((("zda", "zl2"),), to_asked(2), "a_b2", BULK, [sent["r0"][0]])
-    choose(0)
-    alike(0)
-    dma("y", cols("eu1", 64, NF + 64), v("rl1"))
-    dma("y", cols("zq1", 64, NF + 64), v("zl1"))
-    decide(0, "w0")
+    senders, halves = helpers(core, T, topo)[0], carry_engines(core, T, topo)
 
-    def lanes(t, m0, m1, placed):
-        n = m1 - m0
-        L, pay, inv = "w%d" % t, "pay" if t == 1 else "pay2", "inv%d" % t
-        if t == 1:
-            ts(cols("uu", 0, n), placed, -0.5, A.is_ge)
-            ts(cols("dst", 0, n), placed, -0.5, A.is_lt)
-            tt(cols("vb", 0, n), cols("dst", 0, n), cols("yc", m0, m1), A.mult)
-        else:
-            ts(cols("uu", 0, n), placed, 0.5, A.is_lt)
-            tt(cols("vb", 0, n), placed, cols("yc", m0, m1), A.mult)
-        C("v", "scan", out=cols("scn", 0, n), data0=cols("ob", 0, n), data1=cols("uu", 0, n), initial=0.0, op0=A.mult, op1=A.add)
-        mm(ps(KH, KH + n), v("ntr"), cols("uu", 0, n), True, False)
-        mm(ps(KH, KH + n), v("onb"), cols("scn", 0, n), False, True)
-        mm(ps(KH + 64, KH + 65), v("onb1"), cols("scn", n - 1, n))
-        tt(cols("dst", 0, n), ps(KH, KH + n), cols("vb", 0, n), A.max)
-        ts(cols("dsu", 0, n), cols("dst", 0, n), 63.0, A.add)
-        ts(cols("nrow", FIX, NL), cols("pm%d" % t, 0, DYN), ps(KH + 64, KH + 65), A.add)
-        copy("v", ind(v("nrow"), cols("dsu", 0, n)), cols(pay, 16 * m0, 16 * m1))
-        packed = F["last"]()
-        wrapped(KF + 32, 12, "el", "nrow", FIX)
-        wrapped(KF + 44, 12, "el2", "nrow", FIX)
-        copy("v", cols("msg", 24 * t - 24, 24 * t), ps(KF + 32, KF + 56))
-        sent["m%d" % t] = F["last"]()
-        sent["q%d" % t] = tell(cols("msg", 24 * t - 24, 24 * t), 24, "la%d" % t, "a_q%d" % t)
-        mm(ps(KH + 65, KH + 66), v("onb"), cols("scn", n - 1, n))
-        mm(ps(KH + 128, KH + 128 + DYN), v("ex2"), cols("nrow", FIX, NL))
-        if t == 1 or not TB_EARLY:
-            gate[:] = [packed]
-            if t == 1:
-                ts(v("w0"), ps(P6, P6 + 16), float(DUMP), A.add)
-            scatter("tb", "w%d" % (t - 1), cols("z_s", 64, 320) if t == 1 else v("zlh"))
-            gate[:] = []
-            wrap()
-        copy("v", cols(L, 20, 32), ps(KF + 32, KF + 44))
-        if DC == "s":
-            act(cols("dc", FIX, NL), ps(KH + 128, KH + 128 + DYN), AF.Identity, bias=PC["ck"])
-        else:
-            ts(cols("dc", FIX, NL), ps(KH + 128, KH + 128 + DYN), PC["ck"], A.add)
-        act(PC["y"], ps(KH + 65, KH + 66), AF.Identity, bias=float(FIX - 16 * m1))
+    def carry(t, after=()):
+        for c in range(0, NCH, 2):
+            mine = fused([(cols("tb", CH * x, CH * x + CH), [(dst_id(topo, senders[x % 2]), blk("hc", NCH * (t - 1) + x))], halves[x % 2],
+                           "a_c%d" % (NCH * (t - 1) + x)) for x in (c, c + 1)], 4000, after if c == 2 else (), "ltab")
+        arrive([cols("tf%d" % t, 0, NS)], "a_f%d" % t, sum(len(topo.engines(joiner(rank, t, c, T, topo), core)) for c in range(NCH)), [mine], TABLE)
 
-    def way_back(t, m0, m1):
-        gate[:] = [sent[BACK % t]]
-        ts(cols("inv%d" % t, m0, m1), cols("dst", 0, m1 - m0), 63.0, A.add, float(NL), A.min)
-        ts(cols("inv%d" % t, m1, m1 + 12), cols("yw", m1, m1 + 12), PC["y"], A.add, float(NL), A.min)
-        gate[:] = []
-
-    def step(t):
-        sent["e%d" % t] = sent["m%d" % t]
-        L, la, zq, efq = "w%d" % t, "la%d" % t, "zq%d" % t, "eu%d" % t
-        f0 = NF if t == 1 else 704
-        y0 = 0 if t == 1 else 704
-        dyn = cols(L, 20, 32)
-        lazy[0] = True
-        gate[:] = [sent[BACK % (t - 1)]]
-        ts(cols("xp", 0, FIX), cols("eh_s", y0, y0 + FIX), PC["ck"], A.add)
-        copy("v", cols("offh", 0, FIX), cols("eh_s", y0, y0 + FIX))
-        copy("v", cols("offf", 0, FIX), cols(efq, f0, f0 + FIX))
-        gate[:] = []
-        if "vh:0:64" in PLAN[t] or "vh1:0:64" in PLAN[t]:
-            zrep("g", "h", 0, FIX, cols("z_s", y0, y0 + FIX))
-        if "vf:0:64" in PLAN[t] or "vf1:0:64" in PLAN[t]:
-            zrep("g", "f", 0, FIX, cols(zq, y0, y0 + FIX))
-        gate[:] = [sent["e%d" % t]]
-        copy("v", cols(efq, 0, 64), cols(efq, NF, NF + 64))
-        copy("s", cols(zq, 0, 64), cols(zq, NF, NF + 64))
-        gate[:] = []
-        lazy[0] = False
-        copy(ZLH, v("zlh"), ind(v("z_s"), cols(L, 16, 32)))
-        lanes_z = F["last"]()
-        held = [sent["a%d" % (t - 1)]]
-        tt(cols("xp", FIX, NL), ind(v("eh_s"), dyn), cols("dc", FIX, NL), A.add)
-        ts(cols("offh", FIX, NL), cols("xp", FIX, NL), PC["ck"], A.subtract)
-        sent["o%d" % t] = F["last"]()
-
-        for x in PLAN[t].split():
-            if x == "asks":
-                copy("v", v("lq"), ind(v(la), cols("lst", 4 + 2 * t, 5 + 2 * t)))
-                tt(cols("dm", 0, DYN), ind(v(la), cols("lst", 12 * t - 2, 12 * t + 10)), cols("m16", 0, DYN), A.mult)
-                mm(ps(P6 + 64, P6 + 64 + DYN), v("onb"), cols("dm", 0, DYN))
-                copy("v", cols("dq", 0, DYN), ind(v(efq), cols("lq", 0, 12)))
-                copy(ZLF, cols("zlf", FIX, NL), ind(v(zq), cols("lq", 0, 12)))
-                tt(cols("xq", 0, DYN), ps(P6 + 64, P6 + 64 + DYN), cols("dq", 0, DYN), A.add)
-                copy("v", cols("offf", FIX, NL), cols("xq", 0, DYN))
-            elif x == "answer":
-                answer(t)
-            elif x == "choose":
-                choose(t)
-            elif x == "alike":
-                alike(t)
-            else:
-                what, a, b = x.split(":")
-                a, b = int(a), int(b)
-                src = None if a else cols("z_s", y0, y0 + FIX) if what[1] == "h" else cols(zq, f0, f0 + FIX)
-                if what[0] == "z":
-                    zrep(what[2], what[1], a, b, src)
-                else:
-                    gate[:] = [lanes_z] if ZLH == "s" and (t == 1 or a) else []
-                    inline[:] = [held[0]] if STRICT else []
-                    look(what[0], what[1], a, b, src=src, part=int(what[2:] or 0))
-                    held[0] = inline[0] if STRICT else 0
-                    gate[:], inline[:] = [], []
-        gate[:] = [sent["a%d" % t]]
-        copy("s", v("lnf%d" % t), ind(v("idf"), cols(L, 16, 32)))
-        gate[:] = []
-
-    lanes(1, 4, 20, ps(P6, P6 + 16))
-    step(1)
-    way_back(1, 4, 20)
+    asks = [dma("y", v("zlf"), v("zl0")), dma("y", v("efq0"), v("rl0"))]
+    carry(1, asks[:1])
+    by_group("zd0", "zk1", to_asker(1), "a_zu", ASK0)
+    flights = (("ef_s", "ef", 0), ("eh_s", "eh", NL), ("z_s", "zf", NL))
+    for name, src, a in flights:
+        dma("y", cols(name, 0, 64), v(src, ALL, slice(704, NF)), after=asks)
     lazy[0] = True
-    if OCC != "t1":
-        gate[:] = [sent[OCC]]
-        scatter("occ", "w0", cols("idf", 64, 320))
-        gate[:] = []
-    wrapped(KH, 32, "el3", "pay", 0, True, False)
+    for a in range(0, NT, NT // 16):
+        fill(cols("occ", a, a + NT // 16), -1)
+
+    def known(t):
+        y0 = (64, 0, 704)[t]
+        ts(cols("xp%d" % t, 0, FIX), cols("eh_s", y0, y0 + FIX), PC["ck"], A.add)
+        copy("v", cols("oh%d" % t, 0, FIX), cols("eh_s", y0, y0 + FIX))
+        copy("v", cols("of%d" % t, 0, FIX), cols("ef_s", y0, y0 + FIX))
+        copy("s", cols("zl%d" % t, 0, FIX), cols("z_s", y0, y0 + FIX))
+        lookups(t, "th:0:64:s")
+
     lazy[0] = False
-    decide(1, "w1")
-    by_group((("eda", "rl2"),), to_asked(2), "a_b3", BULK, [sent["q1"][0]])
-    dma("y", cols("zq2", 64, NF + 64), v("zl2"), after=[sent["q1"][1]])
-    dma("y", cols("eu2", 64, NF + 64), v("rl2"), after=[sent["r1"][1]])
-    copy("s", cols("r1", 0, NL), row)
+    STAGE["asks"] = lambda t: copy("v", v("of0"), v("efq0"))
+    lookups(0)
+    for name, src, a in flights:
+        dma("y", cols(name, 64 + a, 512), v(src, ALL, slice(a, 448)), after=[sent["r0"]])
+    dma("y", v("zu1"), v("zk1"))
+    for name, src, a in flights:
+        dma("y", cols(name, 512, NF), v(src, ALL, slice(448, 704)))
+    lazy[0] = True
+    known(1)
+    lazy[0] = False
+    Y, Y2, M, CNT = B[4], B[5], PS[1] + 384, PS[0] + 384
+    for a, t, o, c in ((Y, "tri", "o32", "crow"), (Y2, "tri2", "ob", "crow2")):
+        mm(ps(a, a + NL), v(t), v("ob"), True, False)
+        mm(ps(a, a + NL), rows(o, 1, 0, 128), rows(c, 1, 0, NL), False, False)
+    for h in range(2):
+        fin(0, h)
+    growth(0)
+    act(v("d0r"), ps(R, R + NL))
+    tt(cols("eh_s", 64, 320), ps(R, R + NL), cols("eh_s", 64, 320), A.add)
+    decide(0)
+    for a, t, o in ((Y, "tri", "o32"), (Y2, "tri2", "o2")):
+        mm(ps(a, a + 128), v(t), half("sgn", 0), False, False)
+        mm(ps(a + 128, a + NL), v(o), half("sgn", 0), False, False)
+    for a, t in ((Y, "tri"), (Y2, "tri2")):
+        mm(ps(a + 128, a + NL), v(t), half("sgn", 1), False, True)
+    for h in range(2):
+        mm(ps(CNT, CNT + 1), half("sgn", h), cols("ob", 0, 1), h == 0, h == 1)
+    act(v("sq"), ps(Y2, Y2 + NL), AF.Square, bias=0.5)
+    act(PC["nu"], ps(CNT, CNT + 1), AF.Identity, scale=-0.5, bias=-128.0)
+    act(cols("fresh", 0, 12), cols("yw", 0, 12), AF.Relu, bias=PC["nu"])
+    report(0)
+    copy("v", v("ri"), ps(Y, Y + NL))
+    tt(v("apad", ALL, ALL, slice(0, 3, 2), ALL), ps(Y, Y + NL), v("ri"), A.is_equal)
+    for h in range(2):
+        ts(half("bv", h), half("sq", h), 64.0, A.is_lt, PC["v%d" % h], A.mult)
+    mm(ps(M, M + 12), v("idn"), cols("fresh", 0, 12), True, False)
+    for h in range(2):
+        for k in range(NG):
+            a, q = 128 * h + 16 * k, 32 * (k // 2)
+            mm(v("psb", slice(q, q + 32), slice(M, M + 12)), v("apad", ALL, 4 * h + k // 2, slice(k % 2, k % 2 + 2), ALL), cols("bv", a, a + 12),
+               False, h == 1 and k % 2 == 1)
+    scatter("tb", "w0", cols("z_s", 64, 320))
+    carry(2)
+    wrap("tb")
+    lookups(1, "gh:0:64")
+    ts(cols("w1", 20, 32), ps(M, M + 12), -1.0, A.mult, 320.0, A.add)
+    dyn = cols("w1", 20, 32)
+    copy("v", cols("oh1", FIX, NL), ind(cols("eh_s", 0, 512), dyn))
+    tt(cols("ef_s", 64, 320), ps(R, R + NL), cols("ef_s", 64, 320), A.add)
+    act(cols("zl1", FIX, NL), ind(cols("z_s", 0, 512), dyn))
+    dma("y", v("zd1"), v("zl1"), LOAD)
+    by_group("zd1", "zk3", to_asker(2), "a_z1", ASKZ)
+    dma("y", v("zu3"), v("zk3"))
+    n = 32
+
+    def keys(t):
+        if t == 1:
+            ts(cols("xp1", FIX, NL), cols("oh1", FIX, NL), PC["ck"], A.add)
+
+    def offsets(t):
+        if t == 1:
+            copy("v", cols("of1", FIX, NL), ind(cols("ef_s", 0, 512), cols("w1", 20, 32)))
+        else:
+            tt(cols("xq", FIX, NL), ind(v("ef_s"), cols("w2", 20, 32)), cols("dc", FIX, NL), A.add)
+            ts(cols("of2", FIX, NL), cols("xq", FIX, NL), PC["ck"], A.subtract)
+
+    def back(t, part):
+        if t == 1 and part == 0:
+            ts(v("pl0"), cols("msg", 0, 16), float(DUMP), A.is_lt, -80.0, A.mult)
+            tt(v("xw"), ps(Y2, Y2 + NL), v("m16"), A.mult)
+            for h in range(2):
+                mm(ps(CNT + 16 + 8 * h, CNT + 24 + 8 * h), half("xw", h), cols("blk", 0, 8), h == 0, False)
+            mm(ps(CNT + 16, CNT + 32), v("i8k"), v("pl0"), False, True)
+        elif t == 1:
+            ts(cols("tmq", 0, 12), cols("yw", 20, 32), PC["nu"], A.subtract, -256.0, A.add)
+            ts(cols("inv1", 20, 32), cols("tmq", 0, 12), float(NL), A.min)
+            ts(cols("inv1", 4, 20), ps(CNT + 16, CNT + 32), PC["ia"], A.add, float(NL), A.min)
+        elif part:
+            ts(cols("inv2", 0, n), cols("dst", 0, n), 63.0, A.add, float(NL), A.min)
+            ts(cols("inv2", n, n + 12), cols("yw", n, n + 12), PC["y"], A.add, float(NL), A.min)
+
+    def spare(t):
+        if t == 1:
+            known(2)
+        else:
+            tt(v("wk"), cols("yw", 80, 96), cols("uu", 4, 20), A.mult)
+            tt(v("wk"), v("wk"), cols("msg", 0, 16), A.max)
+            copy("v", v("w0k"), v("wk"))
+
+    def names(t):
+        act(v("lnf%d" % t), ind(v("idf"), cols("w%d" % t, 16, 32)))
+
+    STAGE.update({"keys": keys, "offsets": offsets, "back": back, "spare": spare, "names": names})
+
+    lookups(1)
+    growth(1)
+    decide(1)
+    report(1)
+    act(cols("r1", 0, NL), ps(R, R + NL), AF.Identity, bias=PC["b3"])
     scatter("occ", "w1", v("lnf1"))
-    copy("s", cols("g1", 0, 512), ind(v("r1"), v("inv1")))
-    tt(v("b1"), ind(v("occ"), v("w0")), cols("idf", 64, 320), A.not_equal)
-    if TB_EARLY:
-        scatter("tb", "w1", v("zlh"))
-        wrap()
-    wrapped(KH, 32, "el3", "g1", 0, False, False)
-    wrapped(KH + 4, 16, "eln", "b1", 0, False, True)
-    mm(ps(0, 512), v("idb"), cols("pay", 0, 512), True, False)
-    mm(ps(0, 512), v("idb"), cols("g1", 0, 512), False, False)
-    mm(ps(64, 320), v("mk2"), v("b1"), False, True)
-    copy("s", cols("pay2", 0, 512), ps(0, 512))
-    copy("s", cols("pay2", 512, NF), cols("pay", 512, NF))
-    lanes(2, 0, 32, ps(KH, KH + 32))
-    step(2)
-    way_back(2, 0, 32)
-    decide(2, "w2")
-    scatter("tb", "w2", v("zlh"))
+    act(cols("g1", 0, 512), ind(v("r1"), v("inv1")))
+    act(v("b1"), ind(v("occ"), v("w0")), AF.Sign, bias=1.0)
+    scatter("tb", "w1", v("zl1"))
+    PL, POS, NW, DC = PS[1] + 128, PS[0] + 128, PS[1] + 192, PS[0] + 256
+    wrapped(PL, 32, "el3", "g1", 0, True, False)
+    mm(ps(PL + 4, PL + 20), v("idn"), v("pl0"), False, False)
+    wrapped(PL + 4, 16, "eln", "b1", 0, False, True)
+    mm(ps(B[5], B[5] + 512), v("idb"), cols("pay", 0, 512), True, False)
+    mm(ps(B[5], B[5] + 512), v("mk2"), cols("g1", 0, 512), False, False)
+    mm(ps(B[5] + 64, B[5] + 320), v("mk2"), v("b1"), False, True)
+    act(cols("pay2", 0, 512), ps(B[5], B[5] + 512))
+    wrap("tb")
+    lookups(2, "gh:0:64 update gf:0:64")
+    ts(cols("uu", 0, n), ps(PL, PL + n), 40.0, A.is_lt)
+    scan(cols("scn", 0, n), cols("ob", 0, n), cols("uu", 0, n), A.add)
+    ts(cols("nb", 0, n), ps(PL, PL + n), 40.0, A.is_ge)
+    tt(cols("vb", 0, n), cols("nb", 0, n), cols("yw", 48, 48 + n), A.mult)
+    mm(ps(POS, POS + n), v("ntr"), cols("uu", 0, n), True, False)
+    mm(ps(POS, POS + n), v("onb"), cols("scn", 0, n), False, True)
+    mm(ps(POS + 64, POS + 65), v("onb1"), cols("scn", n - 1, n))
+    mm(ps(POS + 65, POS + 66), v("onb"), cols("scn", n - 1, n))
+    gate[:] = [tt(cols("dst", 0, n), ps(POS, POS + n), cols("vb", 0, n), A.max)]
+    ts(cols("nrow", FIX, NL), cols("pay", 512, 512 + DYN), ps(POS + 64, POS + 65), A.subtract)
+    ts(cols("dsu", 0, n), cols("dst", 0, n), 63.0, A.add)
+    copy("v", ind(v("nrow"), cols("dsu", 0, n)), cols("pay2", 0, 16 * n))
+    act(PC["y"], ps(POS + 65, POS + 66), AF.Identity, bias=float(FIX - 16 * n))
+    lookups(2, "sh:0:64")
+    gate[:] = []
+    mm(ps(DC, DC + DYN), v("ex2"), cols("nrow", FIX, NL))
+    wrapped(NW, 12, "el", "nrow", FIX)
+    act(cols("dc", FIX, NL), ps(DC, DC + DYN), AF.Identity, bias=PC["ck"])
+    copy("v", cols("w2", 20, 32), ps(NW, NW + 12))
+    dyn = cols("w2", 20, 32)
+    act(cols("zl2", FIX, NL), ind(v("z_s"), dyn))
+    tt(cols("xp2", FIX, NL), ind(v("eh_s"), dyn), cols("dc", FIX, NL), A.add)
+    ts(cols("oh2", FIX, NL), cols("xp2", FIX, NL), PC["ck"], A.subtract)
+
+    lookups(2)
+    growth(2)
+    decide(2)
+    scatter("tb", "w2", v("zl2"))
     dma("y", v("yt"), cols("tb", 0, NS), 5500)
-    copy("s", cols("r2", 0, NL), row)
-    copy("s", v("g2"), ind(v("r2"), v("inv2")))
+    act(cols("r2", 0, NL), ps(R, R + NL))
+    act(v("g2"), ind(v("r2"), v("inv2")))
     scatter("occ", "w2", v("lnf2"))
-    dma("s", v("yo"), v("occ", slice(0, 128, 16), slice(0, NS)))
     tt(cols("r3", 0, NL), ind(v("occ"), cols("w1", 0, 16)), v("lnf1"), A.not_equal)
-    copy("s", cols("g3", 0, 512), ind(v("r3"), v("inv1")))
-    tt(v("b3"), ind(v("occ"), v("w0")), cols("idf", 64, 320), A.not_equal)
-    tt(v("b3"), v("b3"), v("b1"), A.is_gt)
+    act(v("b3"), ind(v("occ"), v("w0k")), AF.Sign, bias=1.0)
+    act(cols("g3", 0, 512), ind(v("r3"), v("inv1")))
+    wrapped(PL, 16, "el3", "b3", 0)
+    tt(v("own"), ps(PL, PL + 16), cols("yw", 80, 96), A.mult)
+    tt(v("wk"), v("wk"), v("own"), A.max)
+    copy("v", v("w0"), v("wk"))
+    scatter("occ", "w0", cols("idf", 64, 320))
+    dma("y", v("yo"), v("occ", slice(0, 128, 16), slice(0, NS)))
+    mm(ps(0, 512), v("idb"), cols("pay2", 0, 512), True, False)
+    mm(ps(64, 320), v("idb"), v("d0r"), False, False)
     for a, b in ((0, 512), (512, NF)):
-        mm(ps(a, b), v("idb"), cols("pay2", a, b), True, False)
-        mm(ps(a, b), v("idb"), cols("g2", a, b), False, a > 0)
+        mm(ps(a, b), v("idb"), cols("g2", a, b), a > 0, a > 0)
     mm(ps(64, 320), v("idb"), v("b3"), False, False)
     mm(ps(0, 512), v("idb"), cols("g3", 0, 512), False, True)
     copy("s", cols("ydf", 512, NF), ps(512, NF))
-    copy("v", cols("ydf", 0, 512), ps(0, 512))
-    dma("y", v("yd", ALL, slice(0, 704)), v("ydf", slice(2, 128, 16), slice(64, NF)))
+    copy("s", cols("ydf", 0, 512), ps(0, 512))
+    dma("s", v("yd", ALL, slice(0, 704)), v("ydf", slice(2, 128, 16), slice(64, NF)))
     dma("s", v("yd", ALL, slice(704, NF)), v("ydf", slice(2, 128, 16), slice(0, 64)))
     F["finish"]()
 
 
 def rank_program(g, core, T, topo):
-    rank = T.rank_of(core)
-    if rank is not None:
-        rank_main(g, core, rank, T, topo)
+    if T.rank_of(core) is not None:
+        rank_main(g, core, T.rank_of(core), T, topo)
+        return
+    for rank in range(N):
+        senders = helpers(T.cores[rank], T, topo)[0]
+        if core in senders:
+            sender_main(g, core, rank, senders.index(core), T, topo)
+        jobs = [(t, c) for t in (1, 2) for c in range(NCH) if joiner(rank, t, c, T, topo) == core]
+        if jobs:
+            joiner_main(g, core, rank, jobs, T, topo)

@@ -11,6 +11,7 @@ FIX = 64
 DYN = NL - FIX
 ZC = NL + 16
 BIG = 8192.0
+TOP = 2.0 ** 61
 NCH, CH = 8, 512
 TYPES = {"b": "bfloat16", "f": "float32", "i": "int32", "u": "uint16"}
 SCRATCH = {"psb": ("psum", [128, 4096], "float32")}
@@ -21,7 +22,7 @@ for _where, _shape, _names in (
         ("sbuf", [128, 4096], "b:zrh b:zrf b:cvh b:cvf b:gth b:gtf"), ("sbuf", [128, 512], "b:each"), ("sbuf", [128, 1280], "b:nrow"),
         ("sbuf", [128, NL], "b:zt0 b:zt1 b:zt2 b:ztf i:efq0 f:xp0 f:xp1 f:xp2 f:xq f:dc u:oh0 u:oh1 u:oh2 u:of0 u:of1 u:of2 b:zl1 b:zl2 b:zlf b:zu1 b:zu2 b:zu3 "
                             "f:lnf1 f:lnf2 b:b1 b:b3 b:st f:kh b:kf b:rst b:m16 b:rr b:zb b:mid b:cl b:rl b:sgn b:whr b:wr0 "
-                            "f:xx b:sq i:ri b:xw b:d0r b:uu2 b:crow b:crow2 b:bv b:ob"),
+                            "f:xx b:sq i:ri b:xw b:d0r b:zz b:crow b:crow2 b:bv b:ob"),
         ("sbuf", [128, ZC], "b:r1 b:r2 b:r3"), ("sbuf", [128, 8, 384], "b:eq"), ("sbuf", [128, 144], "b:kf0 b:kf1 b:md2 b:rs2"),
         ("sbuf", [128, 8, 3, 16], "b:apad"), ("sbuf", [128, 16, 16], "b:ut"),
         ("sbuf", [128, 16], "u:w0 u:w0k u:lu1 u:lu2 u:lu3 i:hki f:own f:tmp f:tmq b:wq b:pl0 b:fresh f:wk u:lst"),
@@ -31,7 +32,7 @@ for _where, _shape, _names in (
         ("sbuf", [128, 48], "b:uu b:nb f:vb b:scn f:dst u:inv2"), ("sbuf", [128, 96], "f:yw"),
         ("sbuf", [128, 8], "i:pi f:sel"), ("sbuf", [128, 32], "f:pc b:blk u:lrep"),
         ("sbuf", [128, 144], "b:el b:el3 b:eln"),
-        ("sbuf", [128, 128], "f:id32 b:idb b:idn b:i8k b:i8n b:onb b:onb1 b:ntr b:ex2 b:mk2 b:rsel b:wsel b:tri b:tri2 b:o32 b:o2"),
+        ("sbuf", [128, 128], "f:id32 b:idb b:idn b:i8k b:i8n b:i4n b:clb b:onb b:onb1 b:ntr b:ex2 b:mk2 b:rsel b:wsel b:tri b:tri2 b:o32 b:o2"),
         ("sbuf", [128, 8, 128], "b:sg"), ("sbuf", [128, 8, 16], "b:osr"),
         ("dram", [1024, 32], "i:ed0 b:zd0 i:rl0 b:zl0 b:zd1 b:zk1 b:zk2 b:zk3"),
         ("dram", [2 * NCH * 128, CH], "b:hc"), ("dram", [2 * NCH * 1024, CH // 8], "b:hp b:ha")):
@@ -46,24 +47,28 @@ ENG = {"v": "ev", "s": "es", "p": "ep", "g": "eg"}
 SEMAPHORES = (["ev", "es", "ep", "eg", "lsem", "ltab", "a_z0", "a_q0", "a_r0", "a_u0", "a_u1", "a_zu", "a_z1", "a_f1", "a_f2"]
               + ["a_c%d" % c for c in range(2 * NCH)] + ["a_p%d" % k for k in range(2 * NCH)] + ["d%d" % k for k in range(40)])
 WRITES = ("out", "accum_out", "ap")
-CYCLE, TENSOR, WAKE = 1.0, 0.5, 60.0
-TELL, ASK0, ASKZ = 2200, 5500, 5000
-SHORT, LOAD = 1600, 6300
+CYCLE, TENSOR, WAKE = 1.1, 0.55, 60.0
+TELL, ASK0, ASKZ = 2000, 3000, 2800
+SHORT, LOAD = 1600, 4500
+ISSUE = 600
 SLACK = 1500
 TABLE = 10000
 FUSED = 1.56
 CALL = 0.0
 ON_SCALAR = {0: (0, 1, 2), 1: (), 2: ()}
 OWN_PLANE = {(t, c) for t in (1, 2) for c in range(0, NCH, 2)}
-PLAN = {1: "keys offsets th:64:128:s back:0 gh:64:128 th:224:256:s gh:224:256 zh:128:224:v sh:64:128 vh:128:224 update sh:224:256 sh:0:64 "
-           "mh:0:128:s vf:128:224 mh:224:256:s mh:128:224:v gf:0:64 choose chosen spare back:1 alike gf:64:128 sf:0:64 gf:224:256 sf:64:128 "
-           "sf:224:256 mf:128:224:v mf:224:256:s mf:0:128:s fin:0 names fin:1",
-        2: "th:192:256:s gh:64:128 th:64:128:s sf:0:64 offsets gh:224:256 sh:64:128 zh:128:224:v mh:0:128:s sh:224:256 mh:224:256:s vf:128:192 "
-           "vh:128:224 mh:128:224:v gf:64:128 choose gf:192:256 sf:64:128 back:1 chosen sf:192:256 spare alike mf:128:192:v names mf:0:128:s "
-           "mf:192:256:s fin:0 fin:1"}
+PLAN = {1: "back:0 gh:64:128 th:64:128:s th:224:256:s zh:128:224:v keys gh:224:256 vh:128:224 update mh:128:224:v offsets sh:64:128 vf:128:224 "
+           "sh:0:64 mf:128:224:v sh:224:256 mh:224:256:s mh:0:128:s gf:0:64 gf:64:128 sf:0:64 choose chosen back:1 sf:64:128 gf:224:256 spare "
+           "sf:224:256 mf:224:256:s mf:0:128:s alike fin:0 fin:1 names",
+        2: "zh:128:224:v th:224:256:s gh:64:128 offsets th:64:128:s gh:224:256 vh:128:224 sh:64:128 mh:128:224:v sh:224:256 gf:0:64 mh:224:256:s "
+           "mh:0:128:s vf:128:224 choose back:1 chosen gf:64:128 sf:0:64 sf:64:128 spare mf:128:224:v alike gf:224:256 sf:224:256 mf:0:128:s "
+           "fin:0 mf:224:256:s fin:1 names"}
 PLAN[0] = ("zh:0:128:s th:128:256:s gh:192:256 vh:0:128 gh:128:192 sh:192:256 sh:128:192 mh:0:128:v mh:128:256:s "
            "zf:0:160:v tf:128:256:s asks gf:192:256 vf:0:128 gf:160:192 sf:192:256 vf:128:160 sf:160:192 mf:0:128:v mf:192:256:s mf:128:160:v mf:160:192:s "
-           "choose answer chosen alike")
+           "choose chosen answer alike")
+PACK = ("gh:0:64", "sh:0:64 update")
+CARRY = {1: ((0, 1), (2, 3), (4, 5), (6, 7)), 2: ((0, 1), (2, 3, 4, 5), (6, 7))}
+FILL = 2 * NL
 MASKS = {}
 ALL = slice(None)
 
@@ -262,7 +267,7 @@ def flow(g, T):
                            for k in range(n) if ops[k]["q"] == q and not ops[k]["lazy"]) for q in queues}
         for k in sorted(range(n), key=lambda k: (due[k], k)):
             if ops[k]["lazy"]:
-                t = first = max([0.0] + [start[d] + busy[d] + lag + (SLACK if ops[d]["q"] == "g" != ops[k]["q"] else 0.0) for d, lag in before[k]])
+                t = first = max([0.0] + [start[d] + busy[d] + lag + (SLACK if ops[d]["q"] == "g" != ops[k]["q"] and ops[d]["lazy"] else 0.0) for d, lag in before[k]])
                 for a, b in taken[ops[k]["q"]]:
                     if b > t:
                         if a >= t + busy[k]:
@@ -337,7 +342,7 @@ def flow(g, T):
              "tensor_scalar": lambda: eng.tensor_scalar(**args), "scan": lambda: eng.tensor_tensor_scan(**args),
              "memset": lambda: eng.memset(args["ap"], args["constant"]),
              "activation": lambda: eng.activation(**args), "matmul": lambda: eng.matmul(**args),
-             "affine_select": lambda: eng.affine_select(**args),
+             "affine_select": lambda: eng.affine_select(**args), "tensor_reduce": lambda: eng.tensor_reduce(**args),
              "iota": lambda: eng.iota(**args)}[meth]
         return add(q, reads, writes, lambda: f().then_inc(T.sem[ENG[q]], 1), ENG[q], 1, cost(q, meth, kw))
 
@@ -354,7 +359,7 @@ def flow(g, T):
         go = lambda: g.remote_dma_fused(
             [RemoteDMATransfer(dst_ids=[d[0] for d in t[1]], dma_engine_mask=bits(t[2]), remote_sem=T.sem[t[3]],
                                srcs=[ap(t[0])], dsts=[ap(d[1]) for d in t[1]]) for t in transfers], local_sem=T.sem[local])
-        return add("g", [t[0] for t in transfers], [], go, local, sum(len(t[2]) for t in transfers), 300, late, after)
+        return add("g", [t[0] for t in transfers], [], go, local, sum(len(t[2]) for t in transfers), ISSUE, late, after)
 
     def finish():
         event = {}
@@ -386,17 +391,18 @@ def rows(name, n, a, b, step=None):
     return v(name, slice(0, n), slice(a, b, step))
 
 
-def carry_engines(core, T, topo):
-    senders = helpers(core, T, topo)[0]
-    every = topo.engines(core, senders[0])
-    return [every[k * len(every) // 2:(k + 1) * len(every) // 2] for k in range(2)]
+def carry_engines(core, t, c, T, topo):
+    every = topo.engines(core, helpers(core, T, topo)[0][0])
+    call = [x for x in CARRY[t] if c in x][0]
+    n = len(every) // len(call)
+    return every[n * call.index(c):n * call.index(c) + n]
 
 
 def sender_main(g, core, rank, j, T, topo):
     mine = range(j, 2 * NCH, 2)
     for s in mine:
         t, c = 1 + s // NCH, s % NCH
-        g.sync.wait_ge(T.sem["a_c%d" % s], len(carry_engines(T.cores[rank], T, topo)[j]))
+        g.sync.wait_ge(T.sem["a_c%d" % s], len(carry_engines(T.cores[rank], t, c, T, topo)))
         g.sync.dma_start(out=T["hp"][1024 * s:1024 * s + 1024, :], in_=T["hc"][128 * s:128 * s + 128, :]).then_inc(T.sem["d%d" % s], 16)
         g.wait_ge(T.sem["d%d" % s], 16)
         dst = [joiner(asker(rank, k, t), t, c, T, topo) for k in range(NG)]
@@ -467,7 +473,7 @@ def rank_main(g, core, rank, T, topo):
         return C("v", "scan", out=out, data0=d0, data1=d1, initial=0.0, op0=A.mult, op1=op)
 
     def fill(x, c):
-        iota(x, [[0, size(x)[0]]], c, 0)
+        C("v", "memset", ap=x, constant=c)
 
     def keep(out, in_, op, base, ch, pattern, other=0.0):
         C("g", "affine_select", out=out, in_=in_, pattern=pattern, compare_op=op, fill=other, base=base, channel_multiplier=ch)
@@ -501,7 +507,7 @@ def rank_main(g, core, rank, T, topo):
     dma("y", v("ed0"), v("ef", ALL, slice(0, NL)), 1800)
     dma("s", v("zd0"), v("zf", ALL, slice(0, NL)))
     dma("s", cols("z_s", 64, 320), v("zf", ALL, slice(0, NL)), 2000)
-    dma("y", cols("eh_s", 64, 320), v("eh", ALL, slice(0, NL)), 2200)
+    dma("y", cols("eh_s", 64, 320), v("eh", ALL, slice(0, NL)), 2900)
     dma("y", cols("tb", 0, NS), v("tab"), LOAD)
 
     iota(v("pi"), [[0, 8]], 0, 1)
@@ -509,8 +515,18 @@ def rank_main(g, core, rank, T, topo):
     by_group("zd0", "zl0", to_asked(0), "a_z0", ASKZ)
     sent["q0"] = by_group("ed0", "rl0", to_asked(0), "a_q0", ASK0)
     iota(v("each"), [[1, 32], [0, 16]], 0, 0)
+    by16 = lambda s, n=8: [[s, n], [0, 16]]
+    C("v", "memset", ap=v("ob"), constant=1.0)
+    lazy[0] = True
+    keep(v("rsel"), half("ob", 0), A.is_ge, 0, 1, by16(-4))
+    keep(v("rsel"), v("rsel"), A.is_ge, 2, -1, by16(4))
+    keep(v("osr"), v("rsel"), A.not_equal, -2, 1, by16(-4))
+    iota(v("m16"), [[0, 16], [1, 16]], 0, 0)
+    iota(cols("tmp", 0, 6), [[128, 6]], DUMP, 1)
+    for a, b, c in ((0, 48, 0), (48, 80, 600), (80, 96, DUMP)):
+        iota(cols("yw", a, b), [[16, b - a]], c, 0)
 
-    PC = {n: cols("pc", k, k + 1) for k, n in enumerate("p a g ck y nu v0 v1 b3 ia l c15 m0 m1 m2 m3 m01 m80".split())}
+    PC = {n: cols("pc", k, k + 1) for k, n in enumerate("p a g ck y nu v0 v1 b3 ia l c15 m0 m1 m2 m3 m01 m80 w thr".split())}
     pint = cols("pi", 0, 1)
 
     def bitcol(out, sh, mask, k):
@@ -522,7 +538,6 @@ def rank_main(g, core, rank, T, topo):
     bitcol(PC["a"], 0, 15, 0)
     bitcol(PC["g"], 4, 7, 1)
     ts(PC["ck"], PC["a"], -8192.0, A.mult, 122880.0, A.add)
-    C("v", "memset", ap=v("ob"), constant=1.0)
     C("v", "memset", ap=v("zb"), constant=0.0)
     ts(v("id32"), cols("rr", 0, 128), PC["p"], A.is_equal)
     ts(v("idb"), cols("rr", 0, 128), PC["p"], A.is_equal)
@@ -600,11 +615,11 @@ def rank_main(g, core, rank, T, topo):
             mm(ps(KH + 128 * h, KH + 128 * h + 128, 32), v("cd", ALL, slice(8 * h, 8 * h + 8), ALL), v("idb"))
 
     def chosen(t):
-        copy("v", rows("st", 32, 0, NL), ps(KH, KH + NL, 32))
+        copy("s" if ON_SCALAR[t] else "v", rows("st", 32, 0, NL), ps(KH, KH + NL, 32))
         for h in range(2):
             mm(ps(OWN + 8 * h, OWN + 8 * h + 8), rows("st", 32, 128 * h, 128 * h + 128), v("osr", slice(0, 32), ALL, 0))
         if ON_SCALAR[t]:
-            copy("v" if t else "s", v("own"), ps(OWN, OWN + 16))
+            copy("s", v("own"), ps(OWN, OWN + 16))
         sent["c%d" % t] = F["last"]()
         if t == 0:
             for h in range(2):
@@ -613,26 +628,23 @@ def rank_main(g, core, rank, T, topo):
 
     def alike(t, first=0, end=NG):
         for k in range(first, end):
-            a, sg = bank() if k in ON_SCALAR[t] else B[4 + k % 2], v("sg", slice(0, 32), k, ALL)
-            mm(ps(a + 128, a + 384), sg, rows("st", 32, 0, NL), True, False)
-            mm(ps(a, a + 128), sg, rows("st", 32, 128, NL), False, False)
-            mm(ps(a, a + NL), v("i8k"), v("uu2"), False, True)
+            a = bank() if k in ON_SCALAR[t] else B[4 + k % 2]
+            mm(ps(a, a + NL), v("sg", slice(0, 32), k, ALL), rows("st", 32, 0, NL))
             for h, x, y in ((1, 0, 128), (0, 128, 384)):
                 own = cols("own", 8 * h + k, 8 * h + k + 1) if ON_SCALAR[t] else ps(OWN + 8 * h + k, OWN + 8 * h + k + 1)
                 if k in ON_SCALAR[t]:
-                    act(cols("gtf", 384 * k + x, 384 * k + y), ps(a + x, a + y), AF.Abs, scale=-1.0, bias=own)
+                    act(cols("gth", 384 * k + x, 384 * k + y), ps(a + 128 * h, a + NL), AF.Abs, scale=-1.0, bias=own)
                 else:
-                    ts(v("eq", ALL, k, slice(x, y)), ps(a + x, a + y), own, A.is_equal, BIG, A.mult)
+                    ts(v("eq", ALL, k, slice(x, y)), ps(a + 128 * h, a + NL), own, A.is_equal)
             if k in ON_SCALAR[t]:
-                act(v("eq", ALL, k, ALL), cols("gtf", 384 * k, 384 * k + 384), AF.Relu, scale=-BIG, bias=BIG)
-        sent["g%d" % t] = F["last"]()
+                act(v("eq", ALL, k, ALL), cols("gth", 384 * k, 384 * k + 384), AF.Relu, scale=-1.0, bias=1.0)
 
     def answer(t):
         scan(v("kf"), v("rst"), ps(KF[0], KF[0] + NL), A.max)
         sent["a0"] = copy("v", v("wq"), cols("kf", 15, NL, 16))
         sent["r0"] = tell(v("wq"), "lr0", "a_r0")
 
-    known_ = set()
+    SLOT = lambda t, h: B[4 + h] if t else B[h]
 
     def fin(t, h):
         if t == 0:
@@ -642,18 +654,20 @@ def rank_main(g, core, rank, T, topo):
             mm(ps(KF[h] + 16, KF[h] + 136, 128, 17), v("idb"), v("cd", ALL, slice(8 * h, 8 * h + 8), 3))
             scan(cols("kf%d" % h, 0, 136), cols("rs2", 0, 136), ps(KF[h], KF[h] + 136), A.max)
             w = ind(cols("kf%d" % h, 0, 136), cols("lrep", 16, 24))
-        ts(half("cl", h), w, 8.0, A.is_lt)
+        ts(half("cl", h), w, 8.0, A.is_lt, PC["w"], A.mult)
+        if h == 0 and t == 0:
+            ts(v("clb"), w, 8.0, A.is_lt, TOP, A.mult)
+        elif h == 0:
+            act(v("clb"), w, AF.Relu, scale=-TOP, bias=8 * TOP)
         act(half("rl", h), w, AF.Relu, bias=-8.0)
-        mm(ps(PS[h], PS[h] + 128), rows("st", 32, 128 * h, 128 * h + 128), rows("rsel", 32, 0, 128), True, False)
-        known_.add((t, h))
-        other = (t, 1 - h) in known_
-        todo = ([(128, 0, 0)] if h == 0 else []) + ([(256, 0, 1)] if other else []) + ([(0, 1, 1)] if h == 1 else [])
-        for at, (c, j, i) in enumerate(todo):
-            if i == j:
-                mm(ps(PS[i], PS[i] + 128), v("i8k"), half("cl", i), False, False)
+        for at, (c, cl) in enumerate(((128, half("cl", 0)),) if h == 0 else ((256, v("clb")), (0, half("cl", 1)))):
+            last_ = h == 0 or at == 1
+            if last_:
+                mm(ps(PS[h], PS[h] + 128), v("i4n"), half("cl", h), h == 0, False)
             for k in range(NG):
-                mm(ps(PS[i] + 16 * k, PS[i] + 16 * k + 16), v("eq", ALL, k, slice(c, c + 128)), cols("cl", 128 * j + 16 * k, 128 * j + 16 * k + 16),
-                   False, k == NG - 1 and (i == 0 or (other and at == len(todo) - 1)))
+                mm(ps(PS[h] + 16 * k, PS[h] + 16 * k + 16), v("eq", ALL, k, slice(c, c + 128)), v(cl[1], ALL, slice(cl[2][1].start + 16 * k, cl[2][1].start + 16 * k + 16)),
+                   k == 0 and not last_, last_ and k == NG - 1)
+        mm(ps(SLOT(t, h), SLOT(t, h) + 128), rows("st", 32, 128 * h, 128 * h + 128), v("osr", slice(0, 32), ALL, ALL), True, False)
 
     def scatter(table, lists, vals):
         return copy("v", ind(v(table), cols(lists, 0, 16)), vals)
@@ -683,12 +697,15 @@ def rank_main(g, core, rank, T, topo):
 
     def decide(t):
         for h in range(2):
-            tt(half("xx", h), ps(PS[h], PS[h] + 128), cols("dm", NL * t + 128 * h, NL * t + 128 * h + 128), A.min)
+            ts(half("zz", h), ps(PS[h], PS[h] + 128), PC["thr"], A.is_ge, BIG, A.mult)
+            mm(ps(SLOT(t, h), SLOT(t, h) + 128), v("idb"), half("zz", h), False, True)
+        for h in range(2):
+            tt(half("xx", h), ps(SLOT(t, h), SLOT(t, h) + 128), cols("dm", NL * t + 128 * h, NL * t + 128 * h + 128), A.min)
             mm(ps(LW + 8 * h, LW + 8 * h + 8), half("xx", h), v("sel"))
             if t == 0:
-                act(half("sgn", h), ps(PS[h], PS[h] + 128), AF.Sign, bias=-6000.0)
+                act(half("sgn", h), half("zz", h), AF.Sign, bias=-1.0)
             if t == 1:
-                act(v("ut", ALL, slice(8 * h, 8 * h + 8), 3), ps(PS[h], PS[h] + 128, 128, 16), AF.Sign, bias=-6000.0)
+                act(v("ut", ALL, slice(8 * h, 8 * h + 8), 3), cols("zz", 128 * h, 128 * h + 128, 16), AF.Sign, bias=-1.0)
                 mm(ps(R + 128 * h, R + 128 * h + 128), v("ut", ALL, slice(8 * h, 8 * h + 8), ALL), v("i8k"), False, h == 1)
         copy("v", cols("w%d" % t, 0, 16), ps(LW, LW + 16))
 
@@ -701,20 +718,23 @@ def rank_main(g, core, rank, T, topo):
             mm(ps(a, a + n), cols(el, 15 - i, 143 - i), cols(src, first + i, first + 16 * n, 16), start and i == 0, stop and i == 15)
 
     one, zero = half("ob", 0), half("zb", 0)
-    line, by16, in16 = lambda s, n=128: [[s, n]], lambda s, n=8: [[s, n], [0, 16]], lambda n=8: [[0, n], [1, 16]]
+    line, in16 = lambda s, n=128: [[s, n]], lambda n=8: [[0, n], [1, 16]]
     keep(v("rst"), v("ob"), A.not_equal, 0, 0, in16(16))
-    iota(v("di", ALL, ALL, 2), [[0, 16]], int(BIG), 0)
-    keep(v("rsel"), one, A.is_ge, 0, 1, by16(-4))
-    keep(v("rsel"), v("rsel"), A.is_ge, 2, -1, by16(4))
-    keep(v("osr"), v("rsel"), A.not_equal, -2, 1, by16(-4))
+    fill(v("di", ALL, ALL, 2), 0)
     for k in range(8):
-        dma("s", v("sg", slice(0, 32), ALL, slice(16 * k, 16 * k + 16)), v("osr", slice(0, 32), ALL, ALL))
+        ts(v("sg", slice(0, 32), k, ALL), rows("ob", 32, 0, 128), v("osr", slice(0, 32), k, slice(0, 1)), A.mult)
     keep(v("wsel"), one, A.is_equal, -3, 1, by16(-4))
-    for name, c in (("i8k", -BIG), ("i8n", -8.0), ("idn", -1.0)):
+    for name, c in (("i4n", -4.0), ("i8k", -BIG), ("idn", -1.0)):
         keep(v(name), zero, A.not_equal, 0, 1, line(-1), c)
-    keep(v("uu2"), v("ob"), A.is_ge, 0, 1, [[0, 2], [-1, 128]])
+    for h, (first, step) in enumerate(((TOP, 0.5), (-8.0 / TOP, 2.0))):
+        C("v", "memset", ap=half("xq", h), constant=step)
+        C("v", "scan", out=half("xx", h), data0=half("xq", h), data1=zero, initial=first, op0=A.mult, op1=A.add)
+    tt(v("i8n"), half("xx", 1), v("idb"), A.mult)
+    tt(half("xq", 0), half("xx", 0), v("id32"), A.mult)
+    C("v", "tensor_reduce", out=PC["w"], in_=half("xq", 0), axis=AxisListType.X, op=A.add)
+    ts(PC["thr"], PC["w"], -1.5, A.mult)
     ts(v("sel"), cols("rr", 0, 8), PC["g"], A.is_equal)
-    keep(v("tri2"), zero, A.is_ge, 0, 1, line(-1), 0.5)
+    ts(v("tri2"), cols("rr", 0, 128), PC["p"], A.is_gt, 0.5, A.mult)
     keep(v("tri"), zero, A.is_ge, 0, 1, line(-1), 1.0 / 32)
     keep(v("tri"), v("tri"), A.not_equal, 0, 1, line(-1), -1.0 / 64)
     keep(v("o32"), zero, A.is_gt, 0, 0, line(0), 1.0 / 32)
@@ -722,25 +742,21 @@ def rank_main(g, core, rank, T, topo):
     iota(v("crow"), [[128, 2], [0, 8], [-2, 16]], 1, 0)
     iota(v("crow2"), [[64, 2], [0, 8], [-16, 16]], -8, 0)
     iota(cols("pc", 6, 8), [[-128, 2]], 256, -1)
-    iota(cols("tmp", 0, 6), [[128, 6]], DUMP, 1)
-    iota(v("m16"), in16(16), 0, 0)
     ts(PC["b3"], PC["a"], 3.0, A.is_equal, BIG, A.mult)
     ts(PC["ia"], PC["a"], 16.0, A.mult, 72.0, A.add)
     ts(v("m16"), v("m16"), PC["a"], A.is_equal)
     for x in range(6):
         act(cols("dm", 128 * x, 128 * x + 128), half("m16", 0), AF.Identity, scale=cols("tmp", x, x + 1))
     fill(v("apad", ALL, ALL, 1, ALL), 0)
-    for a, b, c in ((0, 48, 0), (48, 80, 600), (80, 96, DUMP)):
-        iota(cols("yw", a, b), line(16, b - a), c, 0)
     act(v("yw"), v("yw"), AF.Identity, bias=PC["a"])
     copy("v", cols("w1", 16, 20), cols("yw", 0, 4))
     copy("v", cols("inv1", 0, 4), cols("yw", 0, 4))
     copy("v", cols("w2", 16, 20), cols("yw", 44, 48))
     copy("v", cols("inv2", 44, 48), cols("yw", 0, 4))
-    keep(cols("rs2", 0, 136), cols("ob", 0, 136), A.not_equal, 0, 0, [[0, 8], [1, 17]])
-    fill(cols("md2", 0, 136), 8)
+    iota(cols("md2", 0, 136), [[0, 136]], 8, 0)
     keep(cols("md2", 0, 136), cols("md2", 0, 136), A.not_equal, -16, 0, [[0, 8], [1, 17]])
-    fill(v("ut"), 0)
+    keep(cols("rs2", 0, 136), cols("ob", 0, 136), A.not_equal, 0, 0, [[0, 8], [1, 17]])
+    iota(v("ut"), [[0, NL]], 0, 0)
     keep(v("onb"), one, A.is_ge, 0, 1, by16(-16))
     keep(v("onb"), v("onb"), A.is_ge, 15, -1, by16(16))
     keep(v("onb1"), v("onb"), A.is_equal, -1, 0, in16())
@@ -771,18 +787,16 @@ def rank_main(g, core, rank, T, topo):
     ts(cols("hki", 0, 2), cols("hki", 0, 2), float(rank + 1), A.add)
     ts(cols("hki", 0, 2), cols("hki", 0, 2), N - 1, A.bitwise_and)
     ts(cols("lst", 0, 4, 2), cols("hki", 0, 2), 16.0, A.mult, PC["a"], A.add)
-    for name in ("lr0", "la0", "la1"):
-        fill(cols(name, 16 * rank, 16 * rank + 16), 0)
-    for name in ("r1", "r2", "r3"):
-        fill(cols(name, NL, ZC), 0)
+    for x in [cols(name, 16 * rank, 16 * rank + 16) for name in ("lr0", "la0", "la1")] + [cols(name, NL, ZC) for name in ("r1", "r2", "r3")]:
+        iota(x, [[0, 16]], 0, 0)
     lazy[0] = False
 
-    senders, halves = helpers(core, T, topo)[0], carry_engines(core, T, topo)
+    senders = helpers(core, T, topo)[0]
 
     def carry(t, after=()):
-        for c in range(0, NCH, 2):
-            mine = fused([(cols("tb", CH * x, CH * x + CH), [(dst_id(topo, senders[x % 2]), blk("hc", NCH * (t - 1) + x))], halves[x % 2],
-                           "a_c%d" % (NCH * (t - 1) + x)) for x in (c, c + 1)], 4000, after if c == 2 else (), "ltab")
+        for call in CARRY[t]:
+            mine = fused([(cols("tb", CH * x, CH * x + CH), [(dst_id(topo, senders[x % 2]), blk("hc", NCH * (t - 1) + x))],
+                           carry_engines(core, t, x, T, topo), "a_c%d" % (NCH * (t - 1) + x)) for x in call], 4000, after if call[0] == NCH // 2 else (), "ltab")
         arrive([cols("tf%d" % t, 0, NS)], "a_f%d" % t, sum(len(topo.engines(joiner(rank, t, c, T, topo), core)) for c in range(NCH)), [mine], TABLE)
 
     asks = [dma("y", v("zlf"), v("zl0")), dma("y", v("efq0"), v("rl0"))]
@@ -791,9 +805,13 @@ def rank_main(g, core, rank, T, topo):
     flights = (("ef_s", "ef", 0), ("eh_s", "eh", NL), ("z_s", "zf", NL))
     for name, src, a in flights:
         dma("y", cols(name, 0, 64), v(src, ALL, slice(704, NF)), after=asks)
+    for name, src, a in flights:
+        dma("y", cols(name, 64 + a, 512), v(src, ALL, slice(a, 448)))
     lazy[0] = True
-    for a in range(0, NT, NT // 16):
-        fill(cols("occ", a, a + NT // 16), -1)
+    for a in range(0, FILL, NL):
+        act(cols("occ", a, a + NL), v("rr"), AF.Identity, scale=0.0, bias=-1.0)
+    for a in range(FILL, NT, 336):
+        iota(cols("occ", a, min(a + 336, NT)), [[0, min(336, NT - a)]], -1, 0)
 
     def known(t):
         y0 = (64, 0, 704)[t]
@@ -806,9 +824,7 @@ def rank_main(g, core, rank, T, topo):
     lazy[0] = False
     STAGE["asks"] = lambda t: copy("v", v("of0"), v("efq0"))
     lookups(0)
-    for name, src, a in flights:
-        dma("y", cols(name, 64 + a, 512), v(src, ALL, slice(a, 448)), after=[sent["r0"]])
-    dma("y", v("zu1"), v("zk1"))
+    dma("y", v("zu1"), v("zk1"), after=[sent["r0"]])
     for name, src, a in flights:
         dma("y", cols(name, 512, NF), v(src, ALL, slice(448, 704)))
     lazy[0] = True
@@ -821,9 +837,8 @@ def rank_main(g, core, rank, T, topo):
     for h in range(2):
         fin(0, h)
     growth(0)
-    act(v("d0r"), ps(R, R + NL))
-    tt(cols("eh_s", 64, 320), ps(R, R + NL), cols("eh_s", 64, 320), A.add)
     decide(0)
+    tt(cols("eh_s", 64, 320), ps(R, R + NL), cols("eh_s", 64, 320), A.add)
     for a, t, o in ((Y, "tri", "o32"), (Y2, "tri2", "o2")):
         mm(ps(a, a + 128), v(t), half("sgn", 0), False, False)
         mm(ps(a + 128, a + NL), v(o), half("sgn", 0), False, False)
@@ -835,6 +850,7 @@ def rank_main(g, core, rank, T, topo):
     act(PC["nu"], ps(CNT, CNT + 1), AF.Identity, scale=-0.5, bias=-128.0)
     act(cols("fresh", 0, 12), cols("yw", 0, 12), AF.Relu, bias=PC["nu"])
     report(0)
+    act(v("d0r"), ps(R, R + NL))
     copy("v", v("ri"), ps(Y, Y + NL))
     tt(v("apad", ALL, ALL, slice(0, 3, 2), ALL), ps(Y, Y + NL), v("ri"), A.is_equal)
     for h in range(2):
@@ -846,14 +862,14 @@ def rank_main(g, core, rank, T, topo):
             mm(v("psb", slice(q, q + 32), slice(M, M + 12)), v("apad", ALL, 4 * h + k // 2, slice(k % 2, k % 2 + 2), ALL), cols("bv", a, a + 12),
                False, h == 1 and k % 2 == 1)
     scatter("tb", "w0", cols("z_s", 64, 320))
+    tt(cols("ef_s", 64, 320), ps(R, R + NL), cols("ef_s", 64, 320), A.add)
     carry(2)
     wrap("tb")
     lookups(1, "gh:0:64")
     ts(cols("w1", 20, 32), ps(M, M + 12), -1.0, A.mult, 320.0, A.add)
     dyn = cols("w1", 20, 32)
     copy("v", cols("oh1", FIX, NL), ind(cols("eh_s", 0, 512), dyn))
-    tt(cols("ef_s", 64, 320), ps(R, R + NL), cols("ef_s", 64, 320), A.add)
-    act(cols("zl1", FIX, NL), ind(cols("z_s", 0, 512), dyn))
+    copy("v", cols("zl1", FIX, NL), ind(cols("z_s", 0, 512), dyn))
     dma("y", v("zd1"), v("zl1"), LOAD)
     by_group("zd1", "zk3", to_asker(2), "a_z1", ASKZ)
     dma("y", v("zu3"), v("zk3"))
@@ -892,6 +908,7 @@ def rank_main(g, core, rank, T, topo):
             tt(v("wk"), cols("yw", 80, 96), cols("uu", 4, 20), A.mult)
             tt(v("wk"), v("wk"), cols("msg", 0, 16), A.max)
             copy("v", v("w0k"), v("wk"))
+            scatter("occ", "w0k", cols("idf", 64, 320))
 
     def names(t):
         act(v("lnf%d" % t), ind(v("idf"), cols("w%d" % t, 16, 32)))
@@ -916,7 +933,7 @@ def rank_main(g, core, rank, T, topo):
     mm(ps(B[5] + 64, B[5] + 320), v("mk2"), v("b1"), False, True)
     act(cols("pay2", 0, 512), ps(B[5], B[5] + 512))
     wrap("tb")
-    lookups(2, "gh:0:64 update gf:0:64")
+    lookups(2, PACK[0])
     ts(cols("uu", 0, n), ps(PL, PL + n), 40.0, A.is_lt)
     scan(cols("scn", 0, n), cols("ob", 0, n), cols("uu", 0, n), A.add)
     ts(cols("nb", 0, n), ps(PL, PL + n), 40.0, A.is_ge)
@@ -930,7 +947,7 @@ def rank_main(g, core, rank, T, topo):
     ts(cols("dsu", 0, n), cols("dst", 0, n), 63.0, A.add)
     copy("v", ind(v("nrow"), cols("dsu", 0, n)), cols("pay2", 0, 16 * n))
     act(PC["y"], ps(POS + 65, POS + 66), AF.Identity, bias=float(FIX - 16 * n))
-    lookups(2, "sh:0:64")
+    lookups(2, PACK[1])
     gate[:] = []
     mm(ps(DC, DC + DYN), v("ex2"), cols("nrow", FIX, NL))
     wrapped(NW, 12, "el", "nrow", FIX)
@@ -944,29 +961,23 @@ def rank_main(g, core, rank, T, topo):
     lookups(2)
     growth(2)
     decide(2)
-    scatter("tb", "w2", v("zl2"))
-    dma("y", v("yt"), cols("tb", 0, NS), 5500)
     act(cols("r2", 0, NL), ps(R, R + NL))
     act(v("g2"), ind(v("r2"), v("inv2")))
+    scatter("tb", "w2", v("zl2"))
+    dma("y", v("yt"), cols("tb", 0, NS), 5500)
     scatter("occ", "w2", v("lnf2"))
-    tt(cols("r3", 0, NL), ind(v("occ"), cols("w1", 0, 16)), v("lnf1"), A.not_equal)
-    act(v("b3"), ind(v("occ"), v("w0k")), AF.Sign, bias=1.0)
-    act(cols("g3", 0, 512), ind(v("r3"), v("inv1")))
-    wrapped(PL, 16, "el3", "b3", 0)
-    tt(v("own"), ps(PL, PL + 16), cols("yw", 80, 96), A.mult)
-    tt(v("wk"), v("wk"), v("own"), A.max)
-    copy("v", v("w0"), v("wk"))
-    scatter("occ", "w0", cols("idf", 64, 320))
     dma("y", v("yo"), v("occ", slice(0, 128, 16), slice(0, NS)))
-    mm(ps(0, 512), v("idb"), cols("pay2", 0, 512), True, False)
-    mm(ps(64, 320), v("idb"), v("d0r"), False, False)
-    for a, b in ((0, 512), (512, NF)):
-        mm(ps(a, b), v("idb"), cols("g2", a, b), a > 0, a > 0)
-    mm(ps(64, 320), v("idb"), v("b3"), False, False)
-    mm(ps(0, 512), v("idb"), cols("g3", 0, 512), False, True)
-    copy("s", cols("ydf", 512, NF), ps(512, NF))
-    copy("s", cols("ydf", 0, 512), ps(0, 512))
-    dma("s", v("yd", ALL, slice(0, 704)), v("ydf", slice(2, 128, 16), slice(64, NF)))
+    parts = (("g2", 0, NF), ("pay2", 0, 512), ("d0r", 64, 320), ("b3", 64, 320), ("g3", 0, 512))
+    for x, q in ((2, "s"), (1, "s"), (0, "v")):
+        if x == 1:
+            tt(cols("r3", 0, NL), ind(v("occ"), cols("w1", 0, 16)), v("lnf1"), A.not_equal)
+            act(cols("g3", 0, 512), ind(v("r3"), v("inv1")))
+            tt(v("b3"), ind(v("occ"), v("w0k")), cols("idf", 64, 320), A.not_equal)
+        mine = [(name, max(a, NL * x), min(b, NL * x + NL), a % 128) for name, a, b in parts if a < NL * x + NL and NL * x < b]
+        for k, (name, a, b, first) in enumerate(mine):
+            mm(ps(B[x] + a - NL * x, B[x] + b - NL * x), v("idb"), cols(name, a - first, b - first), k == 0, k == len(mine) - 1)
+        copy(q, cols("ydf", NL * x, NL * x + NL), ps(B[x], B[x] + NL))
+    dma("y", v("yd", ALL, slice(0, 704)), v("ydf", slice(2, 128, 16), slice(64, NF)))
     dma("s", v("yd", ALL, slice(704, NF)), v("ydf", slice(2, 128, 16), slice(0, 64)))
     F["finish"]()
 

import numpy as np
from concourse.bass import DstId, RemoteDMATransfer
from concourse.mybir import AluOpType as A, AxisListType, ActivationFunctionType as AF

N, NG, NS, NF, NL = 8, 8, 4096, 768, 256
CORES_ALL = 64
WR = 32
NT = NS + WR + 3 * NL
DUMP = NS + WR
FIX = 64
DYN = NL - FIX
ZC = NL + 16
BIG = 8192.0
TOP = 2.0 ** 61
NCH, CH = 8, 512
TYPES = {"b": "bfloat16", "f": "float32", "i": "int32", "u": "uint16"}
SCRATCH = {"psb": ("psum", [128, 4096], "float32")}
PACKED = {}
for _where, _shape, _names in (
        ("sbuf", [128, NT], "b:tb b:tf1 b:tf2 f:occ"),
        ("sbuf", [128, NF], "i:eh_s i:ef_s b:z_s b:pay b:pay2 f:idf b:g1 b:g2 b:g3 f:ydf f:dm"),
        ("sbuf", [128, 4096], "b:zrh b:zrf b:cvh b:cvf b:gth b:gtf"), ("sbuf", [128, 512], "b:each"), ("sbuf", [128, 1280], "b:nrow"),
        ("sbuf", [128, NL], "b:zt0 b:zt1 b:zt2 b:ztf i:efq0 f:xp0 f:xp1 f:xp2 f:xq f:dc u:oh0 u:oh1 u:oh2 u:of0 u:of1 u:of2 b:zl1 b:zl2 b:zlf b:zu1 b:zu2 b:zu3 "
                            "f:lnf1 f:lnf2 b:b1 b:b3 b:st f:kh b:kf b:rst b:m16 b:rr b:zb b:mid b:cl b:rl b:sgn b:whr b:wr0 "
                            "f:xx b:sq i:ri b:xw b:d0r b:zz b:crow b:crow2 b:bv b:ob"),
        ("sbuf", [128, ZC], "b:r1 b:r2 b:r3"), ("sbuf", [128, 8, 384], "b:eq"), ("sbuf", [128, 144], "b:kf0 b:kf1 b:md2 b:rs2"),
        ("sbuf", [128, 8, 3, 16], "b:apad"), ("sbuf", [128, 16, 16], "b:ut"),
        ("sbuf", [128, 16], "u:w0 u:w0k u:lu1 u:lu2 u:lu3 i:hki f:own f:tmp f:tmq b:wq b:pl0 b:fresh f:wk u:lst"),
        ("sbuf", [128, 32], "u:w1 u:w2 u:inv1 u:dsu f:msg"),
        ("sbuf", [128, N * 16], "b:lr0 f:la0 f:la1"),
        ("sbuf", [128, 16, 4], "i:di b:cd"),
        ("sbuf", [128, 48], "b:uu b:nb f:vb b:scn f:dst u:inv2"), ("sbuf", [128, 96], "f:yw"),
        ("sbuf", [128, 8], "i:pi f:sel"), ("sbuf", [128, 32], "f:pc b:blk u:lrep"),
        ("sbuf", [128, 144], "b:el b:el3 b:eln"),
        ("sbuf", [128, 128], "f:id32 b:idb b:idn b:i8k b:i8n b:i4n b:clb b:onb b:onb1 b:ntr b:ex2 b:mk2 b:rsel b:wsel b:tri b:tri2 b:o32 b:o2"),
        ("sbuf", [128, 8, 128], "b:sg"), ("sbuf", [128, 8, 16], "b:osr"),
        ("dram", [1024, 32], "i:ed0 b:zd0 i:rl0 b:zl0 b:zd1 b:zk1 b:zk2 b:zk3"),
        ("dram", [2 * NCH * 128, CH], "b:hc"), ("dram", [2 * NCH * 1024, CH // 8], "b:hp b:ha")):
    for _n in _names.split():
        if _where == "sbuf" and len(_shape) == 2 and _shape[1] <= ZC:
            _used = SCRATCH.get("all_" + _n[0], (0, [0, 0]))[1][1]
            PACKED[_n[2:]] = ("all_" + _n[0], _used, _shape[1])
            SCRATCH["all_" + _n[0]] = (_where, [128, _used + (_shape[1] + 15) // 16 * 16], TYPES[_n[0]])
        else:
            SCRATCH[_n[2:]] = (_where, _shape, TYPES[_n[0]])
ENG = {"v": "ev", "s": "es", "p": "ep", "g": "eg"}
SEMAPHORES = (["ev", "es", "ep", "eg", "lsem", "ltab", "a_z0", "a_q0", "a_r0", "a_u0", "a_u1", "a_zu", "a_z1", "a_f1", "a_f2"]
              + ["a_c%d" % c for c in range(2 * NCH)] + ["a_p%d" % k for k in range(2 * NCH)] + ["d%d" % k for k in range(40)])
WRITES = ("out", "accum_out", "ap")
CYCLE, TENSOR, WAKE = 1.1, 0.55, 60.0
TELL, ASK0, ASKZ = 2000, 3000, 2800
SHORT, LOAD = 1600, 4500
ISSUE = 600
SLACK = 1500
TABLE = 10000
FUSED = 1.56
CALL = 0.0
ON_SCALAR = {0: (0, 1, 2), 1: (), 2: ()}
OWN_PLANE = {(t, c) for t in (1, 2) for c in range(0, NCH, 2)}
PLAN = {1: "back:0 gh:64:128 th:64:128:s th:224:256:s zh:128:224:v keys gh:224:256 vh:128:224 update mh:128:224:v offsets sh:64:128 vf:128:224 "
           "sh:0:64 mf:128:224:v sh:224:256 mh:224:256:s mh:0:128:s gf:0:64 gf:64:128 sf:0:64 choose chosen back:1 sf:64:128 gf:224:256 spare "
           "sf:224:256 mf:224:256:s mf:0:128:s alike fin:0 fin:1 names",
        2: "zh:128:224:v th:224:256:s gh:64:128 offsets th:64:128:s gh:224:256 vh:128:224 sh:64:128 mh:128:224:v sh:224:256 gf:0:64 mh:224:256:s "
           "mh:0:128:s vf:128:224 choose back:1 chosen gf:64:128 sf:0:64 sf:64:128 spare mf:128:224:v alike gf:224:256 sf:224:256 mf:0:128:s "
           "fin:0 mf:224:256:s fin:1 names"}
PLAN[0] = ("zh:0:128:s th:128:256:s gh:192:256 vh:0:128 gh:128:192 sh:192:256 sh:128:192 mh:0:128:v mh:128:256:s "
           "zf:0:160:v tf:128:256:s asks gf:192:256 vf:0:128 gf:160:192 sf:192:256 vf:128:160 sf:160:192 mf:0:128:v mf:192:256:s mf:128:160:v mf:160:192:s "
           "choose chosen answer alike")
PACK = ("gh:0:64", "sh:0:64 update")
CARRY = {1: ((0, 1), (2, 3), (4, 5), (6, 7)), 2: ((0, 1), (2, 3, 4, 5), (6, 7))}
FILL = 2 * NL
MASKS = {}
ALL = slice(None)


def asked(r, g, t):
    return (r + 1 + (t + g) % (N - 1)) % N


def asker(q, g, t):
    return (q - 1 - (t + g) % (N - 1)) % N


def dst_id(topo, c):
    a = topo.addr(c)
    return DstId(rid=a[0], pnc=a[1])


def off_chip(topo, src, dst):
    return topo.chip(src) != topo.chip(dst)


def far_engines(core, T, topo):
    for c in T.cores:
        if off_chip(topo, core, c) and topo.may_write(core, c):
            return topo.engines(core, c)
    return []


def near_engines(core, dst, T, topo):
    far = far_engines(core, T, topo)
    return [e for e in topo.engines(core, dst) if e not in far]


def singles(core, dsts, T, topo):
    nf, nn, out = 0, 0, []
    for d in dsts:
        if off_chip(topo, core, d):
            out.append(topo.engines(core, d)[nf])
            nf += 1
        else:
            out.append(near_engines(core, d, T, topo)[nn])
            nn += 1
    return out


def bits(engines):
    m = 0
    for e in engines:
        m |= 1 << e
    return m


def helpers(core, T, topo):
    mate = [c for c in range(CORES_ALL) if topo.mates(topo.chip(c), topo.chip(core)) and topo.die(c) == topo.die(core)]
    beside = [c for c in topo.cores_of(core) if c != core and topo.die(c) == topo.die(core)]
    senders = [c for c in beside if topo.may_write(c, mate[0])]
    return senders, [c for c in beside if c not in senders], [c for c in mate if topo.may_write(c, core)]


def joiner(rank, t, c, T, topo):
    senders, own, mate = helpers(T.cores[rank], T, topo)
    return own[0] if (t, c) in OWN_PLANE else mate[c // 2 % 2]


def v(name, *idx):
    if name in PACKED:
        whole, first, width = PACKED[name]
        a, b, c = (idx[1] if len(idx) > 1 else ALL).indices(width)
        return ("v", whole, (idx[0] if idx else ALL, slice(first + a, first + b, c if c > 1 else None)))
    return ("v", name, idx if idx else (ALL,))


def ind(win, off):
    return ("i", win, off)


def is_view(x):
    return isinstance(x, tuple) and len(x) == 3 and x[0] in ("v", "i")


def region(view):
    name, idx = view[1], view[2]
    shape = SCRATCH[name][1]
    key = (name, str(idx))
    if key not in MASKS:
        a, b, c = idx[0].indices(shape[0])
        n = int(np.prod(shape[1:]))
        sel = np.arange(n).reshape(shape[1:])[tuple(idx[1:])] if len(idx) > 1 else np.arange(n)
        m = np.zeros(n, bool)
        m[np.asarray(sel).ravel()] = True
        bank = 0
        if SCRATCH[name][0] == "psum":
            for k in range(n // 512):
                if m[k * 512:(k + 1) * 512].any():
                    bank |= 1 << k
        MASKS[key] = (a, b, int.from_bytes(np.packbits(m).tobytes(), "big"), bank)
    return MASKS[key]


def size(x):
    if x[0] == "i":
        return 16 * size(x[2])[0], False
    return bin(region(x)[2]).count("1"), SCRATCH[x[1]][2] in ("bfloat16", "uint16")


def flow(g, T):
    queues = {"v": g.vector, "s": g.scalar, "p": g.tensor, "g": g, "y": g.sync}
    known = {q: {} for q in queues}
    total, acc, ops, banks = {}, {}, [], [{} for _ in range(8)]
    gate = []
    lazy = [False]

    def ap(x):
        if x[0] == "i":
            return ap(x[1]).indirect(ap(x[2]))
        t = T[x[1]]
        return t[x[2] if len(x[2]) > 1 else x[2][0]]

    def parts(x):
        return [x] if x[0] == "v" else [x[1], x[2]]

    def each(reads, writes):
        for kind, xs in (("r", reads), ("w", writes)):
            for x in xs:
                if x[1] in SCRATCH:
                    yield kind, x[1], region(x)

    def add(q, reads, writes, go, sem, n, busy, late=0.0, after=()):
        me, dep = len(ops), {k: q != "g" or ops[k]["q"] != "g" for k in after}
        for kind, name, (p0, p1, m, bank) in each(reads, writes):
            if bank:
                for b in range(8):
                    if bank >> b & 1:
                        for who, k in banks[b].items():
                            if k != me:
                                dep[k] = dep.get(k, False) or who != q
                        banks[b][q] = me
                continue
            old = acc.get(name, [])
            for e in old:
                if (kind == "w" or e["kind"] == "w") and e["p0"] < p1 and p0 < e["p1"] and (m & e["m"]) and e["op"] != me:
                    dep[e["op"]] = True
            if kind == "w":
                old = [e for e in old if not (p0 <= e["p0"] and e["p1"] <= p1 and (e["m"] & ~m) == 0)]
            acc[name] = old + [{"kind": kind, "p0": p0, "p1": p1, "m": m, "op": me}]
        for k in gate:
            dep.setdefault(k, ops[k]["q"] != q)
        ops.append({"lazy": lazy[0] and q is not None, "q": q, "go": go, "sem": sem, "n": n, "busy": busy, "late": late, "dep": dep})
        return me

    def order():
        n = len(ops)
        before = [[(d, ops[d]["late"] + WAKE if hard else 0.0) for d, hard in o["dep"].items()] for o in ops]
        chain, tail = [list(b) for b in before], {}
        for k, o in enumerate(ops):
            if o["q"] in ("v", "s", "g") and not o["lazy"]:
                if o["q"] in tail:
                    chain[k].append((tail[o["q"]], 0.0))
                tail[o["q"]] = k

        def run(needs, rank_, busy):
            behind, left, ready, start = [[] for _ in ops], [len(x) for x in needs], [0.0] * n, [0.0] * n
            for k in range(n):
                for d, lag in needs[k]:
                    behind[d].append((k, lag))
            free = {q: 0.0 for q in list(queues) + [None]}
            pool = {q: [k for k in range(n) if ops[k]["q"] == q and not left[k]] for q in free}
            out = []
            while len(out) < n:
                now, q = min(((max(free[q], min(ready[k] for k in pool[q])), q) for q in pool if pool[q]), key=lambda x: x[0])
                k = min((k for k in pool[q] if ready[k] <= now), key=rank_)
                pool[q].remove(k)
                out.append(k)
                start[k] = now
                if q is not None:
                    free[q] = now + busy[k]
                for u, lag in behind[k]:
                    ready[u] = max(ready[u], now + busy[k] + lag)
                    left[u] -= 1
                    if not left[u]:
                        pool[ops[u]["q"]].append(u)
            return out, start, behind

        busy = [o["busy"] for o in ops]
        way = [o["late"] for o in ops]
        for k in range(n - 1, -1, -1):
            way[k] += 0.0 if ops[k]["lazy"] else busy[k]
            for d, lag in chain[k]:
                way[d] = max(way[d], way[k] + lag)
        out, start, behind = run(chain, lambda k: (-way[k], k), [0.0 if o["lazy"] else o["busy"] for o in ops])
        due = [1e9] * n
        for k in range(n - 1, -1, -1):
            if ops[k]["lazy"]:
                due[k] = min([1e9] + [(due[u] if ops[u]["lazy"] else start[u]) - lag for u, lag in behind[k]]) - busy[k]
        taken = {q: sorted((start[k] - (SLACK if q == "g" and ops[k]["late"] else 0.0), start[k] + busy[k])
                           for k in range(n) if ops[k]["q"] == q and not ops[k]["lazy"]) for q in queues}
        for k in sorted(range(n), key=lambda k: (due[k], k)):
            if ops[k]["lazy"]:
                t = first = max([0.0] + [start[d] + busy[d] + lag + (SLACK if ops[d]["q"] == "g" != ops[k]["q"] and ops[d]["lazy"] else 0.0) for d, lag in before[k]])
                for a, b in taken[ops[k]["q"]]:
                    if b > t:
                        if a >= t + busy[k]:
                            break
                        t = b
                if t > due[k]:
                    t = max(first, due[k])
                start[k] = t
                taken[ops[k]["q"]] = sorted(taken[ops[k]["q"]] + [(t, t + busy[k])])
        done, out = [False] * n, []

        def emit(k):
            todo = [k]
            while todo:
                j = todo[-1]
                need = [d for d, lag in chain[j] if not done[d]]
                if need:
                    todo.append(min(need, key=lambda d: start[d]))
                else:
                    todo.pop()
                    if not done[j]:
                        done[j] = True
                        out.append(j)

        for k in sorted(range(n), key=lambda k: (start[k], k)):
            emit(k)
        return out

    def settle(q, ev):
        need = {}
        for sem, cnt, clk in ev:
            if sem not in need or need[sem][0] < cnt:
                need[sem] = (cnt, clk)
        for sem in sorted(need, key=lambda s: -sum(need[s][1].values())):
            cnt, clk = need[sem]
            if known[q].get(sem, 0) >= cnt:
                continue
            queues[q].wait_ge(T.sem[sem], cnt)
            for k in clk:
                known[q][k] = max(known[q].get(k, 0), clk[k])
            known[q][sem] = max(known[q].get(sem, 0), cnt)

    def cost(q, meth, kw):
        out = kw.get("out") or kw["ap"]
        n, views = size(out)[0], [kw[k] for k in kw if is_view(kw[k])]
        if meth == "matmul":
            return max(min(64, size(kw["lhsT"])[0]), n) * TENSOR * (1 if size(kw["rhs"])[1] else 4)
        if q == "g":
            return 150 + 2 * n * CYCLE
        if out[0] == "i":
            return 50 + 3.8 * n * CYCLE
        if any(x[0] == "i" for x in views):
            return 60 + (FUSED if meth == "tensor_tensor" else 1.56) * n * CYCLE
        if meth == "tensor_tensor":
            return CALL + max(64, n * (1 if any(x[1] == "psb" for x in views) else 2)) * CYCLE
        narrow = q == "v" and all(size(x)[1] or size(x)[0] == 1 for x in views)
        return CALL + max(64, n / 2 if narrow else n) * CYCLE

    def call(q, meth, **kw):
        reads, writes = [], []
        for k in kw:
            x = kw[k]
            if is_view(x):
                if k in WRITES:
                    writes.append(parts(x)[0])
                    reads += parts(x)[1:]
                else:
                    reads += parts(x)
        args = {k: (ap(kw[k]) if is_view(kw[k]) else kw[k]) for k in kw}
        eng = queues[q]
        f = {"tensor_copy": lambda: eng.tensor_copy(**args), "tensor_tensor": lambda: eng.tensor_tensor(**args),
             "tensor_scalar": lambda: eng.tensor_scalar(**args), "scan": lambda: eng.tensor_tensor_scan(**args),
             "memset": lambda: eng.memset(args["ap"], args["constant"]),
             "activation": lambda: eng.activation(**args), "matmul": lambda: eng.matmul(**args),
             "affine_select": lambda: eng.affine_select(**args), "tensor_reduce": lambda: eng.tensor_reduce(**args),
             "iota": lambda: eng.iota(**args)}[meth]
        return add(q, reads, writes, lambda: f().then_inc(T.sem[ENG[q]], 1), ENG[q], 1, cost(q, meth, kw))

    def dma(q, sem, out, in_, late, after, behind):
        k = add(q, [in_], [out], lambda: queues[q].dma_start(out=ap(out), in_=ap(in_)).then_inc(T.sem[sem], 16), sem, 16, 60, late, after)
        if behind is not None:
            ops[k]["dep"].setdefault(behind, False)
        return k

    def arrive(outs, sem, cnt, mine, late=0):
        return add(None, [], outs, None, sem, cnt, 0, late, mine)

    def fused(transfers, late, after=(), local="lsem"):
        go = lambda: g.remote_dma_fused(
            [RemoteDMATransfer(dst_ids=[d[0] for d in t[1]], dma_engine_mask=bits(t[2]), remote_sem=T.sem[t[3]],
                               srcs=[ap(t[0])], dsts=[ap(d[1]) for d in t[1]]) for t in transfers], local_sem=T.sem[local])
        return add("g", [t[0] for t in transfers], [], go, local, sum(len(t[2]) for t in transfers), ISSUE, late, after)

    def finish():
        event = {}
        for k in order():
            q, sem = ops[k]["q"], ops[k]["sem"]
            total[sem] = total.get(sem, 0) + ops[k]["n"]
            if q is None:
                event[k] = (sem, total[sem], {sem: total[sem]})
                continue
            settle(q, [event[d] for d, hard in ops[k]["dep"].items() if hard])
            ops[k]["go"]()
            event[k] = (sem, total[sem], dict(known[q], **{sem: total[sem]}))
        for sem in total:
            if known["g"].get(sem, 0) < total[sem]:
                g.wait_ge(T.sem[sem], total[sem])

    return {"call": call, "dma": dma, "arrive": arrive, "fused": fused, "finish": finish, "gate": gate, "lazy": lazy, "last": lambda: len(ops) - 1}


def blk(name, k, n=128):
    return v(name, slice(n * k, n * k + n), ALL)


def cols(name, a, b, step=None):
    return v(name, ALL, slice(a, b, step))


def rows(name, n, a, b, step=None):
    return v(name, slice(0, n), slice(a, b, step))


def carry_engines(core, t, c, T, topo):
    every = topo.engines(core, helpers(core, T, topo)[0][0])
    call = [x for x in CARRY[t] if c in x][0]
    n = len(every) // len(call)
    return every[n * call.index(c):n * call.index(c) + n]


def sender_main(g, core, rank, j, T, topo):
    mine = range(j, 2 * NCH, 2)
    for s in mine:
        t, c = 1 + s // NCH, s % NCH
        g.sync.wait_ge(T.sem["a_c%d" % s], len(carry_engines(T.cores[rank], t, c, T, topo)))
        g.sync.dma_start(out=T["hp"][1024 * s:1024 * s + 1024, :], in_=T["hc"][128 * s:128 * s + 128, :]).then_inc(T.sem["d%d" % s], 16)
        g.wait_ge(T.sem["d%d" % s], 16)
        dst = [joiner(asker(rank, k, t), t, c, T, topo) for k in range(NG)]
        eng = singles(core, dst, T, topo)
        part = lambda name, k: T[name][1024 * s + 128 * k:1024 * s + 128 * k + 128, :]
        g.remote_dma_fused([RemoteDMATransfer(dst_ids=[dst_id(topo, dst[k])], dma_engine_mask=bits([eng[k]]), remote_sem=T.sem["a_p%d" % s],
                                              srcs=[part("hp", k)], dsts=[part("ha", k)]) for k in range(NG)], local_sem=T.sem["lsem"])
    g.wait_ge(T.sem["lsem"], NG * len(mine))


def joiner_main(g, core, rank, jobs, T, topo):
    dst, left = T.cores[rank], 0
    for k, (t, c) in enumerate(jobs):
        slot = NCH * (t - 1) + c
        g.sync.wait_ge(T.sem["a_p%d" % slot], NG)
        g.sync.dma_start(out=T["gth"][:, CH * k:CH * k + CH], in_=T["ha"][1024 * slot:1024 * slot + 1024, :]).then_inc(T.sem["d%d" % k], 16)
    for k, (t, c) in enumerate(jobs):
        g.wait_ge(T.sem["d%d" % k], 16)
        g.remote_dma_fused([RemoteDMATransfer(dst_ids=[dst_id(topo, dst)], dma_engine_mask=topo.mask(core, dst), remote_sem=T.sem["a_f%d" % t],
                                              srcs=[T["gth"][:, CH * k:CH * k + CH]], dsts=[T["tf%d" % t][:, CH * c:CH * c + CH]])],
                           local_sem=T.sem["lsem"])
        left += len(topo.engines(core, dst))
    g.wait_ge(T.sem["lsem"], left)


def rank_main(g, core, rank, T, topo):
    F = flow(g, T)
    C, arrive, fused = F["call"], F["arrive"], F["fused"]
    ps = lambda a, b, n=128, step=None: v("psb", slice(0, n), slice(a, b, step))
    B = [512 * k for k in range(8)]
    KH, OWN, LW, KF, PS, R = B[3], B[3] + 256, B[3] + 272, (B[6], B[7]), (B[6], B[7]), B[2]
    nd, turn, last, sent, gate, lazy = [0], [0], {}, {}, F["gate"], F["lazy"]
    setup = [False]

    def bank():
        turn[0] += 1
        return B[turn[0] % 3]

    def dma(q, out, in_, late=SHORT, after=()):
        nd[0] += 1
        last[q] = F["dma"](q, "d%d" % nd[0], out, in_, late, after, last.get(q))
        return last[q]

    def act(out, in_, func=AF.Copy, **kw):
        return C("s", "activation", out=out, in_=in_, func=func, **kw)

    real = lambda *xs: all(SCRATCH[x[1]][2] in ("float32", "bfloat16") for x in xs)

    def copy(q, out, in_):
        if q == "s" or (setup[0] and real(out, in_)):
            return act(out, in_)
        return C("v", "tensor_copy", out=out, in_=in_)

    def tt(out, a, b, op):
        return C("v", "tensor_tensor", out=out, in0=a, in1=b, op=op)

    def ts(out, a, s1, op, s2=None, op1=None):
        if setup[0] and real(out, a) and (op, op1) in ((A.mult, A.add), (A.mult, None), (A.add, None)):
            return act(out, a, AF.Identity, scale=s1 if op == A.mult else 1.0, bias=s1 if op == A.add else s2 or 0.0)
        if op1 is None:
            return C("v", "tensor_scalar", out=out, in0=a, scalar1=s1, scalar2=None, op0=op)
        return C("v", "tensor_scalar", out=out, in0=a, scalar1=s1, scalar2=s2, op0=op, op1=op1)

    def mm(out, lhsT, rhs, start=True, stop=True):
        return C("p", "matmul", out=out, lhsT=lhsT, rhs=rhs, start=start, stop=stop)

    def scan(out, d0, d1, op):
        return C("v", "scan", out=out, data0=d0, data1=d1, initial=0.0, op0=A.mult, op1=op)

    def fill(x, c):
        C("v", "memset", ap=x, constant=c)

    def keep(out, in_, op, base, ch, pattern, other=0.0):
        C("g", "affine_select", out=out, in_=in_, pattern=pattern, compare_op=op, fill=other, base=base, channel_multiplier=ch)

    def iota(out, pattern, base, ch):
        if SCRATCH[out[1]][2] == "int32":
            C("g", "iota", out=out, pattern=pattern, base=base, channel_multiplier=ch)
        else:
            C("g", "iota", out=out, pattern=pattern, base=base, channel_multiplier=ch, allow_small_or_imprecise_dtypes=True)

    def by_group(src, land, dst, sem, late, after=()):
        eng = singles(core, dst, T, topo)
        mine = fused([(blk(src, k), [(dst_id(topo, dst[k]), blk(land, k))], [eng[k]], sem) for k in range(NG)], late, after)
        arrive([v(land)], sem, NG, [mine])
        return mine

    far = far_engines(core, T, topo)

    def tell(src, land, sem, after=()):
        away = [c for c in T.cores if off_chip(topo, core, c)]
        near = [c for c in T.cores if c != core and c not in away]
        mine = fused([(src, [(dst_id(topo, d), cols(land, 16 * rank, 16 * rank + 16)) for d in ds], en, sem)
                      for ds, en in ((away, far), (near, near_engines(core, near[0], T, topo)))], TELL, after)
        told = sum(len(far) if c in away else len(near_engines(c, core, T, topo)) for c in away + near)
        return arrive([cols(land, 16 * r, 16 * r + 16) for r in range(N) if r != rank], sem, told, [mine])

    to_asked = lambda t: [T.cores[asked(rank, k, t)] for k in range(NG)]
    to_asker = lambda t: [T.cores[asker(rank, k, t)] for k in range(NG)]
    half = lambda name, h: cols(name, 128 * h, 128 * h + 128)

    dma("y", v("ed0"), v("ef", ALL, slice(0, NL)), 1800)
    dma("s", v("zd0"), v("zf", ALL, slice(0, NL)))
    dma("s", cols("z_s", 64, 320), v("zf", ALL, slice(0, NL)), 2000)
    dma("y", cols("eh_s", 64, 320), v("eh", ALL, slice(0, NL)), 2900)
    dma("y", cols("tb", 0, NS), v("tab"), LOAD)

    iota(v("pi"), [[0, 8]], 0, 1)
    iota(v("rr"), [[1, NL]], 0, 0)
    by_group("zd0", "zl0", to_asked(0), "a_z0", ASKZ)
    sent["q0"] = by_group("ed0", "rl0", to_asked(0), "a_q0", ASK0)
    iota(v("each"), [[1, 32], [0, 16]], 0, 0)
    by16 = lambda s, n=8: [[s, n], [0, 16]]
    C("v", "memset", ap=v("ob"), constant=1.0)
    lazy[0] = True
    keep(v("rsel"), half("ob", 0), A.is_ge, 0, 1, by16(-4))
    keep(v("rsel"), v("rsel"), A.is_ge, 2, -1, by16(4))
    keep(v("osr"), v("rsel"), A.not_equal, -2, 1, by16(-4))
    iota(v("m16"), [[0, 16], [1, 16]], 0, 0)
    iota(cols("tmp", 0, 6), [[128, 6]], DUMP, 1)
    for a, b, c in ((0, 48, 0), (48, 80, 600), (80, 96, DUMP)):
        iota(cols("yw", a, b), [[16, b - a]], c, 0)

    PC = {n: cols("pc", k, k + 1) for k, n in enumerate("p a g ck y nu v0 v1 b3 ia l c15 m0 m1 m2 m3 m01 m80 w thr".split())}
    pint = cols("pi", 0, 1)

    def bitcol(out, sh, mask, k):
        ts(cols("hki", k, k + 1), pint, sh, A.arith_shift_right, mask, A.bitwise_and)
        copy("v", out, cols("hki", k, k + 1))

    lazy[0] = True
    copy("v", PC["p"], pint)
    bitcol(PC["a"], 0, 15, 0)
    bitcol(PC["g"], 4, 7, 1)
    ts(PC["ck"], PC["a"], -8192.0, A.mult, 122880.0, A.add)
    C("v", "memset", ap=v("zb"), constant=0.0)
    ts(v("id32"), cols("rr", 0, 128), PC["p"], A.is_equal)
    ts(v("idb"), cols("rr", 0, 128), PC["p"], A.is_equal)
    for x, w in enumerate((1.0, 0.5, 131072.0, 65536.0)):
        ts(cols("blk", 8 * x, 8 * x + 8), cols("rr", 0, 8), PC["g"], A.is_equal, w, A.mult)
    bitcol(PC["l"], 0, 31, 4)
    ts(v("each"), v("each"), PC["l"], A.is_equal, -1.0, A.mult)
    ts(v("xp0"), cols("eh_s", 64, 320), PC["ck"], A.add)
    copy("v", v("oh0"), cols("eh_s", 64, 320))
    fill(cols("mid", 128, NL), 8 * 131072)
    fill(cols("mid", 0, 128), 8)

    def lookups(t, plan=None):
        plan = (plan or PLAN[t]).split()
        y0 = (64, 0, 704)[t]
        begun = set()
        for at, x in enumerate(plan):
            what = x.split(":")
            if what[0] in STAGE:
                STAGE[what[0]](t, *[int(y) for y in what[1:]])
                continue
            kind, tab, a, b = x[0], x[1], int(what[1]), int(what[2])
            n, h, p0 = b - a, a // 128, a % 128
            if t == 0:
                z = cols("z_s", 64 + a, 64 + b) if tab == "h" else cols("zlf", a, b)
            else:
                z = cols("zl%d" % t, a, b) if b > FIX else cols("z_s", y0 + a, y0 + b)
            zr, zt = ("zrf", "ztf") if t == 0 and tab == "f" else ("zrh", "zt%d" % t)
            got = lambda x, y: ind(cols("tb" if tab == "h" or t == 0 else "tf%d" % t, 0, DUMP if t else NS), cols("o%s%d" % (tab, t), x, y))
            if kind == "z":
                for k in range(16):
                    copy(what[3], cols(zr, 16 * a + k, 16 * b, 16), z)
            elif kind == "v":
                tt(cols("cv" + tab, 16 * a, 16 * b), got(a, b), cols(zr, 16 * a, 16 * b), A.is_le)
            elif kind == "g":
                act(cols("gt" + tab, 16 * a, 16 * b), got(a, b))
            elif kind == "s":
                for x in range(a, b, 32):
                    bk, part = bank(), slice(x % 128, x % 128 + 32)
                    mm(ps(bk, bk + 512), v(zt, part, slice(128 * h, 128 * h + 128)), v("each", part, ALL), True, False)
                    mm(ps(bk, bk + 512), v("idb"), cols("gt" + tab, 16 * x, 16 * x + 512), False, True)
                    act(cols("cv" + tab, 16 * x, 16 * x + 512), ps(bk, bk + 512), AF.Sign, scale=-1.0, bias=0.5)
            elif kind == "t":
                bk = bank()
                out = v("psb", slice(p0, p0 + n), slice(bk, bk + 128))
                mm(out, z, v("idb"))
                copy(what[3], v(zt, slice(p0, p0 + n), slice(128 * h, 128 * h + 128)), out)
            else:
                wide = tab == "f" and t > 0
                base, step = (KF[h], 17) if wide else ((KH if tab == "h" else KF[0]) + 128 * h, 16)
                out = lambda x, y, s=None: v("psb", slice(p0, p0 + n), slice(base + x, base + y, s))
                start = tab == "f" or not begun
                later = [[int(z) % 128 for z in y.split(":")[1:3]] for y in plan[at + 1:] if y[:2] == "mh"]
                stop = tab == "f" or not any(c < p0 + n and p0 < (d or 128) for c, d in later)
                if tab == "h" and h not in begun:
                    begun.add(h)
                    mm(ps(base, base + 128), half("xp%d" % t, h), v("id32"), start, False)
                    start = False
                if what[3] == "s":
                    mm(out(0, 8 * step), rows("ob", 1, 0, n),
                       rows("md2", 1, 0, 136) if wide else rows("mid", 1, 128, NL) if tab == "h" else rows("mid", 1, 0, 128), start, False)
                    start = False
                w = 8 * ("fv", "fs", "hv", "hs").index(tab + what[3])
                for k in range(16):
                    mm(out(k, 8 * step, step), cols("cv" + tab, 16 * a + k, 16 * b, 16), cols("blk", w, w + 8), start and k == 0, stop and k == 15)

    def choose(t):
        scan(v("kh"), v("rst"), ps(KH, KH + NL), A.max)
        copy("v", v("hki"), cols("kh", 15, NL, 16))
        ts(v("di", ALL, ALL, 0), v("hki"), NS - 64, A.bitwise_and)
        ts(v("di", ALL, ALL, 1), v("hki"), 63, A.bitwise_and)
        ts(v("di", ALL, ALL, 3), v("hki"), 17, A.arith_shift_right)
        copy("v", v("cd"), v("di"))
        for h in range(2):
            mm(ps(KH + 128 * h, KH + 128 * h + 128, 32), v("cd", ALL, slice(8 * h, 8 * h + 8), ALL), v("idb"))

    def chosen(t):
        copy("s" if ON_SCALAR[t] else "v", rows("st", 32, 0, NL), ps(KH, KH + NL, 32))
        for h in range(2):
            mm(ps(OWN + 8 * h, OWN + 8 * h + 8), rows("st", 32, 128 * h, 128 * h + 128), v("osr", slice(0, 32), ALL, 0))
        if ON_SCALAR[t]:
            copy("s", v("own"), ps(OWN, OWN + 16))
        sent["c%d" % t] = F["last"]()
        if t == 0:
            for h in range(2):
                mm(ps(R + 128 * h, R + 128 * h + 128), rows("st", 32, 128 * h, 128 * h + 128), rows("wsel", 32, 0, 128))
            act(v("whr"), ps(R, R + NL))

    def alike(t, first=0, end=NG):
        for k in range(first, end):
            a = bank() if k in ON_SCALAR[t] else B[4 + k % 2]
            mm(ps(a, a + NL), v("sg", slice(0, 32), k, ALL), rows("st", 32, 0, NL))
            for h, x, y in ((1, 0, 128), (0, 128, 384)):
                own = cols("own", 8 * h + k, 8 * h + k + 1) if ON_SCALAR[t] else ps(OWN + 8 * h + k, OWN + 8 * h + k + 1)
                if k in ON_SCALAR[t]:
                    act(cols("gth", 384 * k + x, 384 * k + y), ps(a + 128 * h, a + NL), AF.Abs, scale=-1.0, bias=own)
                else:
                    ts(v("eq", ALL, k, slice(x, y)), ps(a + 128 * h, a + NL), own, A.is_equal)
            if k in ON_SCALAR[t]:
                act(v("eq", ALL, k, ALL), cols("gth", 384 * k, 384 * k + 384), AF.Relu, scale=-1.0, bias=1.0)

    def answer(t):
        scan(v("kf"), v("rst"), ps(KF[0], KF[0] + NL), A.max)
        sent["a0"] = copy("v", v("wq"), cols("kf", 15, NL, 16))
        sent["r0"] = tell(v("wq"), "lr0", "a_r0")

    SLOT = lambda t, h: B[4 + h] if t else B[h]

    def fin(t, h):
        if t == 0:
            w = half("wr0", h)
            tt(w, ind(v("lr0"), cols("lrep", 8 * h, 8 * h + 8)), half("whr", h), A.max)
        else:
            mm(ps(KF[h] + 16, KF[h] + 136, 128, 17), v("idb"), v("cd", ALL, slice(8 * h, 8 * h + 8), 3))
            scan(cols("kf%d" % h, 0, 136), cols("rs2", 0, 136), ps(KF[h], KF[h] + 136), A.max)
            w = ind(cols("kf%d" % h, 0, 136), cols("lrep", 16, 24))
        ts(half("cl", h), w, 8.0, A.is_lt, PC["w"], A.mult)
        if h == 0 and t == 0:
            ts(v("clb"), w, 8.0, A.is_lt, TOP, A.mult)
        elif h == 0:
            act(v("clb"), w, AF.Relu, scale=-TOP, bias=8 * TOP)
        act(half("rl", h), w, AF.Relu, bias=-8.0)
        for at, (c, cl) in enumerate(((128, half("cl", 0)),) if h == 0 else ((256, v("clb")), (0, half("cl", 1)))):
            last_ = h == 0 or at == 1
            if last_:
                mm(ps(PS[h], PS[h] + 128), v("i4n"), half("cl", h), h == 0, False)
            for k in range(NG):
                mm(ps(PS[h] + 16 * k, PS[h] + 16 * k + 16), v("eq", ALL, k, slice(c, c + 128)), v(cl[1], ALL, slice(cl[2][1].start + 16 * k, cl[2][1].start + 16 * k + 16)),
                   k == 0 and not last_, last_ and k == NG - 1)
        mm(ps(SLOT(t, h), SLOT(t, h) + 128), rows("st", 32, 128 * h, 128 * h + 128), v("osr", slice(0, 32), ALL, ALL), True, False)

    def scatter(table, lists, vals):
        return copy("v", ind(v(table), cols(lists, 0, 16)), vals)

    def wrap(table, q="s"):
        copy(q, cols(table, NS, DUMP), cols(table, 0, WR))

    def renew(table, lu, la, pick, vals):
        copy("v", v(lu), ind(v(la), cols("lst", pick, pick + 1)))
        scatter(table, lu, v(vals))

    def update(t):
        if t == 1:
            renew("tf1", "lu1", "la0", 0, "zu1")
        else:
            renew("tf2", "lu3", "la1", 2, "zu3")
        wrap("tf%d" % t, "v")

    STAGE = {"choose": choose, "chosen": chosen, "alike": alike, "answer": answer, "fin": fin, "update": update}

    def growth(t):
        mm(ps(R, R + NL), rows("mid", 1, 0, 128), rows("ob", 1, 0, NL), True, False)
        for h in range(2):
            o = ps(R + 128 * h, R + 128 * h + 128)
            mm(o, half("rl", h), v("idb"), False, False)
            mm(o, half("cl", h), v("i8n"), False, t != 1 and h == 1)

    def decide(t):
        for h in range(2):
            ts(half("zz", h), ps(PS[h], PS[h] + 128), PC["thr"], A.is_ge, BIG, A.mult)
            mm(ps(SLOT(t, h), SLOT(t, h) + 128), v("idb"), half("zz", h), False, True)
        for h in range(2):
            tt(half("xx", h), ps(SLOT(t, h), SLOT(t, h) + 128), cols("dm", NL * t + 128 * h, NL * t + 128 * h + 128), A.min)
            mm(ps(LW + 8 * h, LW + 8 * h + 8), half("xx", h), v("sel"))
            if t == 0:
                act(half("sgn", h), half("zz", h), AF.Sign, bias=-1.0)
            if t == 1:
                act(v("ut", ALL, slice(8 * h, 8 * h + 8), 3), cols("zz", 128 * h, 128 * h + 128, 16), AF.Sign, bias=-1.0)
                mm(ps(R + 128 * h, R + 128 * h + 128), v("ut", ALL, slice(8 * h, 8 * h + 8), ALL), v("i8k"), False, h == 1)
        copy("v", cols("w%d" % t, 0, 16), ps(LW, LW + 16))

    def report(t):
        act(cols("msg", 16 * t, 16 * t + 16), ps(LW, LW + 16))
        sent["u%d" % t] = tell(cols("msg", 16 * t, 16 * t + 16), "la%d" % t, "a_u%d" % t)

    def wrapped(a, n, el, src, first, start=True, stop=True):
        for i in range(16):
            mm(ps(a, a + n), cols(el, 15 - i, 143 - i), cols(src, first + i, first + 16 * n, 16), start and i == 0, stop and i == 15)

    one, zero = half("ob", 0), half("zb", 0)
    line, in16 = lambda s, n=128: [[s, n]], lambda n=8: [[0, n], [1, 16]]
    keep(v("rst"), v("ob"), A.not_equal, 0, 0, in16(16))
    fill(v("di", ALL, ALL, 2), 0)
    for k in range(8):
        ts(v("sg", slice(0, 32), k, ALL), rows("ob", 32, 0, 128), v("osr", slice(0, 32), k, slice(0, 1)), A.mult)
    keep(v("wsel"), one, A.is_equal, -3, 1, by16(-4))
    for name, c in (("i4n", -4.0), ("i8k", -BIG), ("idn", -1.0)):
        keep(v(name), zero, A.not_equal, 0, 1, line(-1), c)
    for h, (first, step) in enumerate(((TOP, 0.5), (-8.0 / TOP, 2.0))):
        C("v", "memset", ap=half("xq", h), constant=step)
        C("v", "scan", out=half("xx", h), data0=half("xq", h), data1=zero, initial=first, op0=A.mult, op1=A.add)
    tt(v("i8n"), half("xx", 1), v("idb"), A.mult)
    tt(half("xq", 0), half("xx", 0), v("id32"), A.mult)
    C("v", "tensor_reduce", out=PC["w"], in_=half("xq", 0), axis=AxisListType.X, op=A.add)
    ts(PC["thr"], PC["w"], -1.5, A.mult)
    ts(v("sel"), cols("rr", 0, 8), PC["g"], A.is_equal)
    ts(v("tri2"), cols("rr", 0, 128), PC["p"], A.is_gt, 0.5, A.mult)
    keep(v("tri"), zero, A.is_ge, 0, 1, line(-1), 1.0 / 32)
    keep(v("tri"), v("tri"), A.not_equal, 0, 1, line(-1), -1.0 / 64)
    keep(v("o32"), zero, A.is_gt, 0, 0, line(0), 1.0 / 32)
    keep(v("o2"), zero, A.is_gt, 0, 0, line(0), 0.5)
    iota(v("crow"), [[128, 2], [0, 8], [-2, 16]], 1, 0)
    iota(v("crow2"), [[64, 2], [0, 8], [-16, 16]], -8, 0)
    iota(cols("pc", 6, 8), [[-128, 2]], 256, -1)
    ts(PC["b3"], PC["a"], 3.0, A.is_equal, BIG, A.mult)
    ts(PC["ia"], PC["a"], 16.0, A.mult, 72.0, A.add)
    ts(v("m16"), v("m16"), PC["a"], A.is_equal)
    for x in range(6):
        act(cols("dm", 128 * x, 128 * x + 128), half("m16", 0), AF.Identity, scale=cols("tmp", x, x + 1))
    fill(v("apad", ALL, ALL, 1, ALL), 0)
    act(v("yw"), v("yw"), AF.Identity, bias=PC["a"])
    copy("v", cols("w1", 16, 20), cols("yw", 0, 4))
    copy("v", cols("inv1", 0, 4), cols("yw", 0, 4))
    copy("v", cols("w2", 16, 20), cols("yw", 44, 48))
    copy("v", cols("inv2", 44, 48), cols("yw", 0, 4))
    iota(cols("md2", 0, 136), [[0, 136]], 8, 0)
    keep(cols("md2", 0, 136), cols("md2", 0, 136), A.not_equal, -16, 0, [[0, 8], [1, 17]])
    keep(cols("rs2", 0, 136), cols("ob", 0, 136), A.not_equal, 0, 0, [[0, 8], [1, 17]])
    iota(v("ut"), [[0, NL]], 0, 0)
    keep(v("onb"), one, A.is_ge, 0, 1, by16(-16))
    keep(v("onb"), v("onb"), A.is_ge, 15, -1, by16(16))
    keep(v("onb1"), v("onb"), A.is_equal, -1, 0, in16())
    keep(v("ntr"), zero, A.is_ge, 0, -1, line(1), -1.0)
    keep(v("ntr"), v("ntr"), A.is_ge, 15, -1, by16(16))
    keep(v("ex2"), one, A.is_equal, -2, 1, by16(-16))
    ts(cols("pc", 12, 16), cols("rr", 0, 4), PC["a"], A.is_equal)
    ts(PC["m01"], PC["a"], 2.0, A.is_lt)
    ts(PC["c15"], PC["g"], 16.0, A.mult, 15.0, A.add)
    ts(PC["m80"], PC["m0"], -80.0, A.mult)
    for name, m in (("el", "m01"), ("el3", "m3"), ("eln", "m80")):
        ts(v(name), cols("rr", 0, 144), PC["c15"], A.is_equal, PC[m], A.mult)
    ts(v("mk2"), v("idb"), PC["m2"], A.mult)
    ts(cols("pc", 20, 23), cols("rr", 0, 3), PC["m0"], A.mult, float(NL), A.mult)
    for x in range(3):
        act(cols("pay", NL * x, NL * x + NL), v("rr"), AF.Identity, scale=PC["m1"], bias=cols("pc", 20 + x, 21 + x))
    for a, b, c in ((0, 64, 704.0), (64, 320, 0.0), (320, 576, 256.0), (576, NF, 512.0)):
        act(cols("idf", a, b), cols("rr", 0, b - a), AF.Identity, bias=c)
    for h in range(2):
        runs = [k for k in range(NG) if k == 0 or asked(rank, k, 0) != asked(rank, k - 1, 0) + 1] + [NG]
        for a, b in zip(runs, runs[1:]):
            iota(cols("ri", 8 * h + a, 8 * h + b), [[17, b - a]], 16 * asked(rank, a, 0) + 8 * h + a, 0)
    iota(cols("ri", 16, 24), line(17, 8), 16, 0)
    copy("v", cols("lrep", 0, 24), cols("ri", 0, 24))
    ts(cols("hki", 0, 2), cols("rr", 1, 3), PC["g"], A.add)
    ts(cols("hki", 8, 10), cols("hki", 0, 2), float(N - 1), A.is_ge, -float(N - 1), A.mult)
    tt(cols("hki", 0, 2), cols("hki", 0, 2), cols("hki", 8, 10), A.add)
    ts(cols("hki", 0, 2), cols("hki", 0, 2), float(rank + 1), A.add)
    ts(cols("hki", 0, 2), cols("hki", 0, 2), N - 1, A.bitwise_and)
    ts(cols("lst", 0, 4, 2), cols("hki", 0, 2), 16.0, A.mult, PC["a"], A.add)
    for x in [cols(name, 16 * rank, 16 * rank + 16) for name in ("lr0", "la0", "la1")] + [cols(name, NL, ZC) for name in ("r1", "r2", "r3")]:
        iota(x, [[0, 16]], 0, 0)
    lazy[0] = False

    senders = helpers(core, T, topo)[0]

    def carry(t, after=()):
        for call in CARRY[t]:
            mine = fused([(cols("tb", CH * x, CH * x + CH), [(dst_id(topo, senders[x % 2]), blk("hc", NCH * (t - 1) + x))],
                           carry_engines(core, t, x, T, topo), "a_c%d" % (NCH * (t - 1) + x)) for x in call], 4000, after if call[0] == NCH // 2 else (), "ltab")
        arrive([cols("tf%d" % t, 0, NS)], "a_f%d" % t, sum(len(topo.engines(joiner(rank, t, c, T, topo), core)) for c in range(NCH)), [mine], TABLE)

    asks = [dma("y", v("zlf"), v("zl0")), dma("y", v("efq0"), v("rl0"))]
    carry(1, asks[:1])
    by_group("zd0", "zk1", to_asker(1), "a_zu", ASK0)
    flights = (("ef_s", "ef", 0), ("eh_s", "eh", NL), ("z_s", "zf", NL))
    for name, src, a in flights:
        dma("y", cols(name, 0, 64), v(src, ALL, slice(704, NF)), after=asks)
    for name, src, a in flights:
        dma("y", cols(name, 64 + a, 512), v(src, ALL, slice(a, 448)))
    lazy[0] = True
    for a in range(0, FILL, NL):
        act(cols("occ", a, a + NL), v("rr"), AF.Identity, scale=0.0, bias=-1.0)
    for a in range(FILL, NT, 336):
        iota(cols("occ", a, min(a + 336, NT)), [[0, min(336, NT - a)]], -1, 0)

    def known(t):
        y0 = (64, 0, 704)[t]
        ts(cols("xp%d" % t, 0, FIX), cols("eh_s", y0, y0 + FIX), PC["ck"], A.add)
        copy("v", cols("oh%d" % t, 0, FIX), cols("eh_s", y0, y0 + FIX))
        copy("v", cols("of%d" % t, 0, FIX), cols("ef_s", y0, y0 + FIX))
        copy("s", cols("zl%d" % t, 0, FIX), cols("z_s", y0, y0 + FIX))
        lookups(t, "th:0:64:s")

    lazy[0] = False
    STAGE["asks"] = lambda t: copy("v", v("of0"), v("efq0"))
    lookups(0)
    dma("y", v("zu1"), v("zk1"), after=[sent["r0"]])
    for name, src, a in flights:
        dma("y", cols(name, 512, NF), v(src, ALL, slice(448, 704)))
    lazy[0] = True
    known(1)
    lazy[0] = False
    Y, Y2, M, CNT = B[4], B[5], PS[1] + 384, PS[0] + 384
    for a, t, o, c in ((Y, "tri", "o32", "crow"), (Y2, "tri2", "ob", "crow2")):
        mm(ps(a, a + NL), v(t), v("ob"), True, False)
        mm(ps(a, a + NL), rows(o, 1, 0, 128), rows(c, 1, 0, NL), False, False)
    for h in range(2):
        fin(0, h)
    growth(0)
    decide(0)
    tt(cols("eh_s", 64, 320), ps(R, R + NL), cols("eh_s", 64, 320), A.add)
    for a, t, o in ((Y, "tri", "o32"), (Y2, "tri2", "o2")):
        mm(ps(a, a + 128), v(t), half("sgn", 0), False, False)
        mm(ps(a + 128, a + NL), v(o), half("sgn", 0), False, False)
    for a, t in ((Y, "tri"), (Y2, "tri2")):
        mm(ps(a + 128, a + NL), v(t), half("sgn", 1), False, True)
    for h in range(2):
        mm(ps(CNT, CNT + 1), half("sgn", h), cols("ob", 0, 1), h == 0, h == 1)
    act(v("sq"), ps(Y2, Y2 + NL), AF.Square, bias=0.5)
    act(PC["nu"], ps(CNT, CNT + 1), AF.Identity, scale=-0.5, bias=-128.0)
    act(cols("fresh", 0, 12), cols("yw", 0, 12), AF.Relu, bias=PC["nu"])
    report(0)
    act(v("d0r"), ps(R, R + NL))
    copy("v", v("ri"), ps(Y, Y + NL))
    tt(v("apad", ALL, ALL, slice(0, 3, 2), ALL), ps(Y, Y + NL), v("ri"), A.is_equal)
    for h in range(2):
        ts(half("bv", h), half("sq", h), 64.0, A.is_lt, PC["v%d" % h], A.mult)
    mm(ps(M, M + 12), v("idn"), cols("fresh", 0, 12), True, False)
    for h in range(2):
        for k in range(NG):
            a, q = 128 * h + 16 * k, 32 * (k // 2)
            mm(v("psb", slice(q, q + 32), slice(M, M + 12)), v("apad", ALL, 4 * h + k // 2, slice(k % 2, k % 2 + 2), ALL), cols("bv", a, a + 12),
               False, h == 1 and k % 2 == 1)
    scatter("tb", "w0", cols("z_s", 64, 320))
    tt(cols("ef_s", 64, 320), ps(R, R + NL), cols("ef_s", 64, 320), A.add)
    carry(2)
    wrap("tb")
    lookups(1, "gh:0:64")
    ts(cols("w1", 20, 32), ps(M, M + 12), -1.0, A.mult, 320.0, A.add)
    dyn = cols("w1", 20, 32)
    copy("v", cols("oh1", FIX, NL), ind(cols("eh_s", 0, 512), dyn))
    copy("v", cols("zl1", FIX, NL), ind(cols("z_s", 0, 512), dyn))
    dma("y", v("zd1"), v("zl1"), LOAD)
    by_group("zd1", "zk3", to_asker(2), "a_z1", ASKZ)
    dma("y", v("zu3"), v("zk3"))
    n = 32

    def keys(t):
        if t == 1:
            ts(cols("xp1", FIX, NL), cols("oh1", FIX, NL), PC["ck"], A.add)

    def offsets(t):
        if t == 1:
            copy("v", cols("of1", FIX, NL), ind(cols("ef_s", 0, 512), cols("w1", 20, 32)))
        else:
            tt(cols("xq", FIX, NL), ind(v("ef_s"), cols("w2", 20, 32)), cols("dc", FIX, NL), A.add)
            ts(cols("of2", FIX, NL), cols("xq", FIX, NL), PC["ck"], A.subtract)

    def back(t, part):
        if t == 1 and part == 0:
            ts(v("pl0"), cols("msg", 0, 16), float(DUMP), A.is_lt, -80.0, A.mult)
            tt(v("xw"), ps(Y2, Y2 + NL), v("m16"), A.mult)
            for h in range(2):
                mm(ps(CNT + 16 + 8 * h, CNT + 24 + 8 * h), half("xw", h), cols("blk", 0, 8), h == 0, False)
            mm(ps(CNT + 16, CNT + 32), v("i8k"), v("pl0"), False, True)
        elif t == 1:
            ts(cols("tmq", 0, 12), cols("yw", 20, 32), PC["nu"], A.subtract, -256.0, A.add)
            ts(cols("inv1", 20, 32), cols("tmq", 0, 12), float(NL), A.min)
            ts(cols("inv1", 4, 20), ps(CNT + 16, CNT + 32), PC["ia"], A.add, float(NL), A.min)
        elif part:
            ts(cols("inv2", 0, n), cols("dst", 0, n), 63.0, A.add, float(NL), A.min)
            ts(cols("inv2", n, n + 12), cols("yw", n, n + 12), PC["y"], A.add, float(NL), A.min)

    def spare(t):
        if t == 1:
            known(2)
        else:
            tt(v("wk"), cols("yw", 80, 96), cols("uu", 4, 20), A.mult)
            tt(v("wk"), v("wk"), cols("msg", 0, 16), A.max)
            copy("v", v("w0k"), v("wk"))
            scatter("occ", "w0k", cols("idf", 64, 320))

    def names(t):
        act(v("lnf%d" % t), ind(v("idf"), cols("w%d" % t, 16, 32)))

    STAGE.update({"keys": keys, "offsets": offsets, "back": back, "spare": spare, "names": names})

    lookups(1)
    growth(1)
    decide(1)
    report(1)
    act(cols("r1", 0, NL), ps(R, R + NL), AF.Identity, bias=PC["b3"])
    scatter("occ", "w1", v("lnf1"))
    act(cols("g1", 0, 512), ind(v("r1"), v("inv1")))
    act(v("b1"), ind(v("occ"), v("w0")), AF.Sign, bias=1.0)
    scatter("tb", "w1", v("zl1"))
    PL, POS, NW, DC = PS[1] + 128, PS[0] + 128, PS[1] + 192, PS[0] + 256
    wrapped(PL, 32, "el3", "g1", 0, True, False)
    mm(ps(PL + 4, PL + 20), v("idn"), v("pl0"), False, False)
    wrapped(PL + 4, 16, "eln", "b1", 0, False, True)
    mm(ps(B[5], B[5] + 512), v("idb"), cols("pay", 0, 512), True, False)
    mm(ps(B[5], B[5] + 512), v("mk2"), cols("g1", 0, 512), False, False)
    mm(ps(B[5] + 64, B[5] + 320), v("mk2"), v("b1"), False, True)
    act(cols("pay2", 0, 512), ps(B[5], B[5] + 512))
    wrap("tb")
    lookups(2, PACK[0])
    ts(cols("uu", 0, n), ps(PL, PL + n), 40.0, A.is_lt)
    scan(cols("scn", 0, n), cols("ob", 0, n), cols("uu", 0, n), A.add)
    ts(cols("nb", 0, n), ps(PL, PL + n), 40.0, A.is_ge)
    tt(cols("vb", 0, n), cols("nb", 0, n), cols("yw", 48, 48 + n), A.mult)
    mm(ps(POS, POS + n), v("ntr"), cols("uu", 0, n), True, False)
    mm(ps(POS, POS + n), v("onb"), cols("scn", 0, n), False, True)
    mm(ps(POS + 64, POS + 65), v("onb1"), cols("scn", n - 1, n))
    mm(ps(POS + 65, POS + 66), v("onb"), cols("scn", n - 1, n))
    gate[:] = [tt(cols("dst", 0, n), ps(POS, POS + n), cols("vb", 0, n), A.max)]
    ts(cols("nrow", FIX, NL), cols("pay", 512, 512 + DYN), ps(POS + 64, POS + 65), A.subtract)
    ts(cols("dsu", 0, n), cols("dst", 0, n), 63.0, A.add)
    copy("v", ind(v("nrow"), cols("dsu", 0, n)), cols("pay2", 0, 16 * n))
    act(PC["y"], ps(POS + 65, POS + 66), AF.Identity, bias=float(FIX - 16 * n))
    lookups(2, PACK[1])
    gate[:] = []
    mm(ps(DC, DC + DYN), v("ex2"), cols("nrow", FIX, NL))
    wrapped(NW, 12, "el", "nrow", FIX)
    act(cols("dc", FIX, NL), ps(DC, DC + DYN), AF.Identity, bias=PC["ck"])
    copy("v", cols("w2", 20, 32), ps(NW, NW + 12))
    dyn = cols("w2", 20, 32)
    act(cols("zl2", FIX, NL), ind(v("z_s"), dyn))
    tt(cols("xp2", FIX, NL), ind(v("eh_s"), dyn), cols("dc", FIX, NL), A.add)
    ts(cols("oh2", FIX, NL), cols("xp2", FIX, NL), PC["ck"], A.subtract)

    lookups(2)
    growth(2)
    decide(2)
    act(cols("r2", 0, NL), ps(R, R + NL))
    act(v("g2"), ind(v("r2"), v("inv2")))
    scatter("tb", "w2", v("zl2"))
    dma("y", v("yt"), cols("tb", 0, NS), 5500)
    scatter("occ", "w2", v("lnf2"))
    dma("y", v("yo"), v("occ", slice(0, 128, 16), slice(0, NS)))
    parts = (("g2", 0, NF), ("pay2", 0, 512), ("d0r", 64, 320), ("b3", 64, 320), ("g3", 0, 512))
    for x, q in ((2, "s"), (1, "s"), (0, "v")):
        if x == 1:
            tt(cols("r3", 0, NL), ind(v("occ"), cols("w1", 0, 16)), v("lnf1"), A.not_equal)
            act(cols("g3", 0, 512), ind(v("r3"), v("inv1")))
            tt(v("b3"), ind(v("occ"), v("w0k")), cols("idf", 64, 320), A.not_equal)
        mine = [(name, max(a, NL * x), min(b, NL * x + NL), a % 128) for name, a, b in parts if a < NL * x + NL and NL * x < b]
        for k, (name, a, b, first) in enumerate(mine):
            mm(ps(B[x] + a - NL * x, B[x] + b - NL * x), v("idb"), cols(name, a - first, b - first), k == 0, k == len(mine) - 1)
        copy(q, cols("ydf", NL * x, NL * x + NL), ps(B[x], B[x] + NL))
    dma("y", v("yd", ALL, slice(0, 704)), v("ydf", slice(2, 128, 16), slice(64, NF)))
    dma("s", v("yd", ALL, slice(704, NF)), v("ydf", slice(2, 128, 16), slice(0, 64)))
    F["finish"]()


def rank_program(g, core, T, topo):
    if T.rank_of(core) is not None:
        rank_main(g, core, T.rank_of(core), T, topo)
        return
    for rank in range(N):
        senders = helpers(T.cores[rank], T, topo)[0]
        if core in senders:
            sender_main(g, core, rank, senders.index(core), T, topo)
        jobs = [(t, c) for t in (1, 2) for c in range(NCH) if joiner(rank, t, c, T, topo) == core]
        if jobs:
            joiner_main(g, core, rank, jobs, T, topo)
